import numpy as np, ml_dtypes
CORES = [2,3,42,43,82,83,122,123]
N = 8
BF = ml_dtypes.bfloat16
def gentries(a):
    return np.ascontiguousarray(a.reshape(8, 16, -1).transpose(0, 2, 1)).reshape(8, -1)
def gtable(e):
    e = np.asarray(e); return np.ascontiguousarray(e.reshape(8, -1, 16).transpose(0, 2, 1)).reshape(128, -1).astype(np.int32)
W0, B, LN, RO, SP, CAP = 3072, 128, 2560, 4, 2, 768
W = W0 + RO * B
def parts(rng):
    scale = np.array([0.5, 1, 1.5, 2, 3, 4, 6, 8])[np.argsort(rng.random((N, 8)), axis=1)][:, :, None, None]; dens = 0.1 + 0.6 * rng.random((N, 8, 1, W0))
    cnt = np.where(rng.random((N, 8, 16, W0)) < dens, np.minimum(15, 1 + (scale * rng.standard_exponential((N, 8, 16, W0))).astype(np.int64)), 0)
    hot = rng.integers(0, W0, (N, 8, 64))
    def some(n, share):
        return np.where(rng.random((N, 8, n)) < share, np.take_along_axis(hot, rng.integers(0, 64, (N, 8, n)), 2), rng.integers(0, W0, (N, 8, n)))
    ptr = some(16 * W0, 0.4).reshape(N, 8, 16, W0); suf = (np.arange(W0) * rng.random((N, 8, W0))).astype(np.int64)
    return cnt, ptr, suf, rng.integers(0, W0, (N, 8, W0)), some(LN, 0.3), rng.integers(0, 256, (N, 8, RO * SP, LN))
def levels(rng, cnt, suf, v, g):
    x = np.arange(W0); b = np.where(x <= 16, 3, np.where(x <= 32, 2, np.where(x <= 48, 1, 0)))
    cnt[:, g] = np.where((np.arange(16) >> 2)[:, None] == b, rng.integers(1, 16, (N, 16, W0)), 0)
    suf[:, g] = rng.integers(1, 17, (N, W0)) + 16 * np.maximum(2 - b, 0)
    v[:, g, :SP - 1, :B] = rng.integers(240, 256, (N, SP - 1, B)); v[:, g, SP - 1, :B] = rng.integers(0, 128, (N, B))
def clones(rng, cnt, ptr, suf, lnk, cx, v, g):
    o = 1 + np.argsort(rng.random((N, W0 - 1)), axis=1); x = o[:, :B]; b = o[:, B:2 * B]; u = o[:, 2 * B:3 * B]
    qi = np.arange(N)[:, None]; z = rng.integers(1, 16, (N, B)); ct = cnt[:, g]; pt = ptr[:, g]
    for y in (x, u):
        ct[qi, :, y] = 0; ct[qi, 0, y] = 1; pt[qi, 0, y] = y
    ct[qi, :, b] = 0; ct[qi, z, b] = 1; pt[qi, z, b] = u
    suf[qi, g, x] = b; suf[qi, g, u] = x; lnk[qi, g, u] = np.maximum(lnk[qi, g, u], 1); cx[:, g, :B] = x
    v[:, g, :, :B] = rng.integers(0, 64, (N, RO * SP, B))
    for s in (SP - 2, 2 * SP - 2): v[:, g, s, :B] = rng.integers(128, 256, (N, B))
    if (RO - 2) * SP > 2:
        v[:, g, RO * SP - 2, :B] = rng.integers(64, 128, (N, B)); v[:, g, RO * SP - 1, :B] = rng.integers(128, 256, (N, B))
def kept(rng, cnt, ptr, suf, cx, v, g):
    o = 1 + np.argsort(rng.random((N, W0 - 1)), axis=1)[:, :(SP + 1) * B]; h = o[:, :SP * B]; b = o[:, SP * B:]
    qi = np.arange(N)[:, None]; z = rng.integers(1, 16, (N, B)); ct = cnt[:, g]; pt = ptr[:, g]
    ct[qi, :, h] = 0; ct[qi, 0, h] = 1; pt[qi, 0, h] = h; suf[qi, g, h] = o[:, B:]
    ct[qi, :, b] = 0; ct[qi, z, b] = 1; cx[:, g] = o[:, np.arange(LN) % B]
    v[:, g, :SP] = rng.integers(0, 128, (N, SP, LN)); v[1::2, g, SP - 1, :B] = rng.integers(128, 256, (N // 2, B))
    v[:, g, 2 * SP - 1, :B] = rng.integers(0, 128, (N, B))
def filled(rng, cnt, ptr, suf, lnk, cx, v, g):
    o = 1 + np.argsort(rng.random((N, W0 - 1)), axis=1)[:, :(2 * SP + 1) * B]; x = o[:, :B]; y = o[:, B:]; b1 = o[:, SP * B:(SP + 1) * B]; b2 = o[:, 2 * SP * B:]
    qi = np.arange(N)[:, None]; ct = cnt[:, g]; pt = ptr[:, g]
    ct[qi, :, o] = 0; ct[qi, 0, o] = 1; pt[qi, 0, o] = o
    for b, lo in ((b1, 1), (b2, 8)):
        ct[qi, 0, b] = 0; ct[qi, rng.integers(lo, lo + 7, (N, B)), b] = 1
    suf[qi, g, x] = np.roll(x, -1, axis=1); suf[qi, g, y[:, :-B]] = y[:, B:]; lnk[qi, g, x] = np.roll(y[:, :B], -1, axis=0)
    cx[:, g] = x[:, np.arange(LN) % B]
    v[:, g, :2 * SP] = rng.integers(0, 128, (N, 2 * SP, LN)); v[:, g, SP - 1, :B] = rng.integers(128, 256, (N, B))
    q4 = np.arange(N) % 4; v[:, g, 2 * SP - 1, :B // 2] += 128 * ((q4 == 1) | (q4 == 2))[:, None]
    if RO > 2: v[:, g, 3 * SP - 1, :B // 2] = rng.integers(0, 128, (N, B // 2))
def pack(cnt, ptr, suf, lnk, cx, v):
    return {"tab": np.ascontiguousarray((16 * ptr + cnt).reshape(N, 128, W0)).astype(np.int32), "suf": suf.astype(np.int32), "lnk": lnk.astype(np.int32),
            "cx": np.stack([gtable(a) for a in cx]), "vv": v.reshape(N, 8, RO * SP * LN).astype(np.float32).astype(BF)}
def setup_inputs(rng):
    return pack(*parts(rng))
def setup_inputs_room(rng):
    cnt, ptr, suf, lnk, cx, v = parts(rng)
    cnt = np.where(np.arange(16)[:, None] == rng.integers(0, 16, (N, 8, 1, W0)), np.maximum(cnt, 1), cnt); ptr = np.maximum(ptr, 1); cx = np.maximum(cx, 1)
    v[:, :, :SP - 1] = rng.integers(0, 128, (N, 8, SP - 1, LN)); opts = (0, 1, CAP - 1, CAP, CAP + 1, LN)
    for q in range(N):
        o = rng.permutation(6)
        for g in range(6):
            m = opts[g] if q == 0 else opts[5 - g] if q == 1 else opts[int(o[g])]
            v[q, g, SP - 1] = np.where(rng.permutation(LN) < m, rng.integers(240, 256, LN), rng.integers(0, 128, LN))
    for g in (6, 7):
        levels(rng, cnt, suf, v, g)
        for q in range(N): cx[q, g, :B] = 64 + rng.permutation(W0 - 64)[:B]
    return pack(cnt, ptr, suf, lnk, cx, v)
def setup_inputs_ties(rng):
    cnt, ptr, suf, lnk, cx, v = parts(rng)
    rows = np.array([4, 1, 2, 8, 1, 0, 16, 4, 8, 8, 16]); vals = np.array([3, 1, 1, 1, 15, 0, 15, 1, 3, 7, 3]); k = rng.integers(0, 11, (N, 8, W0))
    order = np.argsort(rng.random((N, 8, W0, 16)), axis=-1)
    cnt = np.where(order < rows[k][..., None], vals[k][..., None], 0).transpose(0, 1, 3, 2)
    v = np.where(rng.random(v.shape) < 0.6, 16 * rng.integers(0, 17, v.shape), 15 * rng.integers(0, 18, v.shape)) + np.where(rng.random(v.shape) < 0.6, 0, rng.integers(-1, 2, v.shape))
    return pack(cnt, ptr, suf, lnk, cx, np.minimum(np.maximum(v, 0), 255))
def setup_inputs_alike(rng):
    cnt, ptr, suf, lnk, cx, v = parts(rng); few = rng.integers(1, W0, (N, 8, 6))
    def some(n, m):
        return np.take_along_axis(few, rng.integers(0, m, (N, 8, n)), 2)
    ptr = some(16 * W0, 6).reshape(N, 8, 16, W0); suf = np.where(rng.random((N, 8, W0)) < 0.5, some(W0, 6), suf); lnk = np.where(rng.random((N, 8, W0)) < 0.5, some(W0, 6), lnk); cx = some(LN, 4)
    levels(rng, cnt, suf, v, 3); cx[:, 3, :B] = rng.choice(np.array([70, W0 - 1]), (N, B))
    cx[:, 5] = cx[:, 5, :1]; v[:, 5] = v[:, 5, :, :1]
    filled(rng, cnt, ptr, suf, lnk, cx, v, 2); kept(rng, cnt, ptr, suf, cx, v, 6); clones(rng, cnt, ptr, suf, lnk, cx, v, 7)
    return pack(cnt, ptr, suf, lnk, cx, v)
def setup_inputs_ends(rng):
    cnt, ptr, suf, lnk, cx, v = parts(rng); e = np.array([0, 1, W0 - 1])
    ptr = np.where(rng.random(ptr.shape) < 0.3, rng.choice(e, ptr.shape), ptr); lnk = np.where(rng.random(lnk.shape) < 0.5, rng.choice(e, lnk.shape), lnk); cx = np.where(rng.random(cx.shape) < 0.5, rng.choice(e, cx.shape), cx)
    suf[:, 1::2] = np.where(rng.random((N, 4, W0)) < 0.3, np.arange(W0), rng.integers(0, W0, (N, 4, W0))); suf[:, 2] = 0; suf[:, 4] = 0; suf[:, 5] = 0
    cnt[:, 4, :, 0] = 0; cnt[:, 5, :, 0] = 15; cnt[:, 6] = 15 * (cnt[:, 6] > 0); cnt[:, 7, :, W0 - 1] = 0; cnt[:, 0, :, W0 - 1] = 15
    v = np.where(rng.random(v.shape) < 0.7, rng.choice(np.array([0, 1, 127, 128, 239, 240, 254, 255]), v.shape), v)
    return pack(cnt, ptr, suf, lnk, cx, v)
def setup_inputs_spread(rng):
    def low(*shape):
        return np.minimum((W0 * rng.random(shape) ** rng.integers(1, 5, shape[:2] + (1,) * (len(shape) - 2))).astype(np.int64), W0 - 1)
    cnt = np.where(rng.random((N, 8, 16, W0)) < rng.random((N, 8, 1, W0)) ** 2, np.minimum(np.exp2(4 * rng.random((N, 8, 16, W0)) * rng.random((N, 8, 1, W0)) ** 0.5).astype(np.int64), 15), 0)
    v = np.minimum((256 * rng.random((N, 8, RO * SP, LN)) ** 3).astype(np.int64), 255)
    return pack(cnt, low(N, 8, 16, W0), low(N, 8, W0), W0 - 1 - low(N, 8, W0), low(N, 8, LN), np.where(rng.random(v.shape) < 0.5, v, 255 - v))
def check_inputs(d):
    bad = []
    for k, hi in (("tab", 16 * W0 - 1), ("suf", W0 - 1), ("lnk", W0 - 1), ("cx", W0 - 1)):
        if np.min(d[k]) < 0 or np.max(d[k]) > hi: bad.append("range of " + k)
    v = np.asarray(d["vv"]).astype(np.float32)
    if not np.all((v >= 0) & (v <= 255) & (v == np.floor(v))): bad.append("range of vv")
    return bad
def reference(tab, suf, lnk, cx, vv):
    k = tab.astype(np.int32).reshape(N, 8, 16, W0)
    C = np.zeros((N, 8, 16, W), np.int32); S = np.zeros((N, 8, 16, W), np.int32); C[..., :W0] = k & 15; S[..., :W0] = k >> 4
    F = np.zeros((N, 8, W), np.int32); L = np.zeros((N, 8, W), np.int32); F[..., :W0] = suf; L[..., :W0] = lnk
    v = vv.astype(np.float32).astype(np.int32).reshape(N, 8, RO, SP, 1, LN)
    c = np.stack([gentries(a) for a in cx]).astype(np.int32); e = np.zeros((N, 8, 16, LN), np.int32); f = np.full((N, 8, LN), -1, np.int32)
    qi = np.arange(N)[:, None, None]; gi = np.arange(8)[None, :, None]
    for t in range(RO):
        for s in range(SP):
            cc = np.take_along_axis(C, c[:, :, None, :], 3)
            n = cc * (1 - e); P = np.add.accumulate(n, axis=2, dtype=np.int32); E = np.add.reduce((n > 0).astype(np.int32), axis=2)
            z = np.add.reduce((256 * P <= v[:, :, t, s] * (P[:, :, 15] + E)[:, :, None, :]).astype(np.int32), axis=2)
            z = np.where(c == 0, np.minimum(z, 15), z); esc = z == 16
            d, fb = c, f
            f = np.where(esc, np.where(fb < 0, d, fb), -1)
            e = np.where(esc[:, :, None, :], np.maximum(e, (cc > 0).astype(np.int32)), 0)
            c = np.where(esc, F[qi, gi, d], S[qi, gi, np.minimum(z, 15), d])
        for q in range(N):
            for g in range(8):
                j = np.nonzero(~esc[q, g, :B] & (fb[q, g, :B] >= 0))[0]
                a = j[np.unique(fb[q, g, j], return_index=True)[1]]
                w = W0 + B * t + a; to = c[q, g, a]
                cw = (C[q, g][:, to] + 1) >> 1; sw = S[q, g][:, to]
                C[q, g][:, w] = cw; S[q, g][:, w] = sw; F[q, g, w] = to; L[q, g, w] = L[q, g, to]
                C[q, g, z[q, g, a], fb[q, g, a]] = 1; S[q, g, z[q, g, a], fb[q, g, a]] = w
                b = j[np.unique(d[q, g, j], return_index=True)[1]]
                C[q, g, z[q, g, b], d[q, g, b]] = np.minimum(15, C[q, g, z[q, g, b], d[q, g, b]] + 1)
        slot = esc & (np.add.accumulate(esc.astype(np.int32), axis=2) <= CAP)
        c2 = np.array(c); e2 = np.array(e); f2 = np.array(f)
        for r in range(N):
            q = (r - 1) % N
            for g in range(8):
                a = np.nonzero(slot[q, g])[0]; b = np.nonzero(slot[r, g])[0]; m = min(len(a), len(b)); a = a[:m]; b = b[:m]
                c2[r, g, b] = L[q, g, c[q, g, a]]; e2[r, g][:, b] = e[q, g][:, a]; f2[r, g, b] = -1
        c, e, f = c2, e2, f2
    return {"yn": C.reshape(N, 128, W).astype(np.float32).astype(BF), "yc": np.stack([gtable(a) for a in c]).astype(np.float32)}

@@ -1,0 +1,637 @@
+from concourse.mybir import dt, AluOpType as OP, ActivationFunctionType as AF
+
+EPS = 2.0 ** -14
+W0, B, LN, RO, SP, CAP = 3072, 128, 2560, 4, 2, 768
+W = W0 + RO * B
+WD = W + B
+XS = "AB"
+CQ = {"A": slice(0, 96), "B": slice(96, 160)}
+NQ = {"A": 96, "B": 64}
+PIECES = {"A": [0, 1, 2], "B": [3, 4]}
+
+_F, _H, _I, _B, _U = "float32", "float16", "int32", "bfloat16", "uint16"
+SCRATCH = {}
+for _n, _w, _d in (
+        ("tb", WD, _I), ("kt", WD, _F), ("dtb", WD, _F), ("gt", WD, _B), ("lt", WD, _B),
+        ("ci", 1024, _I), ("cb", 1024, _B), ("sg", 1024, _B), ("cb2", 1024, _B), ("sg2", 1024, _B), ("si", 1024, _I), ("s16", 1024, _H), ("rr", 1024, _I),
+        ("dn", 576, _I), ("dg", 1152, _I), ("dgb", 1152, _B), ("v1", 1280, _F), ("v31", 1280, _F),
+        ("iop", 1, _I), ("pi", 2, _I), ("xf", 160, _F), ("xg", 128, _F), ("xr", 128, _F),
+        ("pc", 32, _F), ("oh16", 16, _F), ("m32", 16, _F), ("jg", 160, _F), ("dja", 16, _F), ("djb", 16, _F),
+        ("mats", 14 * 128, _B), ("sels", 5 * 160, _B), ("expa", 2048, _B), ("ones", 512, _B), ("tm1", 128, _F), ("tm2", 128, _F), ("tm3", 128, _I),
+        ("ca", 160, _I), ("cc", 160, _I), ("cl", 160, _U), ("pp", 160, _I), ("vs", 160, _F), ("wp", 160, _F), ("qq", 160, _H),
+        ("ff", 160, _F), ("mm", 160, _I), ("es", 160, _B), ("inc", 168, _F), ("zer", 96, _F), ("sa", 160, _F), ("sb2", 160, _F),
+        ("sl", 160, _U), ("rl", 160, _U), ("nr", 160, _F), ("c1", 160, _F), ("rc", 160, _F), ("yo", 160, _F), ("pw", 2 * LN, _B),
+        ("h0", 8, _F), ("h1", 8, _F), ("ht", 8, _F), ("e8", 8, _F), ("cnd", 8, _F), ("dgi", 16, _I),
+        ("ka", 16, _F), ("k32", 16, _F), ("k16", 32, _H), ("fdu", 16, _U), ("fy", 16, _F), ("lw", 16, _U),
+        ("kr", 256, _B), ("cr", 256, _F), ("ohb", 128, _B), ("ohf", 128, _F), ("oh3", 128, _F), ("o33", 128, _F),
+        ("chi", 128, _I), ("chf", 128, _F), ("cm", 128, _F), ("kf", 128, _F), ("k2", 128, _F), ("xi", 128, _I), ("xs", 128, _I),
+        ("xt", 128, _F), ("xw", 128, _F), ("xv", 128, _F), ("xd", 128, _F), ("wv", 128, _F), ("g1", 128, _B), ("g2", 128, _B), ("gf", 128, _B),
+        ("wdl", 128, _F), ("ynb", W, _B)):
+    SCRATCH[_n] = ("sbuf", [128, _w], _d)
+SCRATCH["vr"] = ("sbuf", [8, 20480], _B)
+SCRATCH["eq"] = ("sbuf", [128, 16, 128], _B)
+SCRATCH["msk"] = ("sbuf", [128, 16, 16], _B)
+for _x in XS:
+    for _n, _d in (("kap", _H), ("ds", _H), ("gg", _B), ("ne", _B), ("em", _B), ("cd", _B)):
+        SCRATCH[_n + _x] = ("sbuf", [128, 16 * NQ[_x]], _d)
+for _k in range(RO):
+    SCRATCH["rb%d" % _k] = ("sbuf", [128, CAP + 16], _B)
+for _k in range(8):
+    SCRATCH["b%d" % _k] = ("psum", [128, 512], _F)
+SEMAPHORES = ["cv", "ct", "cs", "cg"] + ["ld%d" % k for k in range(16)] + ["gd%d" % k for k in range(6)] + ["arr%d" % k for k in range(RO)] + ["snt%d" % k for k in range(RO)]
+
+
+def rank_program(g, core, T, topo):
+    rank = T.rank_of(core)
+    if rank is None:
+        return
+    E = {"v": g.vector, "t": g.tensor, "s": g.scalar, "g": g, "y": g.sync}
+    V, S, PE = g.vector, g.scalar, g.tensor
+    cnt, waited, lw, lr = {}, {}, {}, {}
+
+    def need(eng, sem, val):
+        if waited.get((eng, sem), 0) < val:
+            E[eng].wait_ge(T.sem[sem], val)
+            waited[(eng, sem)] = val
+
+    def deps(eng, r, w):
+        todo = {}
+        ds = [lw[k] for k in list(r) + list(w) if k in lw]
+        for k in w:
+            ds += list(lr.get(k, {}).values())
+        for d in ds:
+            if not (d[0] == eng == "t"):
+                todo[d[1]] = max(todo.get(d[1], 0), d[2])
+        for s in todo:
+            need(eng, s, todo[s])
+
+    def mark(d, r, w):
+        for k in w:
+            lw[k] = d
+            lr[k] = {}
+        for k in r:
+            if k not in w:
+                lr.setdefault(k, {})[d[1]] = d
+
+    def op(eng, fn, r="", w=""):
+        r = r.split()
+        w = w.split()
+        w = w + [k for k in r if len(k) == 2 and k[0] == "b" and k not in w]
+        deps(eng, r, w)
+        sem = "c" + eng
+        cnt[sem] = cnt.get(sem, 0) + 1
+        fn().then_inc(T.sem[sem], 1)
+        mark((eng, sem, cnt[sem]), r, w)
+
+    def dma(eng, out, in_, sem, r="", w=""):
+        r = r.split()
+        w = w.split()
+        deps(eng, r, w)
+        cnt[sem] = cnt.get(sem, 0) + 16
+        E[eng].dma_start(out, in_).then_inc(T.sem[sem], 16)
+        mark(("dma", sem, cnt[sem]), r, w)
+
+    def vts(out, in0, r, w, s1, o0, s2=None, o1=None):
+        if o1 is None:
+            op("v", lambda: V.tensor_scalar(out, in0, s1, None, o0), r, w)
+        else:
+            op("v", lambda: V.tensor_scalar(out, in0, s1, s2, o0, o1), r, w)
+
+    def vtt(out, a, b, r, w, alu):
+        op("v", lambda: V.tensor_tensor(out, a, b, alu), r, w)
+
+    def vcp(out, in_, r, w):
+        op("v", lambda: V.tensor_copy(out, in_), r, w)
+
+    def fill(out, pattern, base, w, cm=0):
+        op("g", lambda: g.iota(out, pattern, base, cm, allow_small_or_imprecise_dtypes=True), "", w)
+
+    def act(out, in_, r, w, func, bias=0.0, scale=1.0):
+        op("s", lambda: S.activation(out, in_, func, bias=bias, scale=scale), r, w)
+
+    def mms(out, pairs, r, w):
+        def f():
+            for i, (a, b) in enumerate(pairs):
+                x = PE.matmul(out, a, b, i == 0, i == len(pairs) - 1)
+            return x
+        op("t", f, r, w)
+
+    for k in range(3):
+        dma("y", T.tb[:, 1024 * k:1024 * k + 1024], T.tab[:, 1024 * k:1024 * k + 1024], "ld%d" % k, "", "tb%d" % k)
+    dma("s", T.ca[:], T.cx[:, :], "ld6", "", "caA caB")
+    dma("s", T.vr[:, :], T.vv[:, :], "ld7", "", "vr")
+    dma("s", T.dn[:, 384:576], T.tab[0::16, :], "ld3", "", "dnt")
+    dma("s", T.dn[:, 0:192], T.suf[:, :], "ld4", "", "dnf")
+    dma("s", T.dn[:, 192:384], T.lnk[:, :], "ld5", "", "dnl")
+
+    PGC, PRC, PFC, P16, PM1, PP1, A1, A2, C15, WDc, WSc, WFc, R01, N15, D15, T1, T2, NPR, Q2, Q3, W2 = range(21)
+
+    def col(i):
+        return T.pc[:, i:i + 1]
+
+    def key(i):
+        return "pc%d" % i
+    fill(T.iop[:], [[1, 1]], 0, "iop", 1)
+    fill(col(PFC), [[1, 1]], 0, key(PFC), 1)
+    fill(T.xf[:], [[1, 160]], 0, "xf")
+    fill(T.xg[:], [[1, 8], [0, 16]], 0, "xg")
+    fill(T.xr[:], [[0, 8], [1, 16]], 0, "xr")
+    fill(T.ones[:], [[0, 512]], 1, "ones")
+    GT = "gtx gt0 gt1 gt2 gt3"
+    LT = "ltx lt0 lt1"
+    fill(T.dtb[:, W0:WD], [[0, WD - W0]], 0, "dtx")
+    fill(T.gt[:], [[0, WD]], 0, GT)
+    fill(T.lt[:], [[0, WD]], -2, LT)
+    fill(T.h0[:], [[0, 8]], 0, "h0")
+    fill(T.inc[:, 0:8], [[0, 8]], 8191, "inc0")
+    fill(T.zer[:], [[0, 96]], 0, "zer")
+    for k in range(RO):
+        fill(T["rb%d" % k][:, CAP:CAP + 16], [[0, 16]], 0, "rbx%d" % k)
+    fill(T.tb[:, W0:WD], [[0, WD - W0]], 0, "tbx")
+    fill(T.tm3[:], [[1, 128]], 0, "tm3")
+    fill(T.pw[:, 0:CAP], [[0, CAP]], 0, "pw")
+
+    vts(T.pi[:, 0:1], T.iop[:], "iop", "pi", 4, OP.arith_shift_right)
+    vts(T.pi[:, 1:2], T.iop[:], "iop", "pi1", 15, OP.bitwise_and)
+    vcp(col(PGC), T.pi[:, 0:1], "pi", key(PGC))
+    vcp(col(PRC), T.pi[:, 1:2], "pi1", key(PRC))
+    vts(T.oh16[:], T.xf[:, 0:16], "xf " + key(PRC), "oh16", col(PRC), OP.is_equal)
+
+    def ohc(i):
+        return T.oh16[:, i:i + 1]
+    names = ["ida", "idb", "idc", "mdf", "mfl", "blk", "tri", "i14", "n8k", "e15", "moh", "mz0", "mz1", "nhf"]
+    M = {n: T.mats[:, 128 * i:128 * i + 128] for i, n in enumerate(names)}
+    M.update({n: T.sels[:, 160 * i:160 * i + 160] for i, n in enumerate(["selt", "seld", "selS", "selF", "vsel"])})
+    xm = T.xf[:, 0:128]
+
+    def mat(out, name, c, m, extra=""):
+        vts(out, xm, "xf " + key(c) + " " + extra, name, col(c), OP.is_equal, m, OP.mult)
+
+    def colop(i, src, srck, s1, o0, s2=None, o1=None):
+        vts(col(i), src, srck, key(i), s1, o0, s2, o1)
+    mat(M["ida"], "ida", PFC, 32.0)
+    mat(M["idb"], "idb", PFC, 1.0)
+    mat(M["idc"], "idc", PFC, EPS)
+    vts(M["blk"], T.xg[:], "xg " + key(PGC), "blk", col(PGC), OP.is_equal)
+    vts(T.m32[:], T.oh16[:], "oh16", "m32", -32.0, OP.mult)
+    for r in range(16):
+        act(T.expa[:, 128 * r:128 * r + 128], M["blk"], "blk m32", "expa%d" % r, AF.Copy, scale=T.m32[:, r:r + 1])
+    EXPA = " ".join("expa%d" % r for r in range(16))
+    colop(T1, col(PFC), key(PFC), 16.0, OP.mult, 16.0, OP.add)
+    vts(M["vsel"], T.xf[:], "xf " + key(T1), "vsel", col(T1), OP.is_equal)
+    colop(P16, col(PGC), key(PGC), 16.0, OP.mult, 16.0, OP.add)
+    vts(M["selt"], T.xf[:], "xf " + key(P16), "selt", col(P16), OP.is_equal)
+    vts(T.tm1[:], T.xr[:], "xr " + key(PRC), "tm1", col(PRC), OP.is_ge)
+    vtt(M["tri"], T.tm1[:], M["blk"], "tm1 blk", "tri", OP.mult)
+    colop(PM1, col(PFC), key(PFC), 1.0, OP.subtract)
+    colop(A1, ohc(0), "oh16", -1.0 / 4096, OP.mult, 1.0 / 4096, OP.add)
+    colop(A2, ohc(15), "oh16", 1.0 / 4096, OP.mult, -1.0 / 4096, OP.add)
+    mat(T.tm1[:], "tm1", PM1, col(A1), key(A1))
+    mat(T.tm2[:], "tm2", PFC, col(A2), key(A2))
+    vtt(M["mdf"], T.tm1[:], T.tm2[:], "tm1 tm2", "mdf", OP.add)
+    vts(M["mfl"], M["idb"], "idb oh16", "mfl", ohc(15), OP.mult, 0.25, OP.mult)
+    colop(N15, ohc(15), "oh16", -1.0, OP.mult, 1.0, OP.add)
+    colop(WDc, ohc(15), "oh16", 2.0 ** 19 - 4096.0, OP.mult, 4096.0, OP.add)
+    colop(WSc, ohc(1), "oh16", 64.0, OP.mult, ohc(0), OP.add)
+    colop(WFc, ohc(3), "oh16", 64.0, OP.mult, ohc(2), OP.add)
+    for n, c in (("seld", WDc), ("selS", WSc), ("selF", WFc)):
+        vts(M[n], T.xf[:], "xf " + key(P16) + " " + key(c), n, col(P16), OP.is_equal, col(c), OP.mult)
+    colop(C15, ohc(15), "oh16", 2.0 ** 25, OP.mult)
+    mat(M["i14"], "i14", PFC, 2.0 ** 14)
+    vts(M["e15"], M["blk"], "blk " + key(C15), "e15", col(C15), OP.mult)
+
+    pb = [0]
+
+    def nextbank():
+        pb[0] += 1
+        return "b%d" % (pb[0] % 7)
+    for k in range(3):
+        c0 = 1024 * k
+        cb, sg = ("cb", "sg") if k % 2 == 0 else ("cb2", "sg2")
+        vts(T.ci[:], T.tb[:, c0:c0 + 1024], "tb%d" % k, "ci", 15, OP.bitwise_and)
+        vcp(T[cb][:], T.ci[:], "ci", cb)
+        act(T[sg][:], T[cb][:], cb, sg, AF.Sign)
+        for h in range(2):
+            p = slice(512 * h, 512 * h + 512)
+            bk = nextbank()
+            mms(T[bk][:], [(M["ida"], T[cb][:, p]), (M["idb"], T[sg][:, p]), (M["idc"], T[sg][:, p])], "ida idb idc " + cb + " " + sg, bk)
+            act(T.kt[:, c0 + 512 * h:c0 + 512 * h + 512], T[bk][:], bk, "kt%d%d" % (k, h), AF.Copy, bias=-EPS)
+    act(T.kt[:, W0:WD], T.dtb[:, W0:WD], "dtx", "ktx", AF.Copy, bias=-EPS)
+    KT = "ktx " + " ".join("kt%d%d" % (k, h) for k in range(3) for h in range(2))
+    DT = "dtx " + " ".join("dt%d%d" % (k, h) for k in range(3) for h in range(2))
+    TB = "tbx tb0 tb1 tb2"
+
+    def digits():
+        q = 192
+        vts(T.dg[:, 0:q], T.dn[:, 384:576], "dnt", "dg0", 4, OP.arith_shift_right, 63, OP.bitwise_and)
+        vts(T.dg[:, q:2 * q], T.dn[:, 384:576], "dnt", "dg1", 10, OP.arith_shift_right)
+        vts(T.dg[:, 2 * q:3 * q], T.dn[:, 0:192], "dnf", "dg2", 63, OP.bitwise_and)
+        vts(T.dg[:, 3 * q:4 * q], T.dn[:, 0:192], "dnf", "dg3", 6, OP.arith_shift_right)
+        vts(T.dg[:, 4 * q:5 * q], T.dn[:, 192:384], "dnl", "dg4", 63, OP.bitwise_and)
+        vts(T.dg[:, 5 * q:6 * q], T.dn[:, 192:384], "dnl", "dg5", 6, OP.arith_shift_right)
+        vcp(T.dgb[:, 0:4 * q], T.dg[:, 0:4 * q], "dg0 dg1 dg2 dg3", "dgb0")
+        vts(T.dgb[:, 4 * q:6 * q], T.dg[:, 4 * q:6 * q], "dg4 dg5", "dgb1", -1.0, OP.mult, -2.0, OP.add)
+        for k in range(4):
+            dma("y", T.gt[k::16, 0:W0], T.dgb[:, k * q:k * q + q], "gd%d" % k, "dgb0", "gt%d" % k)
+        for k in range(2):
+            dma("y", T.lt[k::16, 0:W0], T.dgb[:, (4 + k) * q:(5 + k) * q], "gd%d" % (4 + k), "dgb1", "lt%d" % k)
+
+    def pointers(k):
+        c0 = 1024 * k
+        vts(T.si[:], T.tb[:, c0:c0 + 1024], "tb%d" % k, "si", 4, OP.arith_shift_right)
+        vts(T.s16[:], T.si[:], "si", "s16", 1792.0, OP.subtract)
+        for h in range(2):
+            p = slice(512 * h, 512 * h + 512)
+            bk = "b%d" % (2 * (k % 2) + h)
+            mms(T[bk][:], [(M["mdf"], T.s16[:, p]), (M["mfl"], T.ones[:])], "mdf mfl s16 ones", bk)
+            vcp(T.rr[:, p], T[bk][:], bk, "rr%d" % h)
+            vtt(T.dtb[:, c0 + 512 * h:c0 + 512 * h + 512], T[bk][:], T.rr[:, p], bk + " rr%d" % h, "dt%d%d" % (k, h), OP.subtract)
+        if k == 0:
+            vts(T.dtb[:, 0:1], T.dtb[:, 0:1], "dt00 " + key(N15), "dt00", col(N15), OP.mult)
+
+    def late_constants():
+        colop(PP1, col(PFC), key(PFC), 1.0, OP.add)
+        colop(R01, ohc(0), "oh16", ohc(1), OP.add)
+        colop(D15, ohc(15), "oh16", 10.25, OP.mult, -10.0, OP.add)
+        colop(T2, col(PRC), key(PRC), 2560.0, OP.add)
+        colop(NPR, col(PRC), key(PRC), -1.0, OP.mult)
+        colop(Q2, ohc(2), "oh16", -1.0 / 32, OP.mult)
+        colop(Q3, ohc(3), "oh16", -1.0 / 32, OP.mult)
+        for t in range(RO - 1):
+            colop(W2 + t, ohc(1), "oh16", 2.0 * t, OP.mult)
+        act(T.jg[:], T.xf[:], "xf " + key(T2), "jg", AF.Identity, bias=col(T2), scale=16.0)
+        for h in range(16):
+            act(T.msk[:, h, :], T.xf[:, 0:16], "xf " + key(NPR), "msk%d" % h, AF.Relu, bias=col(NPR))
+        for h in range(2):
+            o = slice(8 * h, 8 * h + 8)
+            vts(T.dja[:, o], T.jg[:, 0:8], "jg", "dja%d" % h, float(W - 2560 - 1792), OP.add, 32.0, OP.mult)
+            vts(T.djb[:, o], T.jg[:, 0:8], "jg", "djb%d" % h, float(W - 2560), OP.add, -512.0, OP.mult)
+        mat(M["n8k"], "n8k", PFC, -8192.0)
+        mat(M["nhf"], "nhf", PFC, -0.5)
+        mat(T.tm1[:], "tm1", PP1, col(N15), key(N15))
+        mat(T.tm2[:], "tm2", PFC, col(N15), key(N15))
+        vtt(M["moh"], T.tm1[:], T.tm2[:], "tm1 tm2", "moh", OP.subtract)
+        mat(M["mz0"], "mz0", PFC, ohc(0), "oh16")
+        mat(T.tm1[:], "tm1", PP1, ohc(0), "oh16")
+        vtt(M["mz1"], T.tm1[:], M["mz0"], "tm1 mz0", "mz1", OP.add)
+        vts(T.xi[:], T.tm3[:], "tm3", "xi", 63, OP.bitwise_and)
+        vts(T.xs[:], T.tm3[:], "tm3", "xs", 6, OP.arith_shift_right)
+        vts(T.tm1[:], T.xi[:], "xi oh16", "tm1", ohc(0), OP.mult)
+        vts(T.tm2[:], T.xs[:], "xs oh16", "tm2", float(W0 // 64), OP.add, ohc(1), OP.mult)
+        vtt(T.wdl[:], T.tm1[:], T.tm2[:], "tm1 tm2", "wdl", OP.add)
+
+    def vlist(st):
+        mms(T.b7[:, 352:512], [(M["vsel"][0:8, 16 - r:144 - r], T.vr[0:8, st * LN + r:(st + 1) * LN:16]) for r in range(16)], "vsel vr", "b7")
+        act(T.v1[:, st * 160:st * 160 + 160], T.b7[:, 352:512], "b7", "v1_%d" % st, AF.Copy)
+        act(T.v31[:, st * 160:st * 160 + 160], T.b7[:, 352:512], "b7", "v31_%d" % st, AF.Copy, scale=31.0)
+
+    CUR = ["ca"]
+    HCUR = ["h0"]
+    for X in XS:
+        vcp(T.cl[:, CQ[X]], T.ca[:, CQ[X]], "ca" + X, "cl" + X)
+
+    def selmm(out, w, base, rhs, rk, start=True, stop=True):
+        def f():
+            for r in range(16):
+                x = PE.matmul(out, M[base][:, 16 - r:144 - r], rhs[:, r::16], start and r == 0, stop and r == 15)
+            return x
+        op("t", f, base + " " + rk, w)
+
+    def every(n, X):
+        return " ".join(n + "b%d" % b for b in PIECES[X])
+
+    def pieces(X):
+        for i, b in enumerate(PIECES[X]):
+            yield "b%d" % b, slice(512 * i, 512 * i + 512), slice(CQ[X].start + 32 * i, CQ[X].start + 32 * i + 32)
+
+    TBANK = {"A": "b7", "B": "b6"}
+    CBANK = {"A": "b5", "B": "b6"}
+    CREG = {"A": T.b5[:, 0:96], "B": T.b6[:, 256:320]}
+    LBANK = {"A": "b7", "B": "b6"}
+    LREG = {"A": T.b7[:, 0:96], "B": T.b6[:, 320:384]}
+
+    def counts(t, s, X):
+        for bk, p, cq in pieces(X):
+            kw = T.kt[:, 0:W0 + B * t].indirect(T.cl[:, cq])
+            if t + s == 0:
+                vcp(T["kap" + X][:, p], kw, KT + " cl" + X, "kap" + bk)
+            else:
+                vtt(T["kap" + X][:, p], kw, T["ne" + X][:, p], KT + " cl" + X + " ne" + bk, "kap" + bk, OP.mult)
+
+    def total(X):
+        selmm(T[TBANK[X]][:, 0:NQ[X]], TBANK[X], "selt", T["kap" + X], every("kap", X))
+
+    def suffixes(t, X):
+        act(T["gg" + X][:], T.gt[:, 0:W0 + B * t].indirect(T.cl[:, CQ[X]]), GT + " cl" + X, "gg" + X, AF.Copy)
+
+    def targets(st, X):
+        c = CQ[X]
+        tk = TBANK[X]
+        tp = T[tk][:, 0:NQ[X]]
+        sc = slice(st * 160 + c.start, st * 160 + c.stop)
+        vts(T.pp[:, c], tp, tk, "pp" + X, 1.0 / 32, OP.mult, 0.25, OP.subtract)
+        vtt(T.vs[:, c], tp, T.v1[:, sc], tk + " v1_%d" % st, "vs" + X, OP.mult)
+        vtt(T.wp[:, c], T.pp[:, c], T.v31[:, sc], "pp" + X + " v31_%d" % st, "wp" + X, OP.mult)
+        vtt(T.vs[:, c], T.vs[:, c], T.wp[:, c], "vs" + X + " wp" + X, "vs" + X, OP.subtract)
+        vts(T.qq[:, c], T.vs[:, c], "vs" + X, "qq" + X, 1.0 / 256, OP.mult, 1024.0 - 127.5 / 256, OP.add)
+
+    def compare(X):
+        for bk, p, cq in pieces(X):
+            def f(bk=bk, p=p, cq=cq):
+                PE.matmul(T[bk][:], M["tri"], T["kap" + X][:, p], True, False)
+                for r in range(16):
+                    x = PE.matmul(T[bk][:, r::16], T.expa[:, 128 * r:128 * r + 128], T.qq[:, cq], False, r == 15)
+                return x
+            op("t", f, "tri kap" + bk + " qq" + X + " " + EXPA, bk)
+            act(T["cd" + X][:, p], T[bk][:], bk, "cd" + bk, AF.Sigmoid, bias=-16.0 * (32768 - 24), scale=-16.0)
+
+    def suffix_sum(X):
+        ap = T.b6[:, 64 + CQ[X].start:64 + CQ[X].stop]
+        selmm(ap, "b6", "selF", T["gg" + X], "gg" + X)
+        act(T.ff[:, CQ[X]], ap, "b6", "ff" + X, AF.Copy, bias=65536.0)
+
+    def first_sum(X):
+        selmm(CREG[X], CBANK[X], "selS", T["gg" + X], "gg" + X, True, False)
+
+    def pointer(t, X):
+        for bk, p, cq in pieces(X):
+            vtt(T["ds" + X][:, p], T.dtb[:, 0:W0 + B * t].indirect(T.cl[:, cq]), T["cd" + X][:, p], DT + " cl" + X + " cd" + bk, "ds" + bk, OP.mult)
+
+    def pointer_sum(X):
+        selmm(CREG[X], CBANK[X], "seld", T["ds" + X], every("ds", X), False, True)
+
+    def context(s, X, new):
+        c = CQ[X]
+        vtt(T.mm[:, c], CREG[X], T.ff[:, c], CBANK[X] + " ff" + X, "mm" + X, OP.min)
+        if X == "A":
+            vts(T.e8[:], T.b5[:, 0:8], "b5", "e8", 70000.0, OP.is_gt)
+        if s == 1:
+            vts(T.es[:, c], CREG[X], CBANK[X], "es" + X, 70000.0, OP.is_gt)
+        vts(T[new][:, c], T.mm[:, c], "mm" + X, new + X, 4095, OP.bitwise_and)
+        vcp(T.cl[:, c], T[new][:, c], new + X, "cl" + X)
+
+    def mark_piece(s, X, bk, p):
+        mms(T[bk][:], [(M["i14"], T["kap" + X][:, p]), (M["e15"], T["ds" + X][:, p])], "i14 e15 kap" + bk + " ds" + bk, bk)
+        if s == 0:
+            act(T["ne" + X][:, p], T[bk][:], bk, "ne" + bk, AF.Sigmoid, bias=256.0 * (2.0 ** 23 - 0.5), scale=-256.0)
+        else:
+            act(T["em" + X][:, p], T[bk][:], bk, "em" + bk, AF.Sign, bias=-(2.0 ** 23 - 0.5))
+
+    def slots(X):
+        c = CQ[X]
+        ik = "inc0" if X == "A" else "incA"
+        mms(T.b7[:, c], [(M["tri"], T.es[:, c]), (M["n8k"], T.es[:, c])], "tri n8k es" + X, "b7")
+        mms(T.b6[:, 0:NQ[X]], [(M["blk"], T.es[:, c])], "blk es" + X, "b6")
+        op("v", lambda: V.tensor_tensor_scan(T.inc[:, 8 + c.start:8 + c.stop], T.b6[:, 0:NQ[X]], T.zer[:, 0:NQ[X]], T.inc[:, 7 + c.start:8 + c.start], OP.add, OP.add), "b6 zer " + ik, "inc" + X)
+        vtt(T.sa[:, c], T.inc[:, 7 + c.start:7 + c.stop], T.b7[:, c], "b7 inc" + X + " " + ik, "sa" + X, OP.add)
+        vtt(T.sb2[:, c], T.sa[:, c], T.jg[:, c], "jg sa" + X, "sb" + X, OP.min)
+        vcp(T.sl[:, c], T.sb2[:, c], "sb" + X, "sl" + X)
+        vts(T.rl[:, c], T.sa[:, c], "sa" + X, "rl" + X, float(CAP), OP.min)
+
+    def first_escape(old):
+        hold = HCUR[0]
+        hnew = "h1" if hold == "h0" else "h0"
+        vts(T.ht[:], T[hold][:], hold, "ht", 0.0, OP.is_equal)
+        vtt(T.ht[:], T.ht[:], T[old][:, 0:8], "ht " + old + "A", "ht", OP.mult)
+        vtt(T.ht[:], T.ht[:], T[hold][:], "ht " + hold, "ht", OP.add)
+        vtt(T[hnew][:], T.ht[:], T.e8[:], "ht e8", hnew, OP.mult)
+        HCUR[0] = hnew
+
+    def flip():
+        old = CUR[0]
+        CUR[0] = "cc" if old == "ca" else "ca"
+        return old, CUR[0]
+
+    def send(t):
+        if t < RO - 1:
+            vlist(SP * t + 2)
+            vlist(SP * t + 3)
+        for X in XS:
+            for bk, p, cq in pieces(X):
+                pwi = T.pw[:].indirect(T.sl[:, cq])
+                if t < RO - 1:
+                    vtt(pwi, T["gg" + X][:, p], T["em" + X][:, p], "sl" + X + " lg" + bk + " em" + bk, "pw", OP.mult)
+                else:
+                    vcp(pwi, T["gg" + X][:, p], "sl" + X + " lg" + bk, "pw")
+        deps("g", ["pw"], [])
+        dst = T.cores[(rank + 1) % len(T.cores)]
+        src = T.cores[(rank - 1) % len(T.cores)]
+        rid, pid, _se = topo.addr(dst)
+        g.remote_dma(T["rb%d" % t][:, 0:CAP], T.pw[:, 0:CAP], T.sem["arr%d" % t], T.sem["snt%d" % t], pid, rid, topo.mask(core, dst))
+        cnt["snt%d" % t] = len(topo.engines(core, dst))
+        cnt["arr%d" % t] = len(topo.engines(src, core))
+        mark(("rem", "snt%d" % t, cnt["snt%d" % t]), ["pw"], [])
+        lw["rb%d" % t] = ("rem", "arr%d" % t, cnt["arr%d" % t])
+        if t < RO - 1:
+            fill(T.pw[:, 0:CAP], [[0, CAP]], 0, "pw")
+
+    PEND = []
+
+    def hop_recv(t):
+        old, new = flip()
+        PEND[:] = [old, new]
+        RB = "rb%d rbx%d" % (t, t)
+        win = T["rb%d" % t][:, 0:CAP + 16]
+        for X in XS:
+            ggk = "gg" + X + " " + every("lg", X)
+            if t == RO - 1:
+                act(T["gg" + X][:], win.indirect(T.rl[:, CQ[X]]), RB + " rl" + X, ggk, AF.Abs)
+                selmm(LREG[X], LBANK[X], "selS", T["gg" + X], "gg" + X)
+                continue
+            act(T["cd" + X][:], win.indirect(T.rl[:, CQ[X]]), RB + " rl" + X, every("cd", X), AF.Copy)
+            act(T["gg" + X][:], T["cd" + X][:], every("cd", X), ggk, AF.Abs)
+            selmm(LREG[X], LBANK[X], "selS", T["gg" + X], "gg" + X)
+            for bk, p, cq in pieces(X):
+                mms(T[bk][:], [(M["idb"], T["cd" + X][:, p]), (M["nhf"], T["em" + X][:, p])], "idb nhf cd" + bk + " em" + bk, bk)
+                act(T["ne" + X][:, p], T[bk][:], bk, "ne" + bk, AF.Sigmoid, scale=256.0)
+        link_context(t, "A")
+        if t == RO - 1:
+            link_context(t, "B")
+        else:
+            h = HCUR[0]
+            vtt(T[h][:], T[h][:], T.nr[:, 0:8], h + " nrA", h, OP.mult)
+
+    def link_context(t, X):
+        old, new = PEND
+        c = CQ[X]
+        vts(T.nr[:, c], LREG[X], LBANK[X], "nr" + X, 1.0, OP.is_lt)
+        vts(T.rc[:, c], LREG[X], LBANK[X], "rc" + X, 130.0, OP.subtract, 0.0, OP.max)
+        vtt(T.c1[:, c], T[old][:, c], T.nr[:, c], old + X + " nr" + X, "c1" + X, OP.mult)
+        if t < RO - 1:
+            vtt(T[new][:, c], T.c1[:, c], T.rc[:, c], "c1" + X + " rc" + X, new + X, OP.add)
+            vcp(T.cl[:, c], T[new][:, c], new + X, "cl" + X)
+        else:
+            vtt(T.yo[:, c], T.c1[:, c], T.rc[:, c], "c1" + X + " rc" + X, "yo" + X, OP.add)
+
+    def write_back(t, old, hb):
+        full = t < RO - 1
+        cur = CUR[0]
+        wn = W0 + B * t
+        wsl = slice(wn, wn + B)
+        l8 = T.cl[:, 0:8]
+        lf = T.fdu[:, 0:8]
+        vts(T.cnd[:], T.e8[:], "e8", "cnd", 8192.0, OP.mult)
+        vtt(T.cnd[:], T[hb][:], T.cnd[:], hb + " cnd", "cnd", OP.is_gt)
+        vts(T.ka[:, 0:8], T[hb][:], hb, "ka0", 3840.0, OP.subtract)
+        vts(T.ka[:, 8:16], T[old][:, 0:8], old + "A", "ka1", 3840.0, OP.subtract)
+        vts(T.fdu[:], T.ka[:], "ka0 ka1", "fdu", 3840.0, OP.add)
+        vtt(T.ka[:, 0:8], T.ka[:, 0:8], T.cnd[:], "ka0 cnd", "ka0", OP.mult)
+        vtt(T.ka[:, 8:16], T.ka[:, 8:16], T.cnd[:], "ka1 cnd", "ka1", OP.mult)
+        vts(T.k16[:, 0:16], T.ka[:], "ka0 ka1", "k16a", 2048.0, OP.add)
+        vts(T.k32[:], T.ka[:], "ka0 ka1", "k32", 2048.0, OP.add, -32.0, OP.mult)
+        nk = 16
+        if full:
+            nk = 32
+            vts(T.dgi[:, 0:8], T[cur][:, 0:8], cur + "A", "dgi0", 63, OP.bitwise_and)
+            vts(T.dgi[:, 8:16], T[cur][:, 0:8], cur + "A", "dgi1", 6, OP.arith_shift_right)
+            vcp(T.k16[:, 16:32], T.dgi[:], "dgi0 dgi1", "k16b")
+
+        def frow():
+            for r in range(16):
+                x = PE.matmul(T.b7[:, r:16 * nk:16], T.expa[:, 128 * r:128 * r + 128], T.k16[:, 0:nk], True, True)
+            return x
+        op("t", frow, EXPA + " k16a k16b", "b7")
+        mms(T.b5[:, 0:B], [(M["moh"], T.cdA[:, 0:B]), (M["mz0"], T.ones[:, 0:B])], "moh cdb0 mz0 ones", "b5")
+        act(T.ohf[:], T.b5[:, 0:B], "b5", "ohf", AF.Copy)
+        act(T.oh3[:], T.b5[:, 0:B], "b5", "oh3", AF.Copy, scale=32.0)
+        act(T.o33[:], T.b5[:, 0:B], "b5", "o33", AF.Copy, bias=-EPS, scale=33.0 + EPS)
+        act(T.kf[:], T.kt[:, 0:wn].indirect(lf), KT + " fdu", "kf", AF.Copy)
+        act(T.k2[:], T.kf[:], "kf", "k2", AF.Copy, bias=33.0, scale=-1.0)
+        if full:
+            act(T.xv[:], T.xf[:, 0:B], "xf", "xv", AF.Copy, bias=float(wn))
+            act(T.wv[:], T.wdl[:], "wdl " + key(W2 + t), "wv", AF.Identity, bias=col(W2 + t))
+            act(T.ohb[:], T.b5[:, 0:B], "b5", "ohb", AF.Copy)
+            act(T.g1[:], T.gt[:, 0:wn].indirect(l8), GT + " clA " + key(R01), "g1", AF.Copy, scale=col(R01))
+            act(T.gf[:], T.gt[:, 0:wn].indirect(lf), GT + " fdu", "gf", AF.Copy)
+            act(T.lt[:, wsl], T.lt[:, 0:wn].indirect(l8), LT + " clA", LT, AF.Copy)
+        for k in range(2):
+            for p in range(8):
+                i = 8 * k + p
+                vts(T.eq[:, i, 0:B - 16 * p], T.b7[:, B * k + 16 * p:B * k + B], "b7 k32", "eq%d" % i, T.k32[:, i:i + 1], OP.is_equal)
+        eqs = " ".join("eq%d" % i for i in range(16))
+        vtt(T.eq[:, :, 0:16], T.eq[:, :, 0:16], T.msk[:, :, :], eqs + " " + " ".join("msk%d" % h for h in range(16)), eqs, OP.mult)
+        vts(T.cr[:], T.b7[:, 0:256], "b7", "cr", -65536.0, OP.is_gt, 1.0, OP.subtract)
+        if full:
+            act(T.xt[:], T.b7[:, 256:384], "b7 " + key(Q2), "xt", AF.Copy, scale=col(Q2))
+            act(T.xw[:], T.b7[:, 384:512], "b7 " + key(Q3), "xw", AF.Copy, scale=col(Q3))
+
+        def fc():
+            for k in range(2):
+                for p in range(8):
+                    x = PE.matmul(T.b6[:, B * k + 16 * p:B * k + B], M["blk"], T.eq[:, 8 * k + p, 0:B - 16 * p], p == 0, p == 7)
+            return x
+        op("t", fc, "blk " + eqs, "b6")
+        dj = " dja0 dja1 djb0 djb1"
+        vts(T.chi[:], T.kt[:, 0:wn].indirect(l8), KT + " clA", "chi", 1.0 / 64, OP.mult, 0.25, OP.add)
+        vtt(T.fy[:], T.k32[:], T.dja[:], "k32" + dj, "fy", OP.add)
+        vtt(T.k2[:], T.k2[:], T.ohf[:], "k2 ohf", "k2", OP.mult)
+        vtt(T.kr[:], T.b6[:, 0:256], T.cr[:], "b6 cr", "kr", OP.is_le)
+        selmm(T.b5[:, 128:144], "b5", "selt", T.kr, "kr")
+        vtt(T.chf[:], T.chi[:], T.kr[:, 0:B], "chi kr", "chf", OP.mult)
+        vts(T.cm[:], T.chf[:], "chf", "cm", 1.0, OP.min, 1.0 + EPS, OP.mult)
+        vts(T.chf[:], T.chf[:], "chf", "chf", 32.0, OP.mult, EPS, OP.subtract)
+        vtt(T.fy[:], T.b5[:, 128:144], T.fy[:], "b5 fy", "fy", OP.mult)
+        vtt(T.fy[:], T.fy[:], T.djb[:], "fy" + dj, "fy", OP.add)
+        vts(T.lw[:], T.fy[:], "fy", "lw", -1.0 / 512, OP.mult)
+        vtt(T.kt[:, wsl], T.chf[:], T.cm[:], "chf cm", KT, OP.add)
+        vtt(T.kt[:].indirect(T.lw[:, 0:8]), T.kf[:], T.k2[:], "kf k2 lw", KT, OP.add)
+        if full:
+            vcp(T.xi[:], T.tb[:, 0:wn].indirect(lf), TB + " fdu", "xi")
+            vcp(T.tb[:, wsl], T.tb[:, 0:wn].indirect(l8), TB + " clA", TB)
+            vts(T.dtb[:, wsl], T.dtb[:, 0:wn].indirect(l8), DT + " clA " + key(D15), DT, col(D15), OP.max)
+            vts(T.xi[:], T.xi[:], "xi", "xi", 4, OP.arith_shift_right)
+            vtt(T.xv[:], T.xv[:], T.xi[:], "xv xi", "xv", OP.subtract)
+            vtt(T.xv[:], T.xv[:], T.ohf[:], "xv ohf", "xv", OP.mult)
+            vtt(T.xv[:], T.xv[:], T.xi[:], "xv xi", "xv", OP.add)
+            vts(T.s16[:, 0:B], T.xv[:], "xv", "s16", 1792.0, OP.subtract)
+            mms(T.b5[:, 0:B], [(M["mdf"], T.s16[:, 0:B]), (M["mfl"], T.ones[:, 0:B])], "mdf mfl s16 ones", "b5")
+            vts(T.xs[:], T.xv[:], "xv", "xs", 16.0, OP.mult)
+            vcp(T.tb[:].indirect(T.lw[:, 0:8]), T.xs[:], "xs lw", TB)
+        vtt(T.k2[:], T.kt[:, 0:wn].indirect(T.fdu[:, 8:16]), T.oh3[:], KT + " fdu oh3", "k2", OP.add)
+        vts(T.k2[:], T.k2[:], "k2", "k2", 481.0, OP.min)
+        vtt(T.kt[:].indirect(T.lw[:, 8:16]), T.k2[:], T.o33[:], "k2 o33 lw", KT, OP.max)
+        if not full:
+            return
+        vcp(T.rr[:, 0:B], T.b5[:, 0:B], "b5", "rr0")
+        vtt(T.xd[:], T.b5[:, 0:B], T.rr[:, 0:B], "b5 rr0", "xd", OP.subtract)
+        vcp(T.dtb[:].indirect(T.lw[:, 0:8]), T.xd[:], "xd lw", DT)
+        mms(T.b6[:, 0:B], [(M["mz1"], T.ohb[:])], "mz1 ohb", "b6")
+        vtt(T.xt[:], T.xt[:], T.xw[:], "xt xw", "xt", OP.add)
+        vtt(T.gt[:, wsl], T.xt[:], T.g1[:], "xt g1", GT, OP.add)
+        vtt(T.wv[:], T.wv[:], T.gf[:], "wv gf", "wv", OP.subtract)
+        vtt(T.g2[:], T.b6[:, 0:B], T.wv[:], "b6 wv", "g2", OP.mult)
+        vtt(T.gt[:].indirect(T.lw[:, 0:8]), T.gf[:], T.g2[:], "gf g2 lw", GT, OP.add)
+
+    for t in range(RO):
+        for s in range(SP):
+            st = SP * t + s
+            if s == 0:
+                if t == 0:
+                    digits()
+                    pointers(0)
+                    vlist(0)
+                    vlist(1)
+                counts(t, 0, "A")
+                total("A")
+                if t > 0:
+                    suffixes(t, "A")
+                    link_context(t - 1, "B")
+                else:
+                    pointers(1)
+                    suffixes(t, "A")
+            targets(st, "A")
+            compare("A")
+            counts(t, s, "B")
+            total("B")
+            targets(st, "B")
+            if st == 0:
+                pointers(2)
+            if s == 1:
+                first_escape(old)
+                hb = HCUR[0]
+            compare("B")
+            suffix_sum("A")
+            first_sum("A")
+            suffixes(t, "B")
+            if st == 0:
+                late_constants()
+            pointer(t, "A")
+            pointer(t, "B")
+            old, new = flip()
+            pointer_sum("A")
+            context(s, "A", new)
+            if s == 0:
+                for bk, p, cq in pieces("A"):
+                    mark_piece(0, "A", bk, p)
+            suffix_sum("B")
+            first_sum("B")
+            pointer_sum("B")
+            if s == 0:
+                for bk, p, cq in pieces("B"):
+                    mark_piece(0, "B", bk, p)
+                counts(t, 1, "A")
+                context(0, "B", new)
+                total("A")
+                suffixes(t, "A")
+                continue
+            for X in XS:
+                if X == "B":
+                    context(1, "B", new)
+                slots(X)
+                for bk, p, cq in pieces(X):
+                    act(T["gg" + X][:, p], T.lt[:, 0:W0 + B * t].indirect(T.cl[:, cq]), LT + " cl" + X, "gg" + X + " lg" + bk, AF.Copy)
+                    if t < RO - 1:
+                        mark_piece(1, X, bk, p)
+        send(t)
+        if t < RO - 1:
+            first_escape(old)
+        write_back(t, old, hb)
+        if t == RO - 1:
+            for h in range(2):
+                p = slice(W // 2 * h, W // 2 * (h + 1))
+                act(T.ynb[:, p], T.kt[:, p], KT, "yn%d" % h, AF.Relu, bias=-1.0 / 32, scale=1.0 / 32)
+                dma("y", T.yn[:, p], T.ynb[:, p], "ld%d" % (8 + h), "yn%d" % h, "")
+        hop_recv(t)
+    dma("y", T.yc[:, :], T.yo[:], "ld10", "yoA yoB", "")
+    for s in sorted(cnt):
+        need("g", s, cnt[s])

@@ -1,44 +1,44 @@
-from concourse.mybir import dt, AluOpType as OP, ActivationFunctionType as AF
+from concourse.mybir import AluOpType as OP, ActivationFunctionType as AF
 
 EPS = 2.0 ** -14
+MAGIC = 1.5 * 2.0 ** 23
 W0, B, LN, RO, SP, CAP = 3072, 128, 2560, 4, 2, 768
 W = W0 + RO * B
 WD = W + B
-XS = "AB"
-CQ = {"A": slice(0, 96), "B": slice(96, 160)}
-NQ = {"A": 96, "B": 64}
-PIECES = {"A": [0, 1, 2], "B": [3, 4]}
+PG = 4096
+MID = 1792
+BASE = 33024
+SU = 2.0 ** -14
+OWN = (RO - 1) * CAP
+CH = {"A": (0, 96), "B": (96, 160)}
+PIECES = {"A": (0, 1, 2), "B": (3, 4)}
+TB = {"A": "b5", "B": "b6"}
 
 _F, _H, _I, _B, _U = "float32", "float16", "int32", "bfloat16", "uint16"
+MATS = ["id", "nid", "blk", "ntri", "i14", "e15", "slt", "blks", "mdf", "moh", "blkw", "blk2", "i31", "i512", "mv", "m150", "u1", "l1", "low"]
+SELS = ["selt", "vsel", "seln", "lsel", "nsel", "sel2", "sel3"]
 SCRATCH = {}
 for _n, _w, _d in (
-        ("tb", WD, _I), ("kt", WD, _F), ("dtb", WD, _F), ("gt", WD, _B), ("lt", WD, _B),
-        ("ci", 1024, _I), ("cb", 1024, _B), ("sg", 1024, _B), ("cb2", 1024, _B), ("sg2", 1024, _B), ("si", 1024, _I), ("s16", 1024, _H), ("rr", 1024, _I),
-        ("dn", 576, _I), ("dg", 1152, _I), ("dgb", 1152, _B), ("v1", 1280, _F), ("v31", 1280, _F),
-        ("iop", 1, _I), ("pi", 2, _I), ("xf", 160, _F), ("xg", 128, _F), ("xr", 128, _F),
-        ("pc", 32, _F), ("oh16", 16, _F), ("m32", 16, _F), ("jg", 160, _F), ("dja", 16, _F), ("djb", 16, _F),
-        ("mats", 14 * 128, _B), ("sels", 5 * 160, _B), ("expa", 2048, _B), ("ones", 512, _B), ("tm1", 128, _F), ("tm2", 128, _F), ("tm3", 128, _I),
-        ("ca", 160, _I), ("cc", 160, _I), ("cl", 160, _U), ("pp", 160, _I), ("vs", 160, _F), ("wp", 160, _F), ("qq", 160, _H),
-        ("ff", 160, _F), ("mm", 160, _I), ("es", 160, _B), ("inc", 168, _F), ("zer", 96, _F), ("sa", 160, _F), ("sb2", 160, _F),
-        ("sl", 160, _U), ("rl", 160, _U), ("nr", 160, _F), ("c1", 160, _F), ("rc", 160, _F), ("yo", 160, _F), ("pw", 2 * LN, _B),
-        ("h0", 8, _F), ("h1", 8, _F), ("ht", 8, _F), ("e8", 8, _F), ("cnd", 8, _F), ("dgi", 16, _I),
-        ("ka", 16, _F), ("k32", 16, _F), ("k16", 32, _H), ("fdu", 16, _U), ("fy", 16, _F), ("lw", 16, _U),
-        ("kr", 256, _B), ("cr", 256, _F), ("ohb", 128, _B), ("ohf", 128, _F), ("oh3", 128, _F), ("o33", 128, _F),
-        ("chi", 128, _I), ("chf", 128, _F), ("cm", 128, _F), ("kf", 128, _F), ("k2", 128, _F), ("xi", 128, _I), ("xs", 128, _I),
-        ("xt", 128, _F), ("xw", 128, _F), ("xv", 128, _F), ("xd", 128, _F), ("wv", 128, _F), ("g1", 128, _B), ("g2", 128, _B), ("gf", 128, _B),
-        ("wdl", 128, _F), ("ynb", W, _B)):
+        ("tb", W0, _I), ("kt", WD, _F), ("dt", PG + WD, _F), ("lf", WD, _B), ("ynb", WD, _B), ("ci", 1536, _I), ("s16", 1536, _H), ("rb", 1024, _B),
+        ("dn", 384, _I), ("dg", 576, _I), ("dgb", 384, _B), ("lfd", 384, _B), ("fd", 192, _F), ("fl", 192, _U), ("lp", W0, _B), ("c1k", WD // 16, _F),
+        ("v8", 1280, _F), ("iop", 1, _I), ("pi", 2, _I), ("xf", 160, _B), ("xg", 128, _B), ("xr", 256, _B), ("pc", 32, _F), ("oh16", 16, _F), ("m31", 16, _F),
+        ("mats", 128 * len(MATS), _B), ("sels", 160 * len(SELS), _B), ("f32m", 384, _F), ("expa", 2048, _B), ("c32k", 96, _B),
+        ("th0", 256, _B), ("th1", 256, _B), ("th2", 16, _F), ("th3", 16, _F), ("thr", 256, _B), ("jg", 640, _F), ("dj", 16, _F),
+        ("ca", 160, _I), ("cl", 160, _U), ("c2", 160, _U), ("cf", 160, _F), ("r32", 160, _H), ("qq", 160, _H), ("yy", 160, _F), ("rr", 160, _F),
+        ("es", 160, _B), ("inc", 168, _F), ("zer", 96, _F), ("sa", 160, _F), ("sx", 160, _F), ("sl", 160, _U), ("rl", 160, _U), ("nr", 160, _F),
+        ("cw", 160, _F), ("yo", 160, _F), ("nsi", 4 * RO, _F), ("nsf", 1, _F),
+        ("kap", LN, _H), ("ds", LN, _H), ("cd", LN, _B), ("ne", LN, _B), ("val", LN, _B), ("lg", LN, _B),
+        ("win", OWN + LN, _B), ("rb3", CAP + 16, _B), ("pw", W0 + LN, _B),
+        ("h0", 8, _F), ("h1", 8, _F), ("ht", 8, _F), ("hz", 8, _F), ("e8", 8, _F), ("cnd", 8, _F), ("ka", 16, _F), ("k32", 16, _F), ("k16", 24, _H),
+        ("nc", 16, _H), ("fdu", 16, _U), ("fy", 16, _F), ("lw", 16, _U), ("eq", 16 * B, _B), ("kr", 256, _B),
+        ("ohb", B, _B), ("ohf", B, _F), ("up", B, _F), ("lo", B, _F), ("cap", B, _F), ("gro", B, _F), ("zr", B, _B), ("hx", B, _B), ("hy", B, _F),
+        ("xa", B, _F), ("xb", B, _B), ("nob", B, _B), ("g1", B, _B), ("af", B, _F), ("wr", B, _F), ("dl", B, _F), ("ax", B, _F), ("ar", B, _F)):
     SCRATCH[_n] = ("sbuf", [128, _w], _d)
-SCRATCH["vr"] = ("sbuf", [8, 20480], _B)
-SCRATCH["eq"] = ("sbuf", [128, 16, 128], _B)
-SCRATCH["msk"] = ("sbuf", [128, 16, 16], _B)
-for _x in XS:
-    for _n, _d in (("kap", _H), ("ds", _H), ("gg", _B), ("ne", _B), ("em", _B), ("cd", _B)):
-        SCRATCH[_n + _x] = ("sbuf", [128, 16 * NQ[_x]], _d)
-for _k in range(RO):
-    SCRATCH["rb%d" % _k] = ("sbuf", [128, CAP + 16], _B)
+SCRATCH["vr"] = ("sbuf", [8, RO * SP * LN], _B)
 for _k in range(8):
     SCRATCH["b%d" % _k] = ("psum", [128, 512], _F)
-SEMAPHORES = ["cv", "ct", "cs", "cg"] + ["ld%d" % k for k in range(16)] + ["gd%d" % k for k in range(6)] + ["arr%d" % k for k in range(RO)] + ["snt%d" % k for k in range(RO)]
+SEMAPHORES = (["cv", "ct", "cs", "cg"] + ["ld%d" % k for k in range(20)]
+              + [n + str(k) for k in range(RO) for n in ("arr", "snt", "nar", "nsn")])
 
 
 def rank_program(g, core, T, topo):
@@ -47,591 +47,662 @@ def rank_program(g, core, T, topo):
         return
     E = {"v": g.vector, "t": g.tensor, "s": g.scalar, "g": g, "y": g.sync}
     V, S, PE = g.vector, g.scalar, g.tensor
-    cnt, waited, lw, lr = {}, {}, {}, {}
+    cnt, waited, seen = {}, {}, {}
+
+    def A(name, lo=0, hi=None, step=1, rows=None):
+        if hi is None:
+            hi = T[name].shape[1]
+        ap = T[name][slice(None) if rows is None else rows, lo:hi:step] if step > 1 else T[name][slice(None) if rows is None else rows, lo:hi]
+        return (ap, [(name, lo, hi)])
+
+    def IX(win, off):
+        return (win[0].indirect(off[0]), win[1], off[1])
 
     def need(eng, sem, val):
         if waited.get((eng, sem), 0) < val:
             E[eng].wait_ge(T.sem[sem], val)
             waited[(eng, sem)] = val
 
-    def deps(eng, r, w):
+    def ranges(ins, outs):
+        rd, wr = [], []
+        for x in ins:
+            if isinstance(x, tuple):
+                rd += x[1] + (x[2] if len(x) > 2 else [])
+        for x in outs:
+            wr += x[1]
+            rd += x[2] if len(x) > 2 else []
+        return [r + (False,) for r in rd] + [r + (True,) for r in wr]
+
+    def psum(name):
+        return len(name) == 2 and name[0] == "b"
+
+    def order(eng, acc):
         todo = {}
-        ds = [lw[k] for k in list(r) + list(w) if k in lw]
-        for k in w:
-            ds += list(lr.get(k, {}).values())
-        for d in ds:
-            if not (d[0] == eng == "t"):
-                todo[d[1]] = max(todo.get(d[1], 0), d[2])
+        for name, lo, hi, w in acc:
+            for l, h, pw, pe, sem, val in seen.get(name, []):
+                if pe == eng == "t":
+                    continue
+                if (psum(name) and pe != eng) or (l < hi and lo < h and (w or pw)):
+                    todo[sem] = max(todo.get(sem, 0), val)
         for s in todo:
             need(eng, s, todo[s])
 
-    def mark(d, r, w):
-        for k in w:
-            lw[k] = d
-            lr[k] = {}
-        for k in r:
-            if k not in w:
-                lr.setdefault(k, {})[d[1]] = d
+    def record(acc, eng, sem, val):
+        for name, lo, hi, w in acc:
+            old = seen.get(name, [])
+            if psum(name):
+                old = [e for e in old if e[3] == eng]
+            seen[name] = [e for e in old if not (lo <= e[0] and e[1] <= hi and (w or (not e[2] and e[4] == sem)))] + [(lo, hi, w, eng, sem, val)]
 
-    def op(eng, fn, r="", w=""):
-        r = r.split()
-        w = w.split()
-        w = w + [k for k in r if len(k) == 2 and k[0] == "b" and k not in w]
-        deps(eng, r, w)
-        sem = "c" + eng
-        cnt[sem] = cnt.get(sem, 0) + 1
-        fn().then_inc(T.sem[sem], 1)
-        mark((eng, sem, cnt[sem]), r, w)
+    held = []
 
-    def dma(eng, out, in_, sem, r="", w=""):
-        r = r.split()
-        w = w.split()
-        deps(eng, r, w)
-        cnt[sem] = cnt.get(sem, 0) + 16
-        E[eng].dma_start(out, in_).then_inc(T.sem[sem], 16)
-        mark(("dma", sem, cnt[sem]), r, w)
-
-    def vts(out, in0, r, w, s1, o0, s2=None, o1=None):
-        if o1 is None:
-            op("v", lambda: V.tensor_scalar(out, in0, s1, None, o0), r, w)
+    def issue(eng, fn):
+        if held:
+            held[-1].append((eng, fn))
         else:
-            op("v", lambda: V.tensor_scalar(out, in0, s1, s2, o0, o1), r, w)
+            fn()
 
-    def vtt(out, a, b, r, w, alu):
-        op("v", lambda: V.tensor_tensor(out, a, b, alu), r, w)
+    def chain(*parts):
+        held.append([])
+        for p in parts:
+            p[0](*p[1:])
+        out = [[]]
+        for e in held.pop():
+            if e[0] == "v" and any(x[0] == "v" for x in out[-1]):
+                out.append([])
+            out[-1].append(e)
+        return out
 
-    def vcp(out, in_, r, w):
-        op("v", lambda: V.tensor_copy(out, in_), r, w)
+    def weave(*chains):
+        for k in range(max(len(c) for c in chains)):
+            for c in chains:
+                for e in (c[k] if k < len(c) else []):
+                    issue(*e)
 
-    def fill(out, pattern, base, w, cm=0):
-        op("g", lambda: g.iota(out, pattern, base, cm, allow_small_or_imprecise_dtypes=True), "", w)
+    def op(eng, fn, ins, outs):
+        def go():
+            acc = ranges(ins, outs)
+            order(eng, acc)
+            sem = "c" + eng
+            cnt[sem] = cnt.get(sem, 0) + 1
+            fn().then_inc(T.sem[sem], 1)
+            record(acc, eng, sem, cnt[sem])
+        issue(eng, go)
 
-    def act(out, in_, r, w, func, bias=0.0, scale=1.0):
-        op("s", lambda: S.activation(out, in_, func, bias=bias, scale=scale), r, w)
+    nd = [0]
 
-    def mms(out, pairs, r, w):
+    def dma(eng, out, in_):
+        def go():
+            sem = "ld%d" % nd[0]
+            nd[0] += 1
+            acc = ranges([in_], [out])
+            order(eng, acc)
+            cnt[sem] = 16
+            E[eng].dma_start(out[0], in_[0]).then_inc(T.sem[sem], 16)
+            record(acc, "d", sem, 16)
+        issue(eng, go)
+
+    def ap(x):
+        return x[0] if isinstance(x, tuple) else x
+
+    def ts(out, a, s1, o0, s2=None, o1=None):
+        if o1 is None:
+            op("v", lambda: V.tensor_scalar(out[0], a[0], ap(s1), None, o0), [a, s1], [out])
+        else:
+            op("v", lambda: V.tensor_scalar(out[0], a[0], ap(s1), ap(s2), o0, o1), [a, s1, s2], [out])
+
+    def tt(out, a, b, alu):
+        op("v", lambda: V.tensor_tensor(out[0], a[0], b[0], alu), [a, b], [out])
+
+    def cp(out, a):
+        op("v", lambda: V.tensor_copy(out[0], a[0]), [a], [out])
+
+    def scan(out, a, b, init, o0, o1):
+        op("v", lambda: V.tensor_tensor_scan(out[0], a[0], b[0], ap(init), o0, o1), [a, b, init], [out])
+
+    def fill(out, pattern, base, cm=0):
+        op("g", lambda: g.iota(out[0], pattern, base, cm, allow_small_or_imprecise_dtypes=True), [], [out])
+
+    def act(out, a, func=AF.Copy, bias=0.0, scale=1.0):
+        op("s", lambda: S.activation(out[0], a[0], func, bias=ap(bias), scale=ap(scale)), [a, bias, scale], [out])
+
+    def mm(items, group=True):
         def f():
-            for i, (a, b) in enumerate(pairs):
-                x = PE.matmul(out, a, b, i == 0, i == len(pairs) - 1)
+            for i, (o, l, r) in enumerate(items):
+                x = PE.matmul(o[0], l[0], r[0], i == 0 or not group, i == len(items) - 1 or not group)
             return x
-        op("t", f, r, w)
+        op("t", f, [x for it in items for x in it[1:]], [it[0] for it in items])
 
-    for k in range(3):
-        dma("y", T.tb[:, 1024 * k:1024 * k + 1024], T.tab[:, 1024 * k:1024 * k + 1024], "ld%d" % k, "", "tb%d" % k)
-    dma("s", T.ca[:], T.cx[:, :], "ld6", "", "caA caB")
-    dma("s", T.vr[:, :], T.vv[:, :], "ld7", "", "vr")
-    dma("s", T.dn[:, 384:576], T.tab[0::16, :], "ld3", "", "dnt")
-    dma("s", T.dn[:, 0:192], T.suf[:, :], "ld4", "", "dnf")
-    dma("s", T.dn[:, 192:384], T.lnk[:, :], "ld5", "", "dnl")
+    def M(n):
+        i = MATS.index(n)
+        return A("mats", 128 * i, 128 * i + 128)
 
-    PGC, PRC, PFC, P16, PM1, PP1, A1, A2, C15, WDc, WSc, WFc, R01, N15, D15, T1, T2, NPR, Q2, Q3, W2 = range(21)
+    def SEL(n, r=None, rows=None):
+        i = 160 * SELS.index(n)
+        return A("sels", i, i + 160) if r is None else A("sels", i + 16 - r, i + 144 - r, rows=rows)
+
+    def tolist(out, sel, name, lo, hi):
+        return [(out, SEL(sel, r), A(name, lo + r, hi, 16)) for r in range(16)]
+
+    def spread(bank, lo, n, src):
+        return [(A(bank, lo + r, lo + 16 * n, 16), A("expa", 128 * r, 128 * r + 128), src) for r in range(16)]
+
+    def X(name, x, base=0):
+        return A(name, base + CH[x][0], base + CH[x][1])
+
+    def TX(x, k):
+        n = CH[x][1] - CH[x][0]
+        return A(TB[x], 96 * k, 96 * k + n)
+
+    def P(name, p, base=0):
+        return A(name, base + 512 * p, base + 512 * p + 512)
+
+    def L(name, p):
+        return A(name, 32 * p, 32 * p + 32)
+
+    def BK(p, lo=0, hi=512):
+        return A("b%d" % p, lo, hi)
+
+    for k in range(4):
+        dma("y", A("tb", 768 * k, 768 * k + 768), (T.tab[:, 768 * k:768 * k + 768], []))
+    dma("s", A("dn", 0, 192), (T.suf[:, :], []))
+    dma("s", A("dn", 192, 384), (T.lnk[:, :], []))
+    dma("s", A("ca"), (T.cx[:, :], []))
+    dma("s", A("vr", 0, SP * LN), (T.vv[:, 0:SP * LN], []))
+    dma("y", A("vr", SP * LN, RO * SP * LN), (T.vv[:, SP * LN:RO * SP * LN], []))
+
+    PGC, PRC, PFC, P16, PM1, PP1, N15, N0, T1, C15, CW, PS, PB, LS, R23, PM2, PM15, J0 = range(18)
 
     def col(i):
-        return T.pc[:, i:i + 1]
+        return A("pc", i, i + 1)
 
-    def key(i):
-        return "pc%d" % i
-    fill(T.iop[:], [[1, 1]], 0, "iop", 1)
-    fill(col(PFC), [[1, 1]], 0, key(PFC), 1)
-    fill(T.xf[:], [[1, 160]], 0, "xf")
-    fill(T.xg[:], [[1, 8], [0, 16]], 0, "xg")
-    fill(T.xr[:], [[0, 8], [1, 16]], 0, "xr")
-    fill(T.ones[:], [[0, 512]], 1, "ones")
-    GT = "gtx gt0 gt1 gt2 gt3"
-    LT = "ltx lt0 lt1"
-    fill(T.dtb[:, W0:WD], [[0, WD - W0]], 0, "dtx")
-    fill(T.gt[:], [[0, WD]], 0, GT)
-    fill(T.lt[:], [[0, WD]], -2, LT)
-    fill(T.h0[:], [[0, 8]], 0, "h0")
-    fill(T.inc[:, 0:8], [[0, 8]], 8191, "inc0")
-    fill(T.zer[:], [[0, 96]], 0, "zer")
-    for k in range(RO):
-        fill(T["rb%d" % k][:, CAP:CAP + 16], [[0, 16]], 0, "rbx%d" % k)
-    fill(T.tb[:, W0:WD], [[0, WD - W0]], 0, "tbx")
-    fill(T.tm3[:], [[1, 128]], 0, "tm3")
-    fill(T.pw[:, 0:CAP], [[0, CAP]], 0, "pw")
+    def oh(i):
+        return A("oh16", i, i + 1)
+    xm = A("xf", 0, 128)
+    fill(A("iop"), [[1, 1]], 0, 1)
+    fill(col(PFC), [[1, 1]], 0, 1)
+    fill(A("xf"), [[1, 160]], 0)
+    fill(A("xg"), [[1, 8], [0, 16]], 0)
+    fill(A("xr"), [[0, 16], [1, 16]], 0)
+    fill(A("c32k"), [[0, 96]], BASE)
+    fill(A("zer"), [[0, 96]], 0)
+    fill(A("c1k"), [[0, WD // 16]], 1024)
+    fill(A("dt", W0, PG + WD), [[0, PG + WD - W0]], 0)
+    fill(A("h0"), [[0, 8]], 0)
+    fill(A("pw", 0, CAP), [[0, CAP]], 0)
+    fill(A("rb3", CAP, CAP + 16), [[0, 16]], 0)
 
-    vts(T.pi[:, 0:1], T.iop[:], "iop", "pi", 4, OP.arith_shift_right)
-    vts(T.pi[:, 1:2], T.iop[:], "iop", "pi1", 15, OP.bitwise_and)
-    vcp(col(PGC), T.pi[:, 0:1], "pi", key(PGC))
-    vcp(col(PRC), T.pi[:, 1:2], "pi1", key(PRC))
-    vts(T.oh16[:], T.xf[:, 0:16], "xf " + key(PRC), "oh16", col(PRC), OP.is_equal)
+    def places():
+        ts(A("pi", 0, 1), A("iop"), 4, OP.arith_shift_right)
+        ts(A("pi", 1, 2), A("iop"), 15, OP.bitwise_and)
+        ts(col(T1), col(PFC), 16.0, OP.mult, 16.0, OP.add)
+        cp(A("pc", PGC, PRC + 1), A("pi"))
+        for i, k in ((PP1, 1.0), (PM15, -15.0), (PM1, -1.0), (PM2, -2.0)):
+            ts(col(i), col(PFC), k, OP.add)
+        ts(A("oh16"), A("xf", 0, 16), col(PRC), OP.is_equal)
+        ts(M("blk"), A("xg"), col(PGC), OP.is_equal)
+        ts(A("m31"), A("oh16"), 31.0 / 32, OP.mult)
+        for r in range(16):
+            act(A("expa", 128 * r, 128 * r + 128), M("blk"), scale=A("m31", r, r + 1))
+        ts(SEL("vsel"), A("xf"), col(T1), OP.is_equal)
+        ts(M("id"), xm, col(PFC), OP.is_equal)
+        ts(col(P16), col(PGC), 16.0, OP.mult, 16.0, OP.add)
+        ts(col(N15), oh(15), -1.0, OP.mult, 1.0, OP.add)
+        ts(col(C15), oh(15), 1.0 / 4096, OP.mult)
+        ts(M("low"), A("xr", 0, 128), col(PRC), OP.is_gt)
+        ts(SEL("selt"), A("xf"), col(P16), OP.is_equal)
+        ts(M("u1"), xm, col(PP1), OP.is_equal, col(N15), OP.mult)
+        tt(M("low"), M("low"), M("blk"), OP.mult)
+        ts(M("nid"), M("id"), -1.0, OP.mult)
+        tt(A("f32m", 256, 384), M("id"), M("u1"), OP.subtract)
+        ts(M("m150"), xm, col(PM15), OP.is_equal, col(C15), OP.mult)
+        ts(M("mdf"), A("f32m", 256, 384), 1.0 / 4096, OP.mult)
+        ts(M("ntri"), M("low"), -1.0, OP.mult)
+        ts(M("i14"), M("id"), 2.0 ** 14, OP.mult)
+        ts(M("e15"), M("blk"), oh(15), OP.mult, 2.0 ** 13, OP.mult)
 
-    def ohc(i):
-        return T.oh16[:, i:i + 1]
-    names = ["ida", "idb", "idc", "mdf", "mfl", "blk", "tri", "i14", "n8k", "e15", "moh", "mz0", "mz1", "nhf"]
-    M = {n: T.mats[:, 128 * i:128 * i + 128] for i, n in enumerate(names)}
-    M.update({n: T.sels[:, 160 * i:160 * i + 160] for i, n in enumerate(["selt", "seld", "selS", "selF", "vsel"])})
-    xm = T.xf[:, 0:128]
+    def lanes():
+        cp(A("cl"), A("ca"))
+        ts(A("cf"), A("ca"), float(MID), OP.subtract, 1.0 / 4096, OP.mult)
 
-    def mat(out, name, c, m, extra=""):
-        vts(out, xm, "xf " + key(c) + " " + extra, name, col(c), OP.is_equal, m, OP.mult)
-
-    def colop(i, src, srck, s1, o0, s2=None, o1=None):
-        vts(col(i), src, srck, key(i), s1, o0, s2, o1)
-    mat(M["ida"], "ida", PFC, 32.0)
-    mat(M["idb"], "idb", PFC, 1.0)
-    mat(M["idc"], "idc", PFC, EPS)
-    vts(M["blk"], T.xg[:], "xg " + key(PGC), "blk", col(PGC), OP.is_equal)
-    vts(T.m32[:], T.oh16[:], "oh16", "m32", -32.0, OP.mult)
-    for r in range(16):
-        act(T.expa[:, 128 * r:128 * r + 128], M["blk"], "blk m32", "expa%d" % r, AF.Copy, scale=T.m32[:, r:r + 1])
-    EXPA = " ".join("expa%d" % r for r in range(16))
-    colop(T1, col(PFC), key(PFC), 16.0, OP.mult, 16.0, OP.add)
-    vts(M["vsel"], T.xf[:], "xf " + key(T1), "vsel", col(T1), OP.is_equal)
-    colop(P16, col(PGC), key(PGC), 16.0, OP.mult, 16.0, OP.add)
-    vts(M["selt"], T.xf[:], "xf " + key(P16), "selt", col(P16), OP.is_equal)
-    vts(T.tm1[:], T.xr[:], "xr " + key(PRC), "tm1", col(PRC), OP.is_ge)
-    vtt(M["tri"], T.tm1[:], M["blk"], "tm1 blk", "tri", OP.mult)
-    colop(PM1, col(PFC), key(PFC), 1.0, OP.subtract)
-    colop(A1, ohc(0), "oh16", -1.0 / 4096, OP.mult, 1.0 / 4096, OP.add)
-    colop(A2, ohc(15), "oh16", 1.0 / 4096, OP.mult, -1.0 / 4096, OP.add)
-    mat(T.tm1[:], "tm1", PM1, col(A1), key(A1))
-    mat(T.tm2[:], "tm2", PFC, col(A2), key(A2))
-    vtt(M["mdf"], T.tm1[:], T.tm2[:], "tm1 tm2", "mdf", OP.add)
-    vts(M["mfl"], M["idb"], "idb oh16", "mfl", ohc(15), OP.mult, 0.25, OP.mult)
-    colop(N15, ohc(15), "oh16", -1.0, OP.mult, 1.0, OP.add)
-    colop(WDc, ohc(15), "oh16", 2.0 ** 19 - 4096.0, OP.mult, 4096.0, OP.add)
-    colop(WSc, ohc(1), "oh16", 64.0, OP.mult, ohc(0), OP.add)
-    colop(WFc, ohc(3), "oh16", 64.0, OP.mult, ohc(2), OP.add)
-    for n, c in (("seld", WDc), ("selS", WSc), ("selF", WFc)):
-        vts(M[n], T.xf[:], "xf " + key(P16) + " " + key(c), n, col(P16), OP.is_equal, col(c), OP.mult)
-    colop(C15, ohc(15), "oh16", 2.0 ** 25, OP.mult)
-    mat(M["i14"], "i14", PFC, 2.0 ** 14)
-    vts(M["e15"], M["blk"], "blk " + key(C15), "e15", col(C15), OP.mult)
-
-    pb = [0]
-
-    def nextbank():
-        pb[0] += 1
-        return "b%d" % (pb[0] % 7)
-    for k in range(3):
-        c0 = 1024 * k
-        cb, sg = ("cb", "sg") if k % 2 == 0 else ("cb2", "sg2")
-        vts(T.ci[:], T.tb[:, c0:c0 + 1024], "tb%d" % k, "ci", 15, OP.bitwise_and)
-        vcp(T[cb][:], T.ci[:], "ci", cb)
-        act(T[sg][:], T[cb][:], cb, sg, AF.Sign)
-        for h in range(2):
-            p = slice(512 * h, 512 * h + 512)
-            bk = nextbank()
-            mms(T[bk][:], [(M["ida"], T[cb][:, p]), (M["idb"], T[sg][:, p]), (M["idc"], T[sg][:, p])], "ida idb idc " + cb + " " + sg, bk)
-            act(T.kt[:, c0 + 512 * h:c0 + 512 * h + 512], T[bk][:], bk, "kt%d%d" % (k, h), AF.Copy, bias=-EPS)
-    act(T.kt[:, W0:WD], T.dtb[:, W0:WD], "dtx", "ktx", AF.Copy, bias=-EPS)
-    KT = "ktx " + " ".join("kt%d%d" % (k, h) for k in range(3) for h in range(2))
-    DT = "dtx " + " ".join("dt%d%d" % (k, h) for k in range(3) for h in range(2))
-    TB = "tbx tb0 tb1 tb2"
-
-    def digits():
-        q = 192
-        vts(T.dg[:, 0:q], T.dn[:, 384:576], "dnt", "dg0", 4, OP.arith_shift_right, 63, OP.bitwise_and)
-        vts(T.dg[:, q:2 * q], T.dn[:, 384:576], "dnt", "dg1", 10, OP.arith_shift_right)
-        vts(T.dg[:, 2 * q:3 * q], T.dn[:, 0:192], "dnf", "dg2", 63, OP.bitwise_and)
-        vts(T.dg[:, 3 * q:4 * q], T.dn[:, 0:192], "dnf", "dg3", 6, OP.arith_shift_right)
-        vts(T.dg[:, 4 * q:5 * q], T.dn[:, 192:384], "dnl", "dg4", 63, OP.bitwise_and)
-        vts(T.dg[:, 5 * q:6 * q], T.dn[:, 192:384], "dnl", "dg5", 6, OP.arith_shift_right)
-        vcp(T.dgb[:, 0:4 * q], T.dg[:, 0:4 * q], "dg0 dg1 dg2 dg3", "dgb0")
-        vts(T.dgb[:, 4 * q:6 * q], T.dg[:, 4 * q:6 * q], "dg4 dg5", "dgb1", -1.0, OP.mult, -2.0, OP.add)
-        for k in range(4):
-            dma("y", T.gt[k::16, 0:W0], T.dgb[:, k * q:k * q + q], "gd%d" % k, "dgb0", "gt%d" % k)
-        for k in range(2):
-            dma("y", T.lt[k::16, 0:W0], T.dgb[:, (4 + k) * q:(5 + k) * q], "gd%d" % (4 + k), "dgb1", "lt%d" % k)
-
-    def pointers(k):
-        c0 = 1024 * k
-        vts(T.si[:], T.tb[:, c0:c0 + 1024], "tb%d" % k, "si", 4, OP.arith_shift_right)
-        vts(T.s16[:], T.si[:], "si", "s16", 1792.0, OP.subtract)
-        for h in range(2):
-            p = slice(512 * h, 512 * h + 512)
-            bk = "b%d" % (2 * (k % 2) + h)
-            mms(T[bk][:], [(M["mdf"], T.s16[:, p]), (M["mfl"], T.ones[:])], "mdf mfl s16 ones", bk)
-            vcp(T.rr[:, p], T[bk][:], bk, "rr%d" % h)
-            vtt(T.dtb[:, c0 + 512 * h:c0 + 512 * h + 512], T[bk][:], T.rr[:, p], bk + " rr%d" % h, "dt%d%d" % (k, h), OP.subtract)
-        if k == 0:
-            vts(T.dtb[:, 0:1], T.dtb[:, 0:1], "dt00 " + key(N15), "dt00", col(N15), OP.mult)
-
-    def late_constants():
-        colop(PP1, col(PFC), key(PFC), 1.0, OP.add)
-        colop(R01, ohc(0), "oh16", ohc(1), OP.add)
-        colop(D15, ohc(15), "oh16", 10.25, OP.mult, -10.0, OP.add)
-        colop(T2, col(PRC), key(PRC), 2560.0, OP.add)
-        colop(NPR, col(PRC), key(PRC), -1.0, OP.mult)
-        colop(Q2, ohc(2), "oh16", -1.0 / 32, OP.mult)
-        colop(Q3, ohc(3), "oh16", -1.0 / 32, OP.mult)
-        for t in range(RO - 1):
-            colop(W2 + t, ohc(1), "oh16", 2.0 * t, OP.mult)
-        act(T.jg[:], T.xf[:], "xf " + key(T2), "jg", AF.Identity, bias=col(T2), scale=16.0)
-        for h in range(16):
-            act(T.msk[:, h, :], T.xf[:, 0:16], "xf " + key(NPR), "msk%d" % h, AF.Relu, bias=col(NPR))
-        for h in range(2):
-            o = slice(8 * h, 8 * h + 8)
-            vts(T.dja[:, o], T.jg[:, 0:8], "jg", "dja%d" % h, float(W - 2560 - 1792), OP.add, 32.0, OP.mult)
-            vts(T.djb[:, o], T.jg[:, 0:8], "jg", "djb%d" % h, float(W - 2560), OP.add, -512.0, OP.mult)
-        mat(M["n8k"], "n8k", PFC, -8192.0)
-        mat(M["nhf"], "nhf", PFC, -0.5)
-        mat(T.tm1[:], "tm1", PP1, col(N15), key(N15))
-        mat(T.tm2[:], "tm2", PFC, col(N15), key(N15))
-        vtt(M["moh"], T.tm1[:], T.tm2[:], "tm1 tm2", "moh", OP.subtract)
-        mat(M["mz0"], "mz0", PFC, ohc(0), "oh16")
-        mat(T.tm1[:], "tm1", PP1, ohc(0), "oh16")
-        vtt(M["mz1"], T.tm1[:], M["mz0"], "tm1 mz0", "mz1", OP.add)
-        vts(T.xi[:], T.tm3[:], "tm3", "xi", 63, OP.bitwise_and)
-        vts(T.xs[:], T.tm3[:], "tm3", "xs", 6, OP.arith_shift_right)
-        vts(T.tm1[:], T.xi[:], "xi oh16", "tm1", ohc(0), OP.mult)
-        vts(T.tm2[:], T.xs[:], "xs oh16", "tm2", float(W0 // 64), OP.add, ohc(1), OP.mult)
-        vtt(T.wdl[:], T.tm1[:], T.tm2[:], "tm1 tm2", "wdl", OP.add)
-
-    def vlist(st):
-        mms(T.b7[:, 352:512], [(M["vsel"][0:8, 16 - r:144 - r], T.vr[0:8, st * LN + r:(st + 1) * LN:16]) for r in range(16)], "vsel vr", "b7")
-        act(T.v1[:, st * 160:st * 160 + 160], T.b7[:, 352:512], "b7", "v1_%d" % st, AF.Copy)
-        act(T.v31[:, st * 160:st * 160 + 160], T.b7[:, 352:512], "b7", "v31_%d" % st, AF.Copy, scale=31.0)
-
-    CUR = ["ca"]
-    HCUR = ["h0"]
-    for X in XS:
-        vcp(T.cl[:, CQ[X]], T.ca[:, CQ[X]], "ca" + X, "cl" + X)
-
-    def selmm(out, w, base, rhs, rk, start=True, stop=True):
-        def f():
-            for r in range(16):
-                x = PE.matmul(out, M[base][:, 16 - r:144 - r], rhs[:, r::16], start and r == 0, stop and r == 15)
-            return x
-        op("t", f, base + " " + rk, w)
-
-    def every(n, X):
-        return " ".join(n + "b%d" % b for b in PIECES[X])
-
-    def pieces(X):
-        for i, b in enumerate(PIECES[X]):
-            yield "b%d" % b, slice(512 * i, 512 * i + 512), slice(CQ[X].start + 32 * i, CQ[X].start + 32 * i + 32)
-
-    TBANK = {"A": "b7", "B": "b6"}
-    CBANK = {"A": "b5", "B": "b6"}
-    CREG = {"A": T.b5[:, 0:96], "B": T.b6[:, 256:320]}
-    LBANK = {"A": "b7", "B": "b6"}
-    LREG = {"A": T.b7[:, 0:96], "B": T.b6[:, 320:384]}
-
-    def counts(t, s, X):
-        for bk, p, cq in pieces(X):
-            kw = T.kt[:, 0:W0 + B * t].indirect(T.cl[:, cq])
-            if t + s == 0:
-                vcp(T["kap" + X][:, p], kw, KT + " cl" + X, "kap" + bk)
-            else:
-                vtt(T["kap" + X][:, p], kw, T["ne" + X][:, p], KT + " cl" + X + " ne" + bk, "kap" + bk, OP.mult)
-
-    def total(X):
-        selmm(T[TBANK[X]][:, 0:NQ[X]], TBANK[X], "selt", T["kap" + X], every("kap", X))
-
-    def suffixes(t, X):
-        act(T["gg" + X][:], T.gt[:, 0:W0 + B * t].indirect(T.cl[:, CQ[X]]), GT + " cl" + X, "gg" + X, AF.Copy)
-
-    def targets(st, X):
-        c = CQ[X]
-        tk = TBANK[X]
-        tp = T[tk][:, 0:NQ[X]]
-        sc = slice(st * 160 + c.start, st * 160 + c.stop)
-        vts(T.pp[:, c], tp, tk, "pp" + X, 1.0 / 32, OP.mult, 0.25, OP.subtract)
-        vtt(T.vs[:, c], tp, T.v1[:, sc], tk + " v1_%d" % st, "vs" + X, OP.mult)
-        vtt(T.wp[:, c], T.pp[:, c], T.v31[:, sc], "pp" + X + " v31_%d" % st, "wp" + X, OP.mult)
-        vtt(T.vs[:, c], T.vs[:, c], T.wp[:, c], "vs" + X + " wp" + X, "vs" + X, OP.subtract)
-        vts(T.qq[:, c], T.vs[:, c], "vs" + X, "qq" + X, 1.0 / 256, OP.mult, 1024.0 - 127.5 / 256, OP.add)
-
-    def compare(X):
-        for bk, p, cq in pieces(X):
-            def f(bk=bk, p=p, cq=cq):
-                PE.matmul(T[bk][:], M["tri"], T["kap" + X][:, p], True, False)
-                for r in range(16):
-                    x = PE.matmul(T[bk][:, r::16], T.expa[:, 128 * r:128 * r + 128], T.qq[:, cq], False, r == 15)
-                return x
-            op("t", f, "tri kap" + bk + " qq" + X + " " + EXPA, bk)
-            act(T["cd" + X][:, p], T[bk][:], bk, "cd" + bk, AF.Sigmoid, bias=-16.0 * (32768 - 24), scale=-16.0)
-
-    def suffix_sum(X):
-        ap = T.b6[:, 64 + CQ[X].start:64 + CQ[X].stop]
-        selmm(ap, "b6", "selF", T["gg" + X], "gg" + X)
-        act(T.ff[:, CQ[X]], ap, "b6", "ff" + X, AF.Copy, bias=65536.0)
-
-    def first_sum(X):
-        selmm(CREG[X], CBANK[X], "selS", T["gg" + X], "gg" + X, True, False)
-
-    def pointer(t, X):
-        for bk, p, cq in pieces(X):
-            vtt(T["ds" + X][:, p], T.dtb[:, 0:W0 + B * t].indirect(T.cl[:, cq]), T["cd" + X][:, p], DT + " cl" + X + " cd" + bk, "ds" + bk, OP.mult)
-
-    def pointer_sum(X):
-        selmm(CREG[X], CBANK[X], "seld", T["ds" + X], every("ds", X), False, True)
-
-    def context(s, X, new):
-        c = CQ[X]
-        vtt(T.mm[:, c], CREG[X], T.ff[:, c], CBANK[X] + " ff" + X, "mm" + X, OP.min)
-        if X == "A":
-            vts(T.e8[:], T.b5[:, 0:8], "b5", "e8", 70000.0, OP.is_gt)
-        if s == 1:
-            vts(T.es[:, c], CREG[X], CBANK[X], "es" + X, 70000.0, OP.is_gt)
-        vts(T[new][:, c], T.mm[:, c], "mm" + X, new + X, 4095, OP.bitwise_and)
-        vcp(T.cl[:, c], T[new][:, c], new + X, "cl" + X)
-
-    def mark_piece(s, X, bk, p):
-        mms(T[bk][:], [(M["i14"], T["kap" + X][:, p]), (M["e15"], T["ds" + X][:, p])], "i14 e15 kap" + bk + " ds" + bk, bk)
-        if s == 0:
-            act(T["ne" + X][:, p], T[bk][:], bk, "ne" + bk, AF.Sigmoid, bias=256.0 * (2.0 ** 23 - 0.5), scale=-256.0)
-        else:
-            act(T["em" + X][:, p], T[bk][:], bk, "em" + bk, AF.Sign, bias=-(2.0 ** 23 - 0.5))
-
-    def slots(X):
-        c = CQ[X]
-        ik = "inc0" if X == "A" else "incA"
-        mms(T.b7[:, c], [(M["tri"], T.es[:, c]), (M["n8k"], T.es[:, c])], "tri n8k es" + X, "b7")
-        mms(T.b6[:, 0:NQ[X]], [(M["blk"], T.es[:, c])], "blk es" + X, "b6")
-        op("v", lambda: V.tensor_tensor_scan(T.inc[:, 8 + c.start:8 + c.stop], T.b6[:, 0:NQ[X]], T.zer[:, 0:NQ[X]], T.inc[:, 7 + c.start:8 + c.start], OP.add, OP.add), "b6 zer " + ik, "inc" + X)
-        vtt(T.sa[:, c], T.inc[:, 7 + c.start:7 + c.stop], T.b7[:, c], "b7 inc" + X + " " + ik, "sa" + X, OP.add)
-        vtt(T.sb2[:, c], T.sa[:, c], T.jg[:, c], "jg sa" + X, "sb" + X, OP.min)
-        vcp(T.sl[:, c], T.sb2[:, c], "sb" + X, "sl" + X)
-        vts(T.rl[:, c], T.sa[:, c], "sa" + X, "rl" + X, float(CAP), OP.min)
-
-    def first_escape(old):
-        hold = HCUR[0]
-        hnew = "h1" if hold == "h0" else "h0"
-        vts(T.ht[:], T[hold][:], hold, "ht", 0.0, OP.is_equal)
-        vtt(T.ht[:], T.ht[:], T[old][:, 0:8], "ht " + old + "A", "ht", OP.mult)
-        vtt(T.ht[:], T.ht[:], T[hold][:], "ht " + hold, "ht", OP.add)
-        vtt(T[hnew][:], T.ht[:], T.e8[:], "ht e8", hnew, OP.mult)
-        HCUR[0] = hnew
-
-    def flip():
-        old = CUR[0]
-        CUR[0] = "cc" if old == "ca" else "ca"
-        return old, CUR[0]
-
-    def send(t):
-        if t < RO - 1:
-            vlist(SP * t + 2)
-            vlist(SP * t + 3)
-        for X in XS:
-            for bk, p, cq in pieces(X):
-                pwi = T.pw[:].indirect(T.sl[:, cq])
-                if t < RO - 1:
-                    vtt(pwi, T["gg" + X][:, p], T["em" + X][:, p], "sl" + X + " lg" + bk + " em" + bk, "pw", OP.mult)
-                else:
-                    vcp(pwi, T["gg" + X][:, p], "sl" + X + " lg" + bk, "pw")
-        deps("g", ["pw"], [])
-        dst = T.cores[(rank + 1) % len(T.cores)]
-        src = T.cores[(rank - 1) % len(T.cores)]
-        rid, pid, _se = topo.addr(dst)
-        g.remote_dma(T["rb%d" % t][:, 0:CAP], T.pw[:, 0:CAP], T.sem["arr%d" % t], T.sem["snt%d" % t], pid, rid, topo.mask(core, dst))
-        cnt["snt%d" % t] = len(topo.engines(core, dst))
-        cnt["arr%d" % t] = len(topo.engines(src, core))
-        mark(("rem", "snt%d" % t, cnt["snt%d" % t]), ["pw"], [])
-        lw["rb%d" % t] = ("rem", "arr%d" % t, cnt["arr%d" % t])
-        if t < RO - 1:
-            fill(T.pw[:, 0:CAP], [[0, CAP]], 0, "pw")
-
-    PEND = []
-
-    def hop_recv(t):
-        old, new = flip()
-        PEND[:] = [old, new]
-        RB = "rb%d rbx%d" % (t, t)
-        win = T["rb%d" % t][:, 0:CAP + 16]
-        for X in XS:
-            ggk = "gg" + X + " " + every("lg", X)
-            if t == RO - 1:
-                act(T["gg" + X][:], win.indirect(T.rl[:, CQ[X]]), RB + " rl" + X, ggk, AF.Abs)
-                selmm(LREG[X], LBANK[X], "selS", T["gg" + X], "gg" + X)
-                continue
-            act(T["cd" + X][:], win.indirect(T.rl[:, CQ[X]]), RB + " rl" + X, every("cd", X), AF.Copy)
-            act(T["gg" + X][:], T["cd" + X][:], every("cd", X), ggk, AF.Abs)
-            selmm(LREG[X], LBANK[X], "selS", T["gg" + X], "gg" + X)
-            for bk, p, cq in pieces(X):
-                mms(T[bk][:], [(M["idb"], T["cd" + X][:, p]), (M["nhf"], T["em" + X][:, p])], "idb nhf cd" + bk + " em" + bk, bk)
-                act(T["ne" + X][:, p], T[bk][:], bk, "ne" + bk, AF.Sigmoid, scale=256.0)
-        link_context(t, "A")
-        if t == RO - 1:
-            link_context(t, "B")
-        else:
-            h = HCUR[0]
-            vtt(T[h][:], T[h][:], T.nr[:, 0:8], h + " nrA", h, OP.mult)
-
-    def link_context(t, X):
-        old, new = PEND
-        c = CQ[X]
-        vts(T.nr[:, c], LREG[X], LBANK[X], "nr" + X, 1.0, OP.is_lt)
-        vts(T.rc[:, c], LREG[X], LBANK[X], "rc" + X, 130.0, OP.subtract, 0.0, OP.max)
-        vtt(T.c1[:, c], T[old][:, c], T.nr[:, c], old + X + " nr" + X, "c1" + X, OP.mult)
-        if t < RO - 1:
-            vtt(T[new][:, c], T.c1[:, c], T.rc[:, c], "c1" + X + " rc" + X, new + X, OP.add)
-            vcp(T.cl[:, c], T[new][:, c], new + X, "cl" + X)
-        else:
-            vtt(T.yo[:, c], T.c1[:, c], T.rc[:, c], "c1" + X + " rc" + X, "yo" + X, OP.add)
-
-    def write_back(t, old, hb):
-        full = t < RO - 1
-        cur = CUR[0]
-        wn = W0 + B * t
-        wsl = slice(wn, wn + B)
-        l8 = T.cl[:, 0:8]
-        lf = T.fdu[:, 0:8]
-        vts(T.cnd[:], T.e8[:], "e8", "cnd", 8192.0, OP.mult)
-        vtt(T.cnd[:], T[hb][:], T.cnd[:], hb + " cnd", "cnd", OP.is_gt)
-        vts(T.ka[:, 0:8], T[hb][:], hb, "ka0", 3840.0, OP.subtract)
-        vts(T.ka[:, 8:16], T[old][:, 0:8], old + "A", "ka1", 3840.0, OP.subtract)
-        vts(T.fdu[:], T.ka[:], "ka0 ka1", "fdu", 3840.0, OP.add)
-        vtt(T.ka[:, 0:8], T.ka[:, 0:8], T.cnd[:], "ka0 cnd", "ka0", OP.mult)
-        vtt(T.ka[:, 8:16], T.ka[:, 8:16], T.cnd[:], "ka1 cnd", "ka1", OP.mult)
-        vts(T.k16[:, 0:16], T.ka[:], "ka0 ka1", "k16a", 2048.0, OP.add)
-        vts(T.k32[:], T.ka[:], "ka0 ka1", "k32", 2048.0, OP.add, -32.0, OP.mult)
-        nk = 16
-        if full:
-            nk = 32
-            vts(T.dgi[:, 0:8], T[cur][:, 0:8], cur + "A", "dgi0", 63, OP.bitwise_and)
-            vts(T.dgi[:, 8:16], T[cur][:, 0:8], cur + "A", "dgi1", 6, OP.arith_shift_right)
-            vcp(T.k16[:, 16:32], T.dgi[:], "dgi0 dgi1", "k16b")
-
-        def frow():
-            for r in range(16):
-                x = PE.matmul(T.b7[:, r:16 * nk:16], T.expa[:, 128 * r:128 * r + 128], T.k16[:, 0:nk], True, True)
-            return x
-        op("t", frow, EXPA + " k16a k16b", "b7")
-        mms(T.b5[:, 0:B], [(M["moh"], T.cdA[:, 0:B]), (M["mz0"], T.ones[:, 0:B])], "moh cdb0 mz0 ones", "b5")
-        act(T.ohf[:], T.b5[:, 0:B], "b5", "ohf", AF.Copy)
-        act(T.oh3[:], T.b5[:, 0:B], "b5", "oh3", AF.Copy, scale=32.0)
-        act(T.o33[:], T.b5[:, 0:B], "b5", "o33", AF.Copy, bias=-EPS, scale=33.0 + EPS)
-        act(T.kf[:], T.kt[:, 0:wn].indirect(lf), KT + " fdu", "kf", AF.Copy)
-        act(T.k2[:], T.kf[:], "kf", "k2", AF.Copy, bias=33.0, scale=-1.0)
-        if full:
-            act(T.xv[:], T.xf[:, 0:B], "xf", "xv", AF.Copy, bias=float(wn))
-            act(T.wv[:], T.wdl[:], "wdl " + key(W2 + t), "wv", AF.Identity, bias=col(W2 + t))
-            act(T.ohb[:], T.b5[:, 0:B], "b5", "ohb", AF.Copy)
-            act(T.g1[:], T.gt[:, 0:wn].indirect(l8), GT + " clA " + key(R01), "g1", AF.Copy, scale=col(R01))
-            act(T.gf[:], T.gt[:, 0:wn].indirect(lf), GT + " fdu", "gf", AF.Copy)
-            act(T.lt[:, wsl], T.lt[:, 0:wn].indirect(l8), LT + " clA", LT, AF.Copy)
-        for k in range(2):
-            for p in range(8):
-                i = 8 * k + p
-                vts(T.eq[:, i, 0:B - 16 * p], T.b7[:, B * k + 16 * p:B * k + B], "b7 k32", "eq%d" % i, T.k32[:, i:i + 1], OP.is_equal)
-        eqs = " ".join("eq%d" % i for i in range(16))
-        vtt(T.eq[:, :, 0:16], T.eq[:, :, 0:16], T.msk[:, :, :], eqs + " " + " ".join("msk%d" % h for h in range(16)), eqs, OP.mult)
-        vts(T.cr[:], T.b7[:, 0:256], "b7", "cr", -65536.0, OP.is_gt, 1.0, OP.subtract)
-        if full:
-            act(T.xt[:], T.b7[:, 256:384], "b7 " + key(Q2), "xt", AF.Copy, scale=col(Q2))
-            act(T.xw[:], T.b7[:, 384:512], "b7 " + key(Q3), "xw", AF.Copy, scale=col(Q3))
-
-        def fc():
-            for k in range(2):
-                for p in range(8):
-                    x = PE.matmul(T.b6[:, B * k + 16 * p:B * k + B], M["blk"], T.eq[:, 8 * k + p, 0:B - 16 * p], p == 0, p == 7)
-            return x
-        op("t", fc, "blk " + eqs, "b6")
-        dj = " dja0 dja1 djb0 djb1"
-        vts(T.chi[:], T.kt[:, 0:wn].indirect(l8), KT + " clA", "chi", 1.0 / 64, OP.mult, 0.25, OP.add)
-        vtt(T.fy[:], T.k32[:], T.dja[:], "k32" + dj, "fy", OP.add)
-        vtt(T.k2[:], T.k2[:], T.ohf[:], "k2 ohf", "k2", OP.mult)
-        vtt(T.kr[:], T.b6[:, 0:256], T.cr[:], "b6 cr", "kr", OP.is_le)
-        selmm(T.b5[:, 128:144], "b5", "selt", T.kr, "kr")
-        vtt(T.chf[:], T.chi[:], T.kr[:, 0:B], "chi kr", "chf", OP.mult)
-        vts(T.cm[:], T.chf[:], "chf", "cm", 1.0, OP.min, 1.0 + EPS, OP.mult)
-        vts(T.chf[:], T.chf[:], "chf", "chf", 32.0, OP.mult, EPS, OP.subtract)
-        vtt(T.fy[:], T.b5[:, 128:144], T.fy[:], "b5 fy", "fy", OP.mult)
-        vtt(T.fy[:], T.fy[:], T.djb[:], "fy" + dj, "fy", OP.add)
-        vts(T.lw[:], T.fy[:], "fy", "lw", -1.0 / 512, OP.mult)
-        vtt(T.kt[:, wsl], T.chf[:], T.cm[:], "chf cm", KT, OP.add)
-        vtt(T.kt[:].indirect(T.lw[:, 0:8]), T.kf[:], T.k2[:], "kf k2 lw", KT, OP.add)
-        if full:
-            vcp(T.xi[:], T.tb[:, 0:wn].indirect(lf), TB + " fdu", "xi")
-            vcp(T.tb[:, wsl], T.tb[:, 0:wn].indirect(l8), TB + " clA", TB)
-            vts(T.dtb[:, wsl], T.dtb[:, 0:wn].indirect(l8), DT + " clA " + key(D15), DT, col(D15), OP.max)
-            vts(T.xi[:], T.xi[:], "xi", "xi", 4, OP.arith_shift_right)
-            vtt(T.xv[:], T.xv[:], T.xi[:], "xv xi", "xv", OP.subtract)
-            vtt(T.xv[:], T.xv[:], T.ohf[:], "xv ohf", "xv", OP.mult)
-            vtt(T.xv[:], T.xv[:], T.xi[:], "xv xi", "xv", OP.add)
-            vts(T.s16[:, 0:B], T.xv[:], "xv", "s16", 1792.0, OP.subtract)
-            mms(T.b5[:, 0:B], [(M["mdf"], T.s16[:, 0:B]), (M["mfl"], T.ones[:, 0:B])], "mdf mfl s16 ones", "b5")
-            vts(T.xs[:], T.xv[:], "xv", "xs", 16.0, OP.mult)
-            vcp(T.tb[:].indirect(T.lw[:, 0:8]), T.xs[:], "xs lw", TB)
-        vtt(T.k2[:], T.kt[:, 0:wn].indirect(T.fdu[:, 8:16]), T.oh3[:], KT + " fdu oh3", "k2", OP.add)
-        vts(T.k2[:], T.k2[:], "k2", "k2", 481.0, OP.min)
-        vtt(T.kt[:].indirect(T.lw[:, 8:16]), T.k2[:], T.o33[:], "k2 o33 lw", KT, OP.max)
-        if not full:
-            return
-        vcp(T.rr[:, 0:B], T.b5[:, 0:B], "b5", "rr0")
-        vtt(T.xd[:], T.b5[:, 0:B], T.rr[:, 0:B], "b5 rr0", "xd", OP.subtract)
-        vcp(T.dtb[:].indirect(T.lw[:, 0:8]), T.xd[:], "xd lw", DT)
-        mms(T.b6[:, 0:B], [(M["mz1"], T.ohb[:])], "mz1 ohb", "b6")
-        vtt(T.xt[:], T.xt[:], T.xw[:], "xt xw", "xt", OP.add)
-        vtt(T.gt[:, wsl], T.xt[:], T.g1[:], "xt g1", GT, OP.add)
-        vtt(T.wv[:], T.wv[:], T.gf[:], "wv gf", "wv", OP.subtract)
-        vtt(T.g2[:], T.b6[:, 0:B], T.wv[:], "b6 wv", "g2", OP.mult)
-        vtt(T.gt[:].indirect(T.lw[:, 0:8]), T.gf[:], T.g2[:], "gf g2 lw", GT, OP.add)
-
-    for t in range(RO):
+    def targets_list(t):
         for s in range(SP):
             st = SP * t + s
-            if s == 0:
-                if t == 0:
-                    digits()
-                    pointers(0)
-                    vlist(0)
-                    vlist(1)
-                counts(t, 0, "A")
-                total("A")
-                if t > 0:
-                    suffixes(t, "A")
-                    link_context(t - 1, "B")
-                else:
-                    pointers(1)
-                    suffixes(t, "A")
-            targets(st, "A")
-            compare("A")
-            counts(t, s, "B")
-            total("B")
-            targets(st, "B")
-            if st == 0:
-                pointers(2)
-            if s == 1:
-                first_escape(old)
-                hb = HCUR[0]
-            compare("B")
-            suffix_sum("A")
-            first_sum("A")
-            suffixes(t, "B")
-            if st == 0:
-                late_constants()
-            pointer(t, "A")
-            pointer(t, "B")
-            old, new = flip()
-            pointer_sum("A")
-            context(s, "A", new)
-            if s == 0:
-                for bk, p, cq in pieces("A"):
-                    mark_piece(0, "A", bk, p)
-            suffix_sum("B")
-            first_sum("B")
-            pointer_sum("B")
-            if s == 0:
-                for bk, p, cq in pieces("B"):
-                    mark_piece(0, "B", bk, p)
-                counts(t, 1, "A")
-                context(0, "B", new)
-                total("A")
-                suffixes(t, "A")
-                continue
-            for X in XS:
-                if X == "B":
-                    context(1, "B", new)
-                slots(X)
-                for bk, p, cq in pieces(X):
-                    act(T["gg" + X][:, p], T.lt[:, 0:W0 + B * t].indirect(T.cl[:, cq]), LT + " cl" + X, "gg" + X + " lg" + bk, AF.Copy)
-                    if t < RO - 1:
-                        mark_piece(1, X, bk, p)
-        send(t)
+            mm([(BK(7, 160 * s, 160 * s + 160), SEL("vsel", r, slice(0, 8)), A("vr", st * LN + r, (st + 1) * LN, 16)) for r in range(16)])
+        act(A("v8", 320 * t, 320 * t + 320), BK(7, 0, 320), scale=0.125)
+
+    def counts_table(k):
+        c = A("ci", 0, 768)
+        q = A("kt", 768 * k, 768 * k + 768)
+        ts(c, A("tb", 768 * k, 768 * k + 768), 15, OP.bitwise_and)
+        ts(q, c, 31.0, OP.mult, 1.0, OP.max)
+        act(q, q, bias=-1.0 - EPS)
+
+    def pointer_table(k):
+        c = A("ci", 768, 1536)
+        o = 768 * (k % 2)
+        ts(c, A("tb", 768 * k, 768 * k + 768), 4, OP.arith_shift_right)
+        ts(A("s16", o, o + 768), c, float(MID), OP.subtract)
+        if k == 0:
+            mm([(BK(4, 0, 1), M("m150"), A("s16", 0, 1))])
+        hs = [(h, A("s16", o + 384 * h, o + 384 * h + 384), A("rb", 384 * h, 384 * h + 384)) for h in range(2)]
+        for h, s, rb in hs:
+            mm([(BK(h, 0, 384), M("mdf"), s)])
+            act(rb, BK(h, 0, 384), bias=192.0)
+        for h, s, rb in hs:
+            mm([(BK(2 + h, 0, 384), M("mdf"), s), (BK(2 + h, 0, 384), M("nid"), rb)])
+            act(A("dt", 768 * k + 384 * h, 768 * k + 384 * h + 384), BK(2 + h, 0, 384), bias=192.0)
+
+    def escape_page():
+        ts(A("fd"), A("dn", 0, 192), float(MID), OP.subtract, 1.0 / 4096, OP.mult)
+        dma("y", A("dt", PG, PG + W0, rows=slice(0, 128, 16)), A("fd"))
+        dma("y", A("dt", PG, PG + WD, rows=slice(15, 128, 16)), A("c1k"))
+
+    def root_page():
+        act(A("dt", PG, PG + 1), BK(4, 0, 1))
+        act(A("kt", W0, WD), A("dt", W0, WD), bias=-EPS)
+
+    def link_digits():
+        op("v", lambda: V.memset(T.lf[:], 0.0), [], [A("lf")])
+        ts(A("dg", 384, 576), A("dn", 192, 384), float(4096 - MID), OP.add)
+        cp(A("fl"), A("dn", 0, 192))
+        ts(A("dg", 0, 192), A("dg", 384, 576), 63, OP.bitwise_and)
+        ts(A("dg", 192, 384), A("dg", 384, 576), 6, OP.arith_shift_right, 63, OP.bitwise_and)
+        ts(A("dgb"), A("dg", 0, 384), 1.0 / 64, OP.mult)
+        for k in range(2):
+            dma("y", A("lf", 0, W0, rows=slice(2 + k, 128, 16)), A("dgb", 192 * k, 192 * k + 192))
+
+    def suffix_links():
+        act(A("lp"), IX(A("lf", 0, W0), A("fl")))
+
+    def suffix_links_back():
+        mm(tolist(BK(7, 0, 192), "sel2", "lp", 0, W0))
+        mm(tolist(BK(7, 192, 384), "sel3", "lp", 0, W0))
+        act(A("lfd"), BK(7, 0, 384))
+        for k in range(2):
+            dma("y", A("lf", 0, W0, rows=slice(k, 128, 16)), A("lfd", 192 * k, 192 * k + 192))
+
+    def hop_constants():
+        op("v", lambda: V.memset(T.inc[:, 0:8], 0.5), [], [A("inc", 0, 8)])
+        ts(M("slt"), M("id"), -2.0 ** 13, OP.mult)
+        ts(col(J0), col(PRC), float(CAP), OP.add, SU, OP.mult)
+        ts(col(LS), oh(0), 1.0 / 64, OP.mult, oh(1), OP.add)
+        tt(M("slt"), M("slt"), M("low"), OP.add)
+        ts(A("jg", 0, 160), A("xf"), 16 * SU, OP.mult, col(J0), OP.add)
+        ts(M("blks"), M("blk"), 2.0 ** -37, OP.mult)
+        ts(M("slt"), M("slt"), 2.0 ** -37, OP.mult)
+        ts(A("jg", 480, 640), A("jg", 0, 160), 3 * CAP * SU, OP.add)
+        ts(SEL("lsel"), SEL("selt"), col(LS), OP.mult)
+        ts(SEL("nsel"), SEL("selt"), oh(0), OP.mult, -1.0 / 64, OP.mult)
+        ts(SEL("sel2"), SEL("selt"), oh(2), OP.mult)
+        ts(SEL("sel3"), SEL("selt"), oh(3), OP.mult)
+
+    def write_back_constants():
+        ts(A("th0"), A("xr"), 0.0, OP.is_gt, 0.5, OP.mult)
+        ts(A("th1"), A("xr"), 0.0, OP.is_equal, 2.0, OP.mult)
+        ts(col(N0), oh(0), -1.0, OP.mult, 1.0, OP.add)
+        scan(A("thr"), A("th0"), A("th1"), 0.0, OP.mult, OP.add)
+        ts(M("l1"), xm, col(PM1), OP.is_equal, col(N0), OP.mult)
+        tt(A("th2"), A("thr", 0, 16), A("oh16"), OP.mult)
+        tt(M("moh"), M("id"), M("l1"), OP.subtract)
+        scan(A("th3"), A("th2"), A("zer", 0, 16), 0.0, OP.add, OP.add)
+        ts(col(R23), oh(2), oh(3), OP.add)
+        ts(M("blkw"), M("blk"), A("th3", 15, 16), OP.mult, 0.5, OP.mult)
+        ts(M("l1"), xm, col(PM2), OP.is_equal)
+        ts(col(PS), oh(0), 32.0 / 31 / 4096, OP.mult)
+        tt(M("l1"), M("l1"), M("id"), OP.add)
+        ts(col(PB), oh(15), 1024.0, OP.mult)
+        tt(A("f32m", 128, 256), M("ntri"), M("id"), OP.subtract)
+        ts(M("mv"), M("l1"), col(R23), OP.mult)
+        ts(M("blk2"), M("blk"), 2.0, OP.mult)
+        ts(M("i31"), M("id"), 31.0, OP.mult)
+        ts(M("i512"), M("id"), 512.0, OP.mult)
+        ts(SEL("seln"), SEL("selt"), -BASE / 16.0, OP.mult)
+        cp(A("f32m", 0, 128), M("id"))
+
+    def late_constants():
+        for h in range(2):
+            act(A("dj", 8 * h, 8 * h + 8), A("jg", 0, 8), bias=float(W - MID - CAP), scale=1 / SU)
+        for t in (1, 2):
+            act(A("jg", 160 * t, 160 * t + 160), A("jg", 0, 160), bias=t * CAP * SU)
+
+    def counts(t, s, x):
+        for p in PIECES[x]:
+            kw = IX(A("kt", 0, W0 + B * t), L("cl", p))
+            if t + s == 0:
+                cp(P("kap", p), kw)
+            else:
+                tt(P("kap", p), kw, P("ne", p), OP.mult)
+        n = CH[x][1] - CH[x][0]
+        mm([(TX(x, 0), M("id"), A("c32k", 0, n))] + tolist(TX(x, 0), "selt", "kap", 16 * CH[x][0], 16 * CH[x][1]))
+
+    def targets(st, x):
+        s = TX(x, 0)
+        ts(X("r32", x), s, 32.0 / 31, OP.mult, BASE - BASE * 32.0 / 31 + 8.25, OP.add)
+        tt(s, s, X("r32", x), OP.subtract)
+        tt(s, s, X("v8", x, 160 * st), OP.mult)
+        ts(X("qq", x), s, -1.0, OP.mult, BASE - 127.5 / 8, OP.add)
+
+    def page(x):
+        s = TX(x, 0)
+        tt(s, X("qq", x), X("r32", x), OP.is_ge)
+        tt(X("yy", x), s, X("cf", x), OP.add)
+        ts(X("c2", x), X("yy", x), 4096.0, OP.mult, float(MID), OP.add)
+
+    ESC = 1.0 - (MID - 0.5) / 4096
+
+    def compare(p):
+        mm([(BK(p), M("ntri"), P("kap", p))] + spread("b%d" % p, 0, 32, L("qq", p)))
+        act(P("cd", p), BK(p), AF.Sigmoid, bias=-16.0 * (BASE // 32 * 31 - 8), scale=16.0)
+
+    def pointer(t, p):
+        tt(P("ds", p), IX(A("dt", 0, PG + W0 + B * t), L("c2", p)), P("cd", p), OP.mult)
+
+    def pointer_sum(x):
+        mm(tolist(TX(x, 1), "selt", "ds", 16 * CH[x][0], 16 * CH[x][1]))
+
+    def context(x, k):
+        s = TX(x, k)
+        ts(X("rr", x), s, MAGIC, OP.add, MAGIC, OP.subtract)
+        tt(X("cf", x), s, X("rr", x), OP.subtract)
+        ts(X("cl", x), X("cf", x), 4096.0, OP.mult, float(MID), OP.add)
+
+    def marks0(p):
+        mm([(BK(p), M("i14"), P("kap", p)), (BK(p), M("e15"), P("ds", p))])
+        act(P("ne", p), BK(p), AF.Sigmoid, bias=256.0 * (2.0 ** 23 - 0.5), scale=-256.0)
+
+    def marks1(p):
+        mm([(BK(p), M("i14"), P("kap", p))] + spread("b%d" % p, 0, 32, L("es", p)))
+        act(P("win", p, OWN), BK(p), AF.Sigmoid, bias=256.0 * (31 * 2.0 ** 18 - 0.5), scale=-256.0)
+
+    H = ["h0", "h1"]
+
+    def no_f():
+        act(A("hz"), A(H[0]), AF.Relu, bias=1.0, scale=-8.0)
+
+    def first_escape():
+        old, new = H
+        ts(A("e8"), A("yy", 0, 8), ESC, OP.is_gt)
+        tt(A("ht"), A("hz"), A("yy", 0, 8), OP.mult)
+        tt(A("ht"), A("ht"), A(old), OP.add)
+        tt(A(new), A("ht"), A("e8"), OP.mult)
+        H.reverse()
+
+    def escapes(x):
+        ts(X("es", x), X("yy", x), ESC, OP.is_gt, 2.0 ** 23, OP.mult)
+        mm([(TX(x, 2), M("slt"), X("es", x))])
+        mm([(TX(x, 3), M("blks"), X("es", x))])
+
+    def slots(x):
+        lo, hi = CH[x]
+        scan(X("inc", x, 8), TX(x, 3), A("zer", 0, hi - lo), A("inc", 7 + lo, 8 + lo), OP.add, OP.add)
+        tt(X("sa", x), TX(x, 2), X("inc", x, 7), OP.add)
+        tt(X("sx", x), X("sa", x), X("jg", x, 160 * (RO - 1)), OP.min)
+        ts(X("sl", x), X("sx", x), 1 / SU, OP.mult)
+
+    dst = T.cores[(rank + 1) % len(T.cores)]
+    src = T.cores[(rank - 1) % len(T.cores)]
+
+    def remote(out, in_, arr, snt):
+        def go():
+            acc = ranges([in_], [])
+            order("g", acc)
+            rid, pid, _se = topo.addr(dst)
+            g.remote_dma(out[0], in_[0], T.sem[arr], T.sem[snt], pid, rid, topo.mask(core, dst))
+            cnt[snt] = len(topo.engines(core, dst))
+            cnt[arr] = len(topo.engines(src, core))
+            record(acc, "r", snt, cnt[snt])
+            record(ranges([], [out]), "r", arr, cnt[arr])
+        issue("g", go)
+
+    def landing(t):
+        return A("rb3", 0, CAP) if t == RO - 1 else A("win", OWN - CAP * (t + 1), OWN - CAP * t)
+
+    def links(t, x):
+        act(A("lg", 16 * CH[x][0], 16 * CH[x][1]), IX(A("lf", 0, W0 + B * t), X("cl", x)))
+
+    def scatter(t, p):
+        o = IX(A("pw"), L("sl", p))
         if t < RO - 1:
-            first_escape(old)
-        write_back(t, old, hb)
+            tt(o, P("lg", p), P("win", p, OWN), OP.add)
+        else:
+            cp(o, P("lg", p))
+
+    def reading_list(t):
+        ts(A("nsf"), A("nsi", 4 * t + 3, 4 * t + 4), 0.5, OP.subtract, CAP * SU, OP.min)
+        ts(A("nr"), A("sa"), A("nsf"), OP.is_ge)
+        tt(A("sx"), A("nr"), A("sa"), OP.add)
+        if t < RO - 1:
+            tt(A("sx"), A("sx"), A("jg", 160 * t, 160 * t + 160), OP.min)
+            ts(A("rl"), A("sx"), 1 / SU, OP.mult)
+        else:
+            ts(A("rl"), A("sx"), CAP * SU, OP.min, 1 / SU, OP.mult)
+
+    def receive(t, x):
+        last = t == RO - 1
+        win = A("rb3") if last else A("win", OWN - CAP * (t + 1), OWN + LN)
+        for p in PIECES[x]:
+            act(P("val", p), IX(win, L("rl", p)))
+
+    def flags(t, x):
+        last = t == RO - 1
+        lo, hi = 16 * CH[x][0], 16 * CH[x][1]
+        if not last:
+            act(A("ne", lo, hi), A("val", lo, hi), AF.Sigmoid, bias=-127.0 * 256, scale=2.0 ** 15)
+        mm(tolist(TX(x, 4), "lsel", "val", lo, hi) + ([] if last else tolist(TX(x, 4), "nsel", "ne", lo, hi)))
+
+    def link_context(t, x):
+        s = TX(x, 4)
+        tt(s, s, X("cw", x), OP.add)
+        if t < RO - 1:
+            context(x, 4)
+        else:
+            ts(X("rr", x), s, MAGIC, OP.add, MAGIC, OP.subtract)
+            tt(X("cf", x), s, X("rr", x), OP.subtract)
+            ts(X("yo", x), X("cf", x), 4096.0, OP.mult, float(MID), OP.add)
+
+    def wb_keys(t):
+        new, old = H
+        tt(A("cnd"), A(old), A(new), OP.is_gt)
+        tt(A("ka", 0, 8), A("ka", 0, 8), A("cnd"), OP.mult)
+        tt(A("ka", 8, 16), A("ka", 8, 16), A("cnd"), OP.mult)
+        ts(A("k16", 0, 16), A("ka"), 4096.0, OP.mult, 2048.0, OP.add)
+        mm(spread("b7", 0, 16, A("k16", 0, 16)), False)
+        ts(A("k32"), A("k16", 0, 16), 31.0 / 32, OP.mult)
+        ts(A("fdu"), A("k16", 0, 16), float(MID), OP.add, float(W0 + B * t - 1), OP.min)
+        ts(A("nc"), A("k16", 0, 16), 2048.0, OP.is_equal, 4.0, OP.mult)
+
+    def wb_onehot(t):
+        mm([(BK(0, 0, B), M("moh"), A("cd", 0, B))])
+        o = BK(0, 0, B)
+        act(A("ohb"), o)
+        if t < RO - 1:
+            act(A("ohf"), o)
+            act(A("up"), o, bias=1024.0, scale=30.0 - EPS - 1024.0)
+            act(A("lo"), o, bias=-1.0, scale=31.0 - EPS)
+            act(A("cap"), o, bias=1024.0, scale=433.0 - EPS - 1024.0)
+            act(A("zr"), IX(A("kt", 0, W0 + B * t), A("fdu", 8, 16)), AF.Relu, scale=-1 / EPS)
+            mm([(BK(1, 0, B), M("i31"), A("ohb")), (BK(1, 0, B), M("nid"), A("zr"))])
+            act(A("gro"), BK(1, 0, B), AF.Relu)
+        else:
+            act(A("nob"), o, bias=1.0, scale=-1.0)
+            act(A("cap"), o, bias=16.0, scale=-2.0)
+
+    def wb_first(t):
+        for i in range(16):
+            k, p = divmod(i, 8)
+            ts(A("eq", B * i + 16 * p, B * i + B), BK(7, B * k + 16 * p, B * k + B), A("k32", i, i + 1), OP.is_equal)
+        it = [(BK(2, 0, 256), M("nid"), A("thr"))] + spread("b2", 0, 16, A("nc"))
+        for i in range(16):
+            k, p = divmod(i, 8)
+            it.append((BK(2, B * k + 16 * p, B * k + 16 * p + 16), M("blkw"), A("eq", B * i + 16 * p, B * i + 16 * p + 16)))
+            if p < 7:
+                it.append((BK(2, B * k + 16 * p + 16, B * k + B), M("blk2"), A("eq", B * i + 16 * p + 16, B * i + B)))
+        mm(it)
+        act(A("kr"), BK(2, 0, 256), AF.Sigmoid, scale=-2.0 ** 23)
+        o = BK(2, 256, 272)
+        mm([(o, M("id"), A("c32k", 0, 16)), (o, M("id"), A("k16", 0, 16))] + tolist(o, "seln", "kr", 0, 256))
+
+    def wb_places():
+        tt(A("fy"), BK(2, 256, 272), A("dj"), OP.min)
+        ts(A("lw"), A("fy"), float(MID), OP.add)
+
+    def wb_new(t):
+        wn = W0 + B * t
+        l8 = A("cl", 0, 8)
         if t == RO - 1:
+            act(A("hx"), IX(A("ynb", 0, wn), l8), bias=128.25, scale=0.5)
+            mm([(BK(3, 0, B), M("id"), A("hx")), (BK(3, 0, B), M("i512"), A("kr", 0, B))])
+            return
+        act(A("hx"), IX(A("kt", 0, wn), l8), bias=128.25 + 1.0 / 62, scale=1.0 / 62)
+        mm([(BK(3, 0, B), M("i31"), A("hx")), (BK(3, 0, B), M("i512"), A("kr", 0, B))])
+        act(A("dt", wn, wn + B), IX(A("dt", 0, wn), l8))
+        act(A("g1"), IX(A("lf", 0, wn), l8))
+        ts(A("k16", 16, 24), A("cf", 0, 8), 4096.0, OP.mult)
+        mm(spread("b4", 0, 8, A("k16", 16, 24)), False)
+        mm([(BK(4, B, 2 * B), M("mv"), A("g1"))])
+
+    def wb_new_counts(t):
+        wn = W0 + B * t
+        if t == RO - 1:
+            act(A("ynb", wn, wn + B), BK(3, 0, B), AF.Relu, bias=-640.0)
+        else:
+            act(A("hy"), BK(3, 0, B), AF.Relu, bias=-3969.0 - 512.0)
+            act(A("kt", wn, wn + B), A("hy"), bias=-EPS)
+
+    def wb_new_pages(t):
+        wn = W0 + B * t
+        if t < RO - 1:
+            act(A("dt", PG + wn, PG + wn + B), BK(4, 0, B), AF.Identity, bias=col(PB), scale=col(PS))
+            act(A("lf", wn, wn + B), BK(4, B, 2 * B))
+
+    def wb_counts(t):
+        wn = W0 + B * t
+        if t == RO - 1:
+            tt(A("xb"), IX(A("ynb", 0, wn), A("fdu", 0, 8)), A("nob"), OP.mult)
+            tt(IX(A("ynb"), A("lw", 0, 8)), A("xb"), A("ohb"), OP.add)
+            tt(A("xb"), IX(A("ynb", 0, wn), A("fdu", 8, 16)), A("cap"), OP.min)
+            tt(IX(A("ynb"), A("lw", 8, 16)), A("xb"), A("ohb"), OP.add)
+            return
+        tt(A("xa"), IX(A("kt", 0, wn), A("fdu", 0, 8)), A("up"), OP.min)
+        tt(IX(A("kt"), A("lw", 0, 8)), A("xa"), A("lo"), OP.max)
+        tt(A("xa"), IX(A("kt", 0, wn), A("fdu", 8, 16)), A("cap"), OP.min)
+        tt(IX(A("kt"), A("lw", 8, 16)), A("xa"), A("gro"), OP.add)
+
+    def wb_shift(t):
+        wn = W0 + B * t
+        if t == RO - 1:
+            return
+        act(A("wr"), xm, bias=(wn - MID) / 4096.0, scale=1.0 / 4096)
+        act(A("af"), IX(A("dt", 0, wn), A("fdu", 0, 8)))
+        mm([(BK(7, 256, 384), A("f32m", 0, 128), A("wr")), (BK(7, 256, 384), A("f32m", 128, 256), A("af"))])
+
+    def wb_shifted(t):
+        if t == RO - 1:
+            return
+        tt(A("dl"), BK(7, 256, 384), A("ohf"), OP.mult)
+        o = BK(7, 384, 512)
+        mm([(o, A("f32m", 0, 128), A("af")), (o, A("f32m", 256, 384), A("dl"))])
+        act(A("ax"), o)
+        act(A("ar"), o, bias=MAGIC)
+        act(A("ar"), A("ar"), bias=-MAGIC)
+
+    def wb_pointers():
+        tt(IX(A("dt", 0, WD), A("lw", 0, 8)), A("ax"), A("ar"), OP.subtract)
+
+    def counts_out(h):
+        q = A("ynb", WD // 2 * h, WD // 2 * (h + 1))
+        act(q, A("kt", WD // 2 * h, WD // 2 * (h + 1)), bias=128.0 + 1.0 / 31, scale=1.0 / 31)
+        act(q, q, bias=-128.0)
+
+    def compares(x):
+        for p in PIECES[x]:
+            compare(p)
+
+    def pointers(t, x, marks):
+        for p in PIECES[x]:
+            pointer(t, p)
+            if p == PIECES[x][-1]:
+                pointer_sum(x)
+            if marks:
+                marks0(p)
+
+    def marks(t, x):
+        if t < RO - 1:
+            for p in PIECES[x]:
+                marks1(p)
+
+    def count_out(t):
+        remote(A("nsi", 4 * t, 4 * t + 4), A("inc", 164, 168), "nar%d" % t, "nsn%d" % t)
+
+    def scatters(t, ps):
+        for p in ps:
+            scatter(t, p)
+
+    def own_context(x):
+        tt(X("cw", x), X("cf", x), X("nr", x), OP.mult)
+
+    places()
+    link_digits()
+    weave(chain((hop_constants,)), chain((write_back_constants,)), chain((escape_page,), (lanes,)))
+    targets_list(0)
+    for k in range(3):
+        weave(chain((counts_table, k)), chain((pointer_table, k)))
+    counts_table(3)
+    for t in range(RO):
+        last = t == RO - 1
+        s0, s1 = 2 * t, 2 * t + 1
+        no_f()
+        if t == 0:
+            weave(chain((counts, t, 0, "A")), chain((pointer_table, 3), (root_page,)))
+        else:
+            weave(chain((counts, t, 0, "A")), chain((link_context, t - 1, "B")))
+        weave(chain((counts, t, 0, "B")), chain((targets, s0, "A"), (compares, "A")))
+        weave(chain((page, "A"), (first_escape,)), chain((targets, s0, "B"), (compares, "B"), (page, "B")))
+        if t == 0:
+            suffix_links()
+        pointers(t, "A", True)
+        if t == 0:
+            suffix_links_back()
+            late_constants()
+        weave(chain((pointers, t, "B", True)), chain((context, "A", 1)))
+        if last:
+            counts_out(0)
+        weave(chain((counts, t, 1, "A")), chain((context, "B", 1)))
+        links(t, "A")
+        no_f()
+        act(A("ka", 0, 8), A(H[0]), bias=-1.5)
+        act(A("ka", 8, 16), A("cf", 0, 8), bias=-0.5)
+        weave(chain((counts, t, 1, "B")), chain((targets, s1, "A")))
+        if last:
+            counts_out(1)
+        weave(chain((page, "A"), (escapes, "A"), (marks, t, "A"), (links, t, "B")), chain((targets, s1, "B")))
+        weave(chain((page, "B"), (escapes, "B"), (marks, t, "B")), chain((slots, "A")))
+        weave(chain((slots, "B"), (count_out, t), (compares, "A"), (compares, "B")), chain((scatters, t, range(5))))
+        remote(landing(t), A("pw", 0, CAP), "arr%d" % t, "snt%d" % t)
+        if not last:
+            targets_list(t + 1)
+        weave(chain((first_escape,), (wb_keys, t), (wb_onehot, t), (wb_shift, t)), chain((reading_list, t)))
+        pointers(t, "A", False)
+        if not last:
+            tt(A(H[0]), A(H[0]), A("nr", 0, 8), OP.mult)
+        wb_first(t)
+        weave(chain((pointers, t, "B", False)), chain((context, "A", 1), (own_context, "A")))
+        receive(t, "A")
+        wb_new(t)
+        weave(chain((wb_shifted, t), (wb_places,)), chain((context, "B", 1), (own_context, "B")))
+        flags(t, "A")
+        wb_new_counts(t)
+        receive(t, "B")
+        wb_new_pages(t)
+        flags(t, "B")
+        if last:
+            wb_counts(t)
             for h in range(2):
-                p = slice(W // 2 * h, W // 2 * (h + 1))
-                act(T.ynb[:, p], T.kt[:, p], KT, "yn%d" % h, AF.Relu, bias=-1.0 / 32, scale=1.0 / 32)
-                dma("y", T.yn[:, p], T.ynb[:, p], "ld%d" % (8 + h), "yn%d" % h, "")
-        hop_recv(t)
-    dma("y", T.yc[:, :], T.yo[:], "ld10", "yoA yoB", "")
+                dma("y", (T.yn[:, W // 2 * h:W // 2 * (h + 1)], []), A("ynb", W // 2 * h, W // 2 * (h + 1)))
+            weave(chain((link_context, t, "A")), chain((link_context, t, "B")))
+        else:
+            weave(chain((wb_counts, t), (wb_pointers,)), chain((link_context, t, "A")))
+    dma("y", (T.yc[:, :], []), A("yo"))
     for s in sorted(cnt):
         need("g", s, cnt[s])

@@ -4,14 +4,13 @@ EPS = 2.0 ** -14
 MAGIC = 1.5 * 2.0 ** 23
 W0, B, LN, RO, SP, CAP = 3072, 128, 2560, 4, 2, 768
 W = W0 + RO * B
-WD = W + B
 PG = 4096
 MID = 1792
 BASE = 33024
 SU = 2.0 ** -14
 OWN = (RO - 1) * CAP
-CH = {"A": (0, 96), "B": (96, 160)}
-PIECES = {"A": (0, 1, 2), "B": (3, 4)}
+CH = {"A": (0, 64), "B": (64, 160)}
+PIECES = {"A": (0, 1), "B": (2, 3, 4)}
 TB = {"A": "b5", "B": "b6"}
 
 _F, _H, _I, _B, _U = "float32", "float16", "int32", "bfloat16", "uint16"
@@ -19,15 +18,15 @@ MATS = ["id", "nid", "blk", "ntri", "i14", "e15", "slt", "blks", "mdf", "moh", "
 SELS = ["selt", "vsel", "seln", "lsel", "nsel", "sel2", "sel3"]
 SCRATCH = {}
 for _n, _w, _d in (
-        ("tb", W0, _I), ("kt", WD, _F), ("dt", PG + WD, _F), ("lf", WD, _B), ("ynb", WD, _B), ("ci", 1536, _I), ("s16", 1536, _H), ("rb", 1024, _B),
-        ("dn", 384, _I), ("dg", 576, _I), ("dgb", 384, _B), ("lfd", 384, _B), ("fd", 192, _F), ("fl", 192, _U), ("lp", W0, _B), ("c1k", WD // 16, _F),
+        ("tb", W0, _I), ("kt", B + W, _F), ("dt", B + PG + W, _F), ("lf", W, _B), ("ynb", B + W, _B), ("ci", 1536, _I), ("s16", 1536, _H), ("rb", 1024, _B),
+        ("dn", 384, _I), ("dg", 576, _I), ("dgb", 384, _B), ("lfd", 384, _B), ("fd", 192, _F), ("fl", 192, _U), ("c1k", W // 16, _F),
         ("v8", 1280, _F), ("iop", 1, _I), ("pi", 2, _I), ("xf", 160, _B), ("xg", 128, _B), ("xr", 256, _B), ("pc", 32, _F), ("oh16", 16, _F), ("m31", 16, _F),
         ("mats", 128 * len(MATS), _B), ("sels", 160 * len(SELS), _B), ("f32m", 384, _F), ("expa", 2048, _B), ("c32k", 96, _B),
         ("th0", 256, _B), ("th1", 256, _B), ("th2", 16, _F), ("th3", 16, _F), ("thr", 256, _B), ("jg", 640, _F), ("dj", 16, _F),
         ("ca", 160, _I), ("cl", 160, _U), ("c2", 160, _U), ("cf", 160, _F), ("r32", 160, _H), ("qq", 160, _H), ("yy", 160, _F), ("rr", 160, _F),
-        ("es", 160, _B), ("inc", 168, _F), ("zer", 96, _F), ("sa", 160, _F), ("sx", 160, _F), ("sl", 160, _U), ("rl", 160, _U), ("nr", 160, _F),
+        ("es", 160, _B), ("inc", 168, _F), ("zer", 96, _F), ("sa", 160, _F), ("sx", 160, _F), ("sl", 160, _U), ("rl", 160, _U),
         ("cw", 160, _F), ("yo", 160, _F), ("nsi", 4 * RO, _F), ("nsf", 1, _F),
-        ("kap", LN, _H), ("ds", LN, _H), ("cd", LN, _B), ("ne", LN, _B), ("val", LN, _B), ("lg", LN, _B),
+        ("kap", LN, _H), ("ds", LN, _H), ("cd", LN, _B), ("ne", LN, _B), ("val", LN, _B), ("lg", LN, _B), ("ag", LN, _F),
         ("win", OWN + LN, _B), ("rb3", CAP + 16, _B), ("pw", W0 + LN, _B),
         ("h0", 8, _F), ("h1", 8, _F), ("ht", 8, _F), ("hz", 8, _F), ("e8", 8, _F), ("cnd", 8, _F), ("ka", 16, _F), ("k32", 16, _F), ("k16", 24, _H),
         ("nc", 16, _H), ("fdu", 16, _U), ("fy", 16, _F), ("lw", 16, _U), ("eq", 16 * B, _B), ("kr", 256, _B),
@@ -52,6 +51,8 @@ def rank_program(g, core, T, topo):
     def A(name, lo=0, hi=None, step=1, rows=None):
         if hi is None:
             hi = T[name].shape[1]
+        elif name in ("kt", "dt", "ynb"):
+            lo, hi = lo + B, hi + B
         ap = T[name][slice(None) if rows is None else rows, lo:hi:step] if step > 1 else T[name][slice(None) if rows is None else rows, lo:hi]
         return (ap, [(name, lo, hi)])
 
@@ -131,15 +132,16 @@ def rank_program(g, core, T, topo):
 
     nd = [0]
 
-    def dma(eng, out, in_):
+    def dma(eng, *pairs):
         def go():
             sem = "ld%d" % nd[0]
             nd[0] += 1
-            acc = ranges([in_], [out])
+            acc = ranges(pairs[1::2], pairs[0::2])
             order(eng, acc)
-            cnt[sem] = 16
-            E[eng].dma_start(out[0], in_[0]).then_inc(T.sem[sem], 16)
-            record(acc, "d", sem, 16)
+            cnt[sem] = 8 * len(pairs)
+            for out, in_ in zip(pairs[0::2], pairs[1::2]):
+                E[eng].dma_start(out[0], in_[0]).then_inc(T.sem[sem], 16)
+            record(acc, "d", sem, cnt[sem])
         issue(eng, go)
 
     def ap(x):
@@ -166,10 +168,10 @@ def rank_program(g, core, T, topo):
     def act(out, a, func=AF.Copy, bias=0.0, scale=1.0):
         op("s", lambda: S.activation(out[0], a[0], func, bias=ap(bias), scale=ap(scale)), [a, bias, scale], [out])
 
-    def mm(items, group=True):
+    def mm(items, group=True, start=True, stop=True):
         def f():
             for i, (o, l, r) in enumerate(items):
-                x = PE.matmul(o[0], l[0], r[0], i == 0 or not group, i == len(items) - 1 or not group)
+                x = PE.matmul(o[0], l[0], r[0], (start and i == 0) or not group, (stop and i == len(items) - 1) or not group)
             return x
         op("t", f, [x for it in items for x in it[1:]], [it[0] for it in items])
 
@@ -190,9 +192,9 @@ def rank_program(g, core, T, topo):
     def X(name, x, base=0):
         return A(name, base + CH[x][0], base + CH[x][1])
 
-    def TX(x, k):
+    def TX(x, k, m=None):
         n = CH[x][1] - CH[x][0]
-        return A(TB[x], 96 * k, 96 * k + n)
+        return A(TB[x], n * k, n * k + (m or n))
 
     def P(name, p, base=0):
         return A(name, base + 512 * p, base + 512 * p + 512)
@@ -226,8 +228,9 @@ def rank_program(g, core, T, topo):
     fill(A("xr"), [[0, 16], [1, 16]], 0)
     fill(A("c32k"), [[0, 96]], BASE)
     fill(A("zer"), [[0, 96]], 0)
-    fill(A("c1k"), [[0, WD // 16]], 1024)
-    fill(A("dt", W0, PG + WD), [[0, PG + WD - W0]], 0)
+    fill(A("c1k"), [[0, W // 16]], 1024)
+    fill(A("lf", 0, W0), [[0, W0]], 0)
+    fill(A("dt", W0, PG + W0), [[0, PG]], 0)
     fill(A("h0"), [[0, 8]], 0)
     fill(A("pw", 0, CAP), [[0, CAP]], 0)
     fill(A("rb3", CAP, CAP + 16), [[0, 16]], 0)
@@ -265,14 +268,13 @@ def rank_program(g, core, T, topo):
         cp(A("cl"), A("ca"))
         ts(A("cf"), A("ca"), float(MID), OP.subtract, 1.0 / 4096, OP.mult)
 
-    def targets_list(t):
-        for s in range(SP):
-            st = SP * t + s
-            mm([(BK(7, 160 * s, 160 * s + 160), SEL("vsel", r, slice(0, 8)), A("vr", st * LN + r, (st + 1) * LN, 16)) for r in range(16)])
-        act(A("v8", 320 * t, 320 * t + 320), BK(7, 0, 320), scale=0.125)
+    def targets_list(st):
+        if st < RO * SP:
+            mm([(BK(7, 0, 160), SEL("vsel", r, slice(0, 8)), A("vr", st * LN + r, (st + 1) * LN, 16)) for r in range(16)])
+            act(A("v8", 160 * st, 160 * st + 160), BK(7, 0, 160), scale=0.125)
 
     def counts_table(k):
-        c = A("ci", 0, 768)
+        c = A("ci", 768 * (k // 3), 768 * (k // 3) + 768)
         q = A("kt", 768 * k, 768 * k + 768)
         ts(c, A("tb", 768 * k, 768 * k + 768), 15, OP.bitwise_and)
         ts(q, c, 31.0, OP.mult, 1.0, OP.max)
@@ -284,43 +286,41 @@ def rank_program(g, core, T, topo):
         ts(c, A("tb", 768 * k, 768 * k + 768), 4, OP.arith_shift_right)
         ts(A("s16", o, o + 768), c, float(MID), OP.subtract)
         if k == 0:
-            mm([(BK(4, 0, 1), M("m150"), A("s16", 0, 1))])
-        hs = [(h, A("s16", o + 384 * h, o + 384 * h + 384), A("rb", 384 * h, 384 * h + 384)) for h in range(2)]
-        for h, s, rb in hs:
-            mm([(BK(h, 0, 384), M("mdf"), s)])
-            act(rb, BK(h, 0, 384), bias=192.0)
-        for h, s, rb in hs:
-            mm([(BK(2 + h, 0, 384), M("mdf"), s), (BK(2 + h, 0, 384), M("nid"), rb)])
-            act(A("dt", 768 * k + 384 * h, 768 * k + 384 * h + 384), BK(2 + h, 0, 384), bias=192.0)
+            mm([(BK(1, 0, 1), M("m150"), A("s16", 0, 1))])
+        for h in range(2):
+            mm([(BK(2 + h, 0, 384), M("mdf"), A("s16", o + 384 * h, o + 384 * h + 384))])
+            act(A("rb", 384 * h, 384 * h + 384), BK(2 + h, 0, 384), bias=192.0)
+
+    def pointer_rest(k):
+        for h in range(2):
+            o = 768 * (k % 2) + 384 * h
+            bk = BK(4 - 4 * h, 0, 384)
+            mm([(bk, M("mdf"), A("s16", o, o + 384)), (bk, M("nid"), A("rb", 384 * h, 384 * h + 384))])
+            act(A("dt", 768 * k + 384 * h, 768 * k + 384 * h + 384), bk, bias=192.0)
 
     def escape_page():
         ts(A("fd"), A("dn", 0, 192), float(MID), OP.subtract, 1.0 / 4096, OP.mult)
-        dma("y", A("dt", PG, PG + W0, rows=slice(0, 128, 16)), A("fd"))
-        dma("y", A("dt", PG, PG + WD, rows=slice(15, 128, 16)), A("c1k"))
+        dma("y", A("dt", PG, PG + W0, rows=slice(0, 128, 16)), A("fd"), A("dt", PG, PG + W0, rows=slice(15, 128, 16)), A("c1k", 0, W0 // 16))
 
     def root_page():
-        act(A("dt", PG, PG + 1), BK(4, 0, 1))
-        act(A("kt", W0, WD), A("dt", W0, WD), bias=-EPS)
+        act(A("dt", PG, PG + 1), BK(1, 0, 1))
 
     def link_digits():
-        op("v", lambda: V.memset(T.lf[:], 0.0), [], [A("lf")])
         ts(A("dg", 384, 576), A("dn", 192, 384), float(4096 - MID), OP.add)
         cp(A("fl"), A("dn", 0, 192))
         ts(A("dg", 0, 192), A("dg", 384, 576), 63, OP.bitwise_and)
         ts(A("dg", 192, 384), A("dg", 384, 576), 6, OP.arith_shift_right, 63, OP.bitwise_and)
         ts(A("dgb"), A("dg", 0, 384), 1.0 / 64, OP.mult)
-        for k in range(2):
-            dma("y", A("lf", 0, W0, rows=slice(2 + k, 128, 16)), A("dgb", 192 * k, 192 * k + 192))
+        dma("y", A("lf", 0, W0, rows=slice(2, 128, 16)), A("dgb", 0, 192), A("lf", 0, W0, rows=slice(3, 128, 16)), A("dgb", 192, 384))
 
-    def suffix_links():
-        act(A("lp"), IX(A("lf", 0, W0), A("fl")))
+    def suffix_links(h, call):
+        call(A("pw", LN + 1536 * h, LN + 1536 * h + 1536), IX(A("lf", 0, W0), A("fl", 96 * h, 96 * h + 96)))
 
     def suffix_links_back():
-        mm(tolist(BK(7, 0, 192), "sel2", "lp", 0, W0))
-        mm(tolist(BK(7, 192, 384), "sel3", "lp", 0, W0))
+        mm(tolist(BK(7, 0, 192), "sel2", "pw", LN, LN + W0))
+        mm(tolist(BK(7, 192, 384), "sel3", "pw", LN, LN + W0))
         act(A("lfd"), BK(7, 0, 384))
-        for k in range(2):
-            dma("y", A("lf", 0, W0, rows=slice(k, 128, 16)), A("lfd", 192 * k, 192 * k + 192))
+        dma("y", A("lf", 0, W0, rows=slice(0, 128, 16)), A("lfd", 0, 192), A("lf", 0, W0, rows=slice(1, 128, 16)), A("lfd", 192, 384))
 
     def hop_constants():
         op("v", lambda: V.memset(T.inc[:, 0:8], 0.5), [], [A("inc", 0, 8)])
@@ -334,6 +334,8 @@ def rank_program(g, core, T, topo):
         ts(A("jg", 480, 640), A("jg", 0, 160), 3 * CAP * SU, OP.add)
         ts(SEL("lsel"), SEL("selt"), col(LS), OP.mult)
         ts(SEL("nsel"), SEL("selt"), oh(0), OP.mult, -1.0 / 64, OP.mult)
+
+    def link_selectors():
         ts(SEL("sel2"), SEL("selt"), oh(2), OP.mult)
         ts(SEL("sel3"), SEL("selt"), oh(3), OP.mult)
 
@@ -357,12 +359,12 @@ def rank_program(g, core, T, topo):
         ts(M("blk2"), M("blk"), 2.0, OP.mult)
         ts(M("i31"), M("id"), 31.0, OP.mult)
         ts(M("i512"), M("id"), 512.0, OP.mult)
-        ts(SEL("seln"), SEL("selt"), -BASE / 16.0, OP.mult)
+        ts(SEL("seln"), SEL("selt"), BASE / 16.0, OP.mult)
         cp(A("f32m", 0, 128), M("id"))
 
     def late_constants():
         for h in range(2):
-            act(A("dj", 8 * h, 8 * h + 8), A("jg", 0, 8), bias=float(W - MID - CAP), scale=1 / SU)
+            act(A("dj", 8 * h, 8 * h + 8), A("jg", 0, 8), bias=float(-B - MID - CAP), scale=1 / SU)
         for t in (1, 2):
             act(A("jg", 160 * t, 160 * t + 160), A("jg", 0, 160), bias=t * CAP * SU)
 
@@ -437,8 +439,8 @@ def rank_program(g, core, T, topo):
         lo, hi = CH[x]
         scan(X("inc", x, 8), TX(x, 3), A("zer", 0, hi - lo), A("inc", 7 + lo, 8 + lo), OP.add, OP.add)
         tt(X("sa", x), TX(x, 2), X("inc", x, 7), OP.add)
-        tt(X("sx", x), X("sa", x), X("jg", x, 160 * (RO - 1)), OP.min)
-        ts(X("sl", x), X("sx", x), 1 / SU, OP.mult)
+        tt(TX(x, 3), X("sa", x), X("jg", x, 160 * (RO - 1)), OP.min)
+        ts(X("sl", x), TX(x, 3), 1 / SU, OP.mult)
 
     dst = T.cores[(rank + 1) % len(T.cores)]
     src = T.cores[(rank - 1) % len(T.cores)]
@@ -468,28 +470,28 @@ def rank_program(g, core, T, topo):
         else:
             cp(o, P("lg", p))
 
-    def reading_list(t):
-        ts(A("nsf"), A("nsi", 4 * t + 3, 4 * t + 4), 0.5, OP.subtract, CAP * SU, OP.min)
-        ts(A("nr"), A("sa"), A("nsf"), OP.is_ge)
-        tt(A("sx"), A("nr"), A("sa"), OP.add)
+    def reading_list(t, x):
+        if x == "A":
+            ts(A("nsf"), A("nsi", 4 * t + 3, 4 * t + 4), 0.5, OP.subtract, CAP * SU, OP.min)
+        ts(TX(x, 0), X("sa", x), A("nsf"), OP.is_ge)
+        tt(TX(x, 2), TX(x, 0), X("sa", x), OP.add)
         if t < RO - 1:
-            tt(A("sx"), A("sx"), A("jg", 160 * t, 160 * t + 160), OP.min)
-            ts(A("rl"), A("sx"), 1 / SU, OP.mult)
+            tt(X("sx", x), TX(x, 2), X("jg", x, 160 * t), OP.min)
+            ts(X("rl", x), X("sx", x), 1 / SU, OP.mult)
         else:
-            ts(A("rl"), A("sx"), CAP * SU, OP.min, 1 / SU, OP.mult)
+            ts(X("rl", x), TX(x, 2), CAP * SU, OP.min, 1 / SU, OP.mult)
 
-    def receive(t, x):
-        last = t == RO - 1
-        win = A("rb3") if last else A("win", OWN - CAP * (t + 1), OWN + LN)
-        for p in PIECES[x]:
-            act(P("val", p), IX(win, L("rl", p)))
+    def receive(t, p, call):
+        win = A("rb3") if t == RO - 1 else A("win", OWN - CAP * (t + 1), OWN + LN)
+        call(P("val", p), IX(win, L("rl", p)))
 
     def flags(t, x):
         last = t == RO - 1
         lo, hi = 16 * CH[x][0], 16 * CH[x][1]
+        mm(tolist(TX(x, 4), "lsel", "val", lo, hi), stop=last)
         if not last:
-            act(A("ne", lo, hi), A("val", lo, hi), AF.Sigmoid, bias=-127.0 * 256, scale=2.0 ** 15)
-        mm(tolist(TX(x, 4), "lsel", "val", lo, hi) + ([] if last else tolist(TX(x, 4), "nsel", "ne", lo, hi)))
+            ts(A("ne", lo, hi), A("val", lo, hi), 1.0, OP.is_ge)
+            mm(tolist(TX(x, 4), "nsel", "ne", lo, hi), start=False)
 
     def link_context(t, x):
         s = TX(x, 4)
@@ -513,81 +515,91 @@ def rank_program(g, core, T, topo):
         ts(A("nc"), A("k16", 0, 16), 2048.0, OP.is_equal, 4.0, OP.mult)
 
     def wb_onehot(t):
-        mm([(BK(0, 0, B), M("moh"), A("cd", 0, B))])
-        o = BK(0, 0, B)
+        o = BK(1, 0, B)
+        mm([(o, M("moh"), A("cd", 0, B))])
         act(A("ohb"), o)
         if t < RO - 1:
             act(A("ohf"), o)
             act(A("up"), o, bias=1024.0, scale=30.0 - EPS - 1024.0)
             act(A("lo"), o, bias=-1.0, scale=31.0 - EPS)
             act(A("cap"), o, bias=1024.0, scale=433.0 - EPS - 1024.0)
-            act(A("zr"), IX(A("kt", 0, W0 + B * t), A("fdu", 8, 16)), AF.Relu, scale=-1 / EPS)
-            mm([(BK(1, 0, B), M("i31"), A("ohb")), (BK(1, 0, B), M("nid"), A("zr"))])
-            act(A("gro"), BK(1, 0, B), AF.Relu)
         else:
             act(A("nob"), o, bias=1.0, scale=-1.0)
             act(A("cap"), o, bias=16.0, scale=-2.0)
 
-    def wb_first(t):
+    def wb_grow(t):
+        if t < RO - 1:
+            o = BK(1, 0, B)
+            mm([(o, M("i31"), A("ohb")), (o, M("nid"), A("zr"))])
+            act(A("gro"), o, AF.Relu)
+
+    def wb_equal():
+        mm([(BK(0, 0, 256), M("nid"), A("thr"))] + spread("b0", 0, 16, A("nc")), stop=False)
         for i in range(16):
             k, p = divmod(i, 8)
             ts(A("eq", B * i + 16 * p, B * i + B), BK(7, B * k + 16 * p, B * k + B), A("k32", i, i + 1), OP.is_equal)
-        it = [(BK(2, 0, 256), M("nid"), A("thr"))] + spread("b2", 0, 16, A("nc"))
-        for i in range(16):
-            k, p = divmod(i, 8)
-            it.append((BK(2, B * k + 16 * p, B * k + 16 * p + 16), M("blkw"), A("eq", B * i + 16 * p, B * i + 16 * p + 16)))
-            if p < 7:
-                it.append((BK(2, B * k + 16 * p + 16, B * k + B), M("blk2"), A("eq", B * i + 16 * p + 16, B * i + B)))
-        mm(it)
-        act(A("kr"), BK(2, 0, 256), AF.Sigmoid, scale=-2.0 ** 23)
-        o = BK(2, 256, 272)
-        mm([(o, M("id"), A("c32k", 0, 16)), (o, M("id"), A("k16", 0, 16))] + tolist(o, "seln", "kr", 0, 256))
+            if p == 7:
+                it = []
+                for p in range(8):
+                    e = B * (8 * k + p) + 16 * p
+                    it.append((BK(0, B * k + 16 * p, B * k + 16 * p + 16), M("blkw"), A("eq", e, e + 16)))
+                    if p < 7:
+                        it.append((BK(0, B * k + 16 * p + 16, B * k + B), M("blk2"), A("eq", e + 16, e + B - 16 * p)))
+                mm(it, start=False, stop=k == 1)
+
+    def wb_first(t):
+        act(A("kr"), BK(0, 0, 256), AF.Sigmoid, scale=-2.0 ** 23)
+        o = BK(0, 256, 272)
+        mm([(o, M("nid"), A("c32k", 0, 16)), (o, M("id"), A("k16", 0, 16))] + tolist(o, "seln", "kr", 0, 256))
 
     def wb_places():
-        tt(A("fy"), BK(2, 256, 272), A("dj"), OP.min)
-        ts(A("lw"), A("fy"), float(MID), OP.add)
+        tt(A("fy"), BK(0, 256, 272), A("dj"), OP.max)
+        ts(A("lw"), A("fy"), float(MID + B), OP.add)
 
     def wb_new(t):
         wn = W0 + B * t
         l8 = A("cl", 0, 8)
         if t == RO - 1:
             act(A("hx"), IX(A("ynb", 0, wn), l8), bias=128.25, scale=0.5)
-            mm([(BK(3, 0, B), M("id"), A("hx")), (BK(3, 0, B), M("i512"), A("kr", 0, B))])
             return
         act(A("hx"), IX(A("kt", 0, wn), l8), bias=128.25 + 1.0 / 62, scale=1.0 / 62)
-        mm([(BK(3, 0, B), M("i31"), A("hx")), (BK(3, 0, B), M("i512"), A("kr", 0, B))])
         act(A("dt", wn, wn + B), IX(A("dt", 0, wn), l8))
-        act(A("g1"), IX(A("lf", 0, wn), l8))
         ts(A("k16", 16, 24), A("cf", 0, 8), 4096.0, OP.mult)
-        mm(spread("b4", 0, 8, A("k16", 16, 24)), False)
-        mm([(BK(4, B, 2 * B), M("mv"), A("g1"))])
+
+    def wb_new_rows(t):
+        if t < RO - 1:
+            act(A("g1"), IX(A("lf", 0, W0 + B * t), A("cl", 0, 8)))
+            mm(spread("b1", 0, 8, A("k16", 16, 24)), False)
+            mm([(BK(1, B, 2 * B), M("mv"), A("g1"))])
 
     def wb_new_counts(t):
         wn = W0 + B * t
+        o = BK(1, 2 * B, 3 * B)
+        mm([(o, M("id" if t == RO - 1 else "i31"), A("hx")), (o, M("i512"), A("kr", 0, B))])
         if t == RO - 1:
-            act(A("ynb", wn, wn + B), BK(3, 0, B), AF.Relu, bias=-640.0)
+            act(A("ynb", wn, wn + B), o, AF.Relu, bias=-640.0)
         else:
-            act(A("hy"), BK(3, 0, B), AF.Relu, bias=-3969.0 - 512.0)
+            act(A("hy"), o, AF.Relu, bias=-3969.0 - 512.0)
             act(A("kt", wn, wn + B), A("hy"), bias=-EPS)
 
     def wb_new_pages(t):
         wn = W0 + B * t
         if t < RO - 1:
-            act(A("dt", PG + wn, PG + wn + B), BK(4, 0, B), AF.Identity, bias=col(PB), scale=col(PS))
-            act(A("lf", wn, wn + B), BK(4, B, 2 * B))
+            act(A("dt", PG + wn, PG + wn + B), BK(1, 0, B), AF.Identity, bias=col(PB), scale=col(PS))
+            act(A("lf", wn, wn + B), BK(1, B, 2 * B))
 
     def wb_counts(t):
         wn = W0 + B * t
         if t == RO - 1:
             tt(A("xb"), IX(A("ynb", 0, wn), A("fdu", 0, 8)), A("nob"), OP.mult)
-            tt(IX(A("ynb"), A("lw", 0, 8)), A("xb"), A("ohb"), OP.add)
+            tt(IX(A("ynb", -B, wn), A("lw", 0, 8)), A("xb"), A("ohb"), OP.add)
             tt(A("xb"), IX(A("ynb", 0, wn), A("fdu", 8, 16)), A("cap"), OP.min)
-            tt(IX(A("ynb"), A("lw", 8, 16)), A("xb"), A("ohb"), OP.add)
+            tt(IX(A("ynb", -B, wn), A("lw", 8, 16)), A("xb"), A("ohb"), OP.add)
             return
         tt(A("xa"), IX(A("kt", 0, wn), A("fdu", 0, 8)), A("up"), OP.min)
-        tt(IX(A("kt"), A("lw", 0, 8)), A("xa"), A("lo"), OP.max)
+        tt(IX(A("kt", -B, wn), A("lw", 0, 8)), A("xa"), A("lo"), OP.max)
         tt(A("xa"), IX(A("kt", 0, wn), A("fdu", 8, 16)), A("cap"), OP.min)
-        tt(IX(A("kt"), A("lw", 8, 16)), A("xa"), A("gro"), OP.add)
+        tt(IX(A("kt", -B, wn), A("lw", 8, 16)), A("xa"), A("gro"), OP.add)
 
     def wb_shift(t):
         wn = W0 + B * t
@@ -595,32 +607,39 @@ def rank_program(g, core, T, topo):
             return
         act(A("wr"), xm, bias=(wn - MID) / 4096.0, scale=1.0 / 4096)
         act(A("af"), IX(A("dt", 0, wn), A("fdu", 0, 8)))
-        mm([(BK(7, 256, 384), A("f32m", 0, 128), A("wr")), (BK(7, 256, 384), A("f32m", 128, 256), A("af"))])
+        act(A("zr"), IX(A("kt", 0, wn), A("fdu", 8, 16)), AF.Relu, scale=-1 / EPS)
+        mm([(BK(1, 384, 512), A("f32m", 0, 128), A("wr")), (BK(1, 384, 512), A("f32m", 128, 256), A("af"))])
 
     def wb_shifted(t):
         if t == RO - 1:
             return
-        tt(A("dl"), BK(7, 256, 384), A("ohf"), OP.mult)
+        tt(A("dl"), BK(1, 384, 512), A("ohf"), OP.mult)
         o = BK(7, 384, 512)
         mm([(o, A("f32m", 0, 128), A("af")), (o, A("f32m", 256, 384), A("dl"))])
+
+    def wb_reduce(t):
+        if t == RO - 1:
+            return
+        o = BK(7, 384, 512)
         act(A("ax"), o)
         act(A("ar"), o, bias=MAGIC)
         act(A("ar"), A("ar"), bias=-MAGIC)
 
-    def wb_pointers():
-        tt(IX(A("dt", 0, WD), A("lw", 0, 8)), A("ax"), A("ar"), OP.subtract)
+    def wb_pointers(t):
+        tt(IX(A("dt", -B, W0 + B * t), A("lw", 0, 8)), A("ax"), A("ar"), OP.subtract)
 
     def counts_out(h):
-        q = A("ynb", WD // 2 * h, WD // 2 * (h + 1))
-        act(q, A("kt", WD // 2 * h, WD // 2 * (h + 1)), bias=128.0 + 1.0 / 31, scale=1.0 / 31)
+        n = (W - B) // 2
+        q = A("ynb", n * h, n * (h + 1))
+        act(q, A("kt", n * h, n * (h + 1)), bias=128.0 + 1.0 / 31, scale=1.0 / 31)
         act(q, q, bias=-128.0)
 
     def compares(x):
         for p in PIECES[x]:
             compare(p)
 
-    def pointers(t, x, marks):
-        for p in PIECES[x]:
+    def pointers(t, x, marks, first=0):
+        for p in PIECES[x][first:]:
             pointer(t, p)
             if p == PIECES[x][-1]:
                 pointer_sum(x)
@@ -635,74 +654,127 @@ def rank_program(g, core, T, topo):
     def count_out(t):
         remote(A("nsi", 4 * t, 4 * t + 4), A("inc", 164, 168), "nar%d" % t, "nsn%d" % t)
 
+    def payload_out(t):
+        remote(landing(t), A("pw", 0, CAP), "arr%d" % t, "snt%d" % t)
+
+    def twos(c):
+        return [sum(c[k:k + 2], []) for k in range(0, len(c), 2)]
+
     def scatters(t, ps):
         for p in ps:
             scatter(t, p)
 
     def own_context(x):
-        tt(X("cw", x), X("cf", x), X("nr", x), OP.mult)
+        tt(X("cw", x), TX(x, 0), X("cf", x), OP.mult)
+
+    def compares_late(t):
+        for p in PIECES["B"]:
+            mm([(BK(p), M("ntri"), P("kap", p))] + spread("b%d" % p, 0, 32, L("qq", p)))
+            act(BK(p), BK(p), AF.Sigmoid, bias=-16.0 * (BASE // 32 * 31 - 8), scale=16.0)
+
+    def gathers_late(t, x):
+        act(A("ag", 16 * CH[x][0], 16 * CH[x][1]), IX(A("dt", 0, PG + W0 + B * t), X("c2", x)))
+
+    def products_late(x):
+        for p in PIECES[x]:
+            tt(P("ds", p), BK(p), P("ag", p), OP.mult)
+        pointer_sum(x)
+
+    def drop_f():
+        tt(A(H[0]), A(H[0]), TX("A", 0, 8), OP.mult)
+        no_f()
 
     places()
-    link_digits()
-    weave(chain((hop_constants,)), chain((write_back_constants,)), chain((escape_page,), (lanes,)))
+    weave(chain((link_digits,), (escape_page,)), chain((lanes,), (link_selectors,)))
     targets_list(0)
-    for k in range(3):
-        weave(chain((counts_table, k)), chain((pointer_table, k)))
-    counts_table(3)
+    for k in range(2):
+        weave(chain((counts_table, k)), chain((pointer_table, k), (pointer_rest, k)))
+    weave(chain((counts_table, 2)), chain((counts_table, 3)))
+    pointer_table(2)
+    suffix_links(0, cp)
+    spare = chain((hop_constants,), (write_back_constants,))
+
+    def some(n):
+        out = [sum(spare[:n], [])]
+        del spare[:n]
+        return out
     for t in range(RO):
         last = t == RO - 1
         s0, s1 = 2 * t, 2 * t + 1
-        no_f()
         if t == 0:
-            weave(chain((counts, t, 0, "A")), chain((pointer_table, 3), (root_page,)))
+            no_f()
+            pointer_rest(2)
+            counts(t, 0, "A")
+            pointer_table(3)
+            pointer_rest(3)
+            root_page()
+            suffix_links(1, act)
+            weave(chain((counts, t, 0, "B")), chain((targets, s0, "A"), (compares, "A")))
         else:
-            weave(chain((counts, t, 0, "A")), chain((link_context, t - 1, "B")))
-        weave(chain((counts, t, 0, "B")), chain((targets, s0, "A"), (compares, "A")))
-        weave(chain((page, "A"), (first_escape,)), chain((targets, s0, "B"), (compares, "B"), (page, "B")))
-        if t == 0:
-            suffix_links()
-        pointers(t, "A", True)
+            weave(chain((counts, t, 0, "A"), (targets_list, s1)), chain((flags, t - 1, "B")))
+            link_context(t - 1, "B")
+            if last:
+                counts_out(0)
+            weave(chain((counts, t, 0, "B")), chain((targets, s0, "A"), (compares, "A")))
+            wb_pointers(t - 1)
+        weave(chain((page, "A"), (first_escape,)), some(6) + chain((targets, s0, "B"), (compares, "B"), (page, "B")))
         if t == 0:
             suffix_links_back()
-            late_constants()
-        weave(chain((pointers, t, "B", True)), chain((context, "A", 1)))
-        if last:
-            counts_out(0)
-        weave(chain((counts, t, 1, "A")), chain((context, "B", 1)))
-        links(t, "A")
+        weave(some(8))
+        pointers(t, "A", True)
+        weave(chain((pointers, t, "B", True)), [[]] + chain((context, "A", 1)))
+        if t == 0:
+            targets_list(s1)
+        weave(some(6))
+        weave(chain((counts, t, 1, "A")), twos(chain((context, "B", 1))))
         no_f()
         act(A("ka", 0, 8), A(H[0]), bias=-1.5)
         act(A("ka", 8, 16), A("cf", 0, 8), bias=-0.5)
+        links(t, "A")
+        targets_list(s1 + 1)
+        links(t, "B")
         weave(chain((counts, t, 1, "B")), chain((targets, s1, "A")))
+        weave(chain((page, "A"), (escapes, "A"), (marks, t, "A")), some(6) + chain((targets, s1, "B")))
+        weave(chain((page, "B"), (escapes, "B"), (marks, t, "B")), chain((slots, "A")))
+        weave(some(len(spare)))
+        if t == 0:
+            late_constants()
         if last:
             counts_out(1)
-        weave(chain((page, "A"), (escapes, "A"), (marks, t, "A"), (links, t, "B")), chain((targets, s1, "B")))
-        weave(chain((page, "B"), (escapes, "B"), (marks, t, "B")), chain((slots, "A")))
-        weave(chain((slots, "B"), (count_out, t), (compares, "A"), (compares, "B")), chain((scatters, t, range(5))))
-        remote(landing(t), A("pw", 0, CAP), "arr%d" % t, "snt%d" % t)
-        if not last:
-            targets_list(t + 1)
-        weave(chain((first_escape,), (wb_keys, t), (wb_onehot, t), (wb_shift, t)), chain((reading_list, t)))
-        pointers(t, "A", False)
-        if not last:
-            tt(A(H[0]), A(H[0]), A("nr", 0, 8), OP.mult)
-        wb_first(t)
-        weave(chain((pointers, t, "B", False)), chain((context, "A", 1), (own_context, "A")))
-        receive(t, "A")
-        wb_new(t)
-        weave(chain((wb_shifted, t), (wb_places,)), chain((context, "B", 1), (own_context, "B")))
-        flags(t, "A")
-        wb_new_counts(t)
-        receive(t, "B")
-        wb_new_pages(t)
-        flags(t, "B")
+        sb = chain((slots, "B"), (count_out, t), (compares, "A"), (compares_late, t), (wb_onehot, t), (gathers_late, t, "B"))
+        ks = chain((first_escape,), (wb_keys, t))
+        weave(sb[:1], ks[:1])
+        weave(sb[1:], ks[1:6], chain((scatters, t, range(5)), (payload_out, t)))
+        weave(ks[6:], chain((pointers, t, "A", False)))
+        wb_shift(t)
+        wb_equal()
+        wb_shifted(t)
+        weave(chain((context, "A", 1), (wb_new, t), (wb_first, t), (wb_grow, t), (wb_new_rows, t)), chain((reading_list, t, "A")), [[]] + chain((reading_list, t, "B")))
         if last:
-            wb_counts(t)
+            wb_new_counts(t)
+            products_late("B")
+            wb_places()
+            weave(chain((wb_counts, t)), chain((own_context, "A"), (context, "B", 1), (own_context, "B")))
             for h in range(2):
                 dma("y", (T.yn[:, W // 2 * h:W // 2 * (h + 1)], []), A("ynb", W // 2 * h, W // 2 * (h + 1)))
-            weave(chain((link_context, t, "A")), chain((link_context, t, "B")))
+            for p in range(5):
+                receive(t, p, cp if p > 2 else act)
+                if p % 3 == 1:
+                    flags(t, "AB"[p // 3])
+            link_context(t, "A")
+            link_context(t, "B")
         else:
-            weave(chain((wb_counts, t), (wb_pointers,)), chain((link_context, t, "A")))
+            for p in range(4):
+                receive(t, p, act)
+                if p == 1:
+                    wb_new_counts(t)
+            weave(chain((products_late, "B")), chain((own_context, "A"), (drop_f,), (wb_places,)))
+            wb_reduce(t)
+            wb_new_pages(t)
+            weave(chain((wb_counts, t)), [[], []] + chain((context, "B", 1)))
+            flags(t, "A")
+            receive(t, 4, cp)
+            weave(chain((link_context, t, "A")), chain((own_context, "B")))
     dma("y", (T.yc[:, :], []), A("yo"))
     for s in sorted(cnt):
         need("g", s, cnt[s])

@@ -1,43 +1,98 @@
+import math
 from concourse.mybir import AluOpType as OP, ActivationFunctionType as AF
 
 EPS = 2.0 ** -14
 MAGIC = 1.5 * 2.0 ** 23
+BIG = 1.5 * 2.0 ** 27
 W0, B, LN, RO, SP, CAP = 3072, 128, 2560, 4, 2, 768
 W = W0 + RO * B
 PG = 4096
 MID = 1792
 BASE = 33024
 SU = 2.0 ** -14
+LOW = 512
 OWN = (RO - 1) * CAP
-CH = {"A": (0, 64), "B": (64, 160)}
-PIECES = {"A": (0, 1), "B": (2, 3, 4)}
+CH = {"A": (0, 96), "B": (96, 160)}
+PIECES = {"A": (0, 1, 2), "B": (3, 4)}
 TB = {"A": "b5", "B": "b6"}
+CYCLE, PE_CYCLE, GATHER, SCATTER, WAKE, LOCAL, REMOTE = 0.83, 0.42, 1.3, 2.5, 250.0, (2000.0, 250.0), (3500.0, 50.0)
+CFG = dict(late=(1, 2, 3, 4), late0=(), shared=(2, 4), shared1=(2,), flagv="AB", recvv=(2, 4), lpv=(), turns=3, pefix=0.0, vfix=0.0, afix=100.0, cuts=(512, 1024, 1536, 2560), early=True, merge=False, mini=False, modv=(1, 3, 5, 7), rrow=300.0, riss=600.0, mid=0, soft=False, hyv=True, arv=False, ynv=(0, 2, 4), tries=40, amp=400.0)
+ORDER = {}
 
 _F, _H, _I, _B, _U = "float32", "float16", "int32", "bfloat16", "uint16"
-MATS = ["id", "nid", "blk", "ntri", "i14", "e15", "slt", "blks", "mdf", "moh", "blkw", "blk2", "i31", "i512", "mv", "m150", "u1", "l1", "low"]
+MATS = ["id", "nid", "blk", "ntri", "i14", "e15", "slt", "blks", "moh", "blkw", "blk2", "i31", "i512", "mv", "u1", "l1", "l2", "low", "slq"]
 SELS = ["selt", "vsel", "seln", "lsel", "nsel", "sel2", "sel3"]
 SCRATCH = {}
 for _n, _w, _d in (
-        ("tb", W0, _I), ("kt", B + W, _F), ("dt", B + PG + W, _F), ("lf", W, _B), ("ynb", B + W, _B), ("ci", 1536, _I), ("s16", 1536, _H), ("rb", 1024, _B),
-        ("dn", 384, _I), ("dg", 576, _I), ("dgb", 384, _B), ("lfd", 384, _B), ("fd", 192, _F), ("fl", 192, _U), ("c1k", W // 16, _F),
+        ("tb", W0, _I), ("kt", B + W, _F), ("dt", B + PG + W, _F), ("lf", W, _B), ("ynb", B + W, _B), ("ci", 1536, _I), ("rb", 768, _B),
+        ("dn", 384, _I), ("dg", 576, _I), ("dgb", 384, _B), ("lfd", 384, _B), ("fd", 192, _F), ("fl", 192, _U), ("c1k", W0 // 16, _F),
         ("v8", 1280, _F), ("iop", 1, _I), ("pi", 2, _I), ("xf", 160, _B), ("xg", 128, _B), ("xr", 256, _B), ("pc", 32, _F), ("oh16", 16, _F), ("m31", 16, _F),
-        ("mats", 128 * len(MATS), _B), ("sels", 160 * len(SELS), _B), ("f32m", 384, _F), ("expa", 2048, _B), ("c32k", 96, _B),
+        ("mats", 128 * len(MATS), _B), ("sels", 160 * len(SELS), _B), ("f32m", 640, _F), ("expa", 2048, _B), ("c32k", 96, _B),
         ("th0", 256, _B), ("th1", 256, _B), ("th2", 16, _F), ("th3", 16, _F), ("thr", 256, _B), ("jg", 640, _F), ("dj", 16, _F),
         ("ca", 160, _I), ("cl", 160, _U), ("c2", 160, _U), ("cf", 160, _F), ("r32", 160, _H), ("qq", 160, _H), ("yy", 160, _F), ("rr", 160, _F),
-        ("es", 160, _B), ("inc", 168, _F), ("zer", 96, _F), ("sa", 160, _F), ("sx", 160, _F), ("sl", 160, _U), ("rl", 160, _U),
+        ("es", 160, _B), ("inc", 168, _F), ("zer", 96, _F), ("sa", 160, _F), ("sl", 160, _U), ("rl", 160, _U),
         ("cw", 160, _F), ("yo", 160, _F), ("nsi", 4 * RO, _F), ("nsf", 1, _F),
         ("kap", LN, _H), ("ds", LN, _H), ("cd", LN, _B), ("ne", LN, _B), ("val", LN, _B), ("lg", LN, _B), ("ag", LN, _F),
-        ("win", OWN + LN, _B), ("rb3", CAP + 16, _B), ("pw", W0 + LN, _B),
-        ("h0", 8, _F), ("h1", 8, _F), ("ht", 8, _F), ("hz", 8, _F), ("e8", 8, _F), ("cnd", 8, _F), ("ka", 16, _F), ("k32", 16, _F), ("k16", 24, _H),
+        ("win", OWN + LN, _B), ("rb3", CAP + 16, _B), ("pw", LOW + W0 + LN, _B), ("jq", LOW // 16, _F),
+        ("h0", 8, _F), ("h1", 8, _F), ("ht", 8, _F), ("hz", 8, _F), ("c8", 8, _U), ("d8", B, _H), ("e8", 8, _F), ("cnd", 8, _F), ("ka", 16, _F), ("k32", 16, _F), ("k16", 24, _H),
         ("nc", 16, _H), ("fdu", 16, _U), ("fy", 16, _F), ("lw", 16, _U), ("eq", 16 * B, _B), ("kr", 256, _B),
-        ("ohb", B, _B), ("ohf", B, _F), ("up", B, _F), ("lo", B, _F), ("cap", B, _F), ("gro", B, _F), ("zr", B, _B), ("hx", B, _B), ("hy", B, _F),
-        ("xa", B, _F), ("xb", B, _B), ("nob", B, _B), ("g1", B, _B), ("af", B, _F), ("wr", B, _F), ("dl", B, _F), ("ax", B, _F), ("ar", B, _F)):
+        ("ohb", B, _B), ("up", B, _F), ("lo", B, _F), ("cap", B, _F), ("gro", B, _F), ("zr", B, _B), ("hx", B, _B), ("hy", B, _F),
+        ("xa", B, _F), ("xb", B, _B), ("nob", B, _B), ("g1", B, _B), ("af", B, _F), ("wr", 3 * B, _F), ("dl", B, _F), ("ax", B, _F), ("ar", B, _F)):
     SCRATCH[_n] = ("sbuf", [128, _w], _d)
 SCRATCH["vr"] = ("sbuf", [8, RO * SP * LN], _B)
 for _k in range(8):
     SCRATCH["b%d" % _k] = ("psum", [128, 512], _F)
 SEMAPHORES = (["cv", "ct", "cs", "cg"] + ["ld%d" % k for k in range(20)]
-              + [n + str(k) for k in range(RO) for n in ("arr", "snt", "nar", "nsn")])
+              + [n + str(k) for k in range(RO) for n in ("arr", "snt", "nar", "nsn", "har", "hsn", "mar", "msn")])
+
+
+def in_order(calls):
+    n = len(calls)
+    before = [[(p, calls[p][2] - calls[p][1] + (0.0 if p in c[5] else WAKE)) for p in c[3]] for c in calls]
+    after = [[] for _ in range(n)]
+    for i in range(n):
+        for p, gap in before[i]:
+            after[p].append((i, gap))
+
+    def lay(order, needs):
+        end, held = [0.0] * n, {}
+        for i in order:
+            q, busy, banks = calls[i][0], calls[i][1], calls[i][4]
+            t = max([end[p] + gap for p, gap in needs[i]], default=0.0)
+            moved = True
+            while moved:
+                moved = False
+                for r in [q] + banks:
+                    pad = 0.0 if r == q else WAKE
+                    h = held.setdefault(r, [])
+                    k = len(h)
+                    while k and h[k - 1][0] > t - 9000.0:
+                        k -= 1
+                    for a, b, who in h[k:]:
+                        if a - pad >= t + busy and a - pad > t:
+                            break
+                        if b + pad > t and (r == q or who != q):
+                            t, moved = b + pad, True
+            end[i] = t + busy
+            for r in [q] + banks:
+                held[r].append((t, t + busy, q))
+                held[r].sort()
+        return end
+
+    def there_and_back(way):
+        end = lay(sorted(range(n), key=lambda i: (-way[i], i)), before)
+        way = lay(sorted(range(n), key=lambda i: (-end[i], -i)), after)
+        end = lay(sorted(range(n), key=lambda i: (-way[i], i)), before)
+        return max(end[i] + calls[i][2] - calls[i][1] for i in range(n)), end, way
+    best = there_and_back([-i for i in range(n)])
+    for k in range(CFG["tries"]):
+        way = [0.0] * n
+        for i in range(n - 1, -1, -1):
+            way[i] = max([best[2][i] + CFG["amp"] * math.sin((i + 1) * (k + 1) * 12.9898)] + [way[j] + 1.0 for j, gap in after[i]])
+        best = min(best, there_and_back(way), key=lambda b: b[0])
+    CFG["span"] = best[0]
+    loads = [i for i in range(n) if calls[i][0] in "ys" and not calls[i][3]]
+    return loads + sorted(set(range(n)) - set(loads), key=lambda i: (best[1][i] - calls[i][1], i))
 
 
 def rank_program(g, core, T, topo):
@@ -46,7 +101,7 @@ def rank_program(g, core, T, topo):
         return
     E = {"v": g.vector, "t": g.tensor, "s": g.scalar, "g": g, "y": g.sync}
     V, S, PE = g.vector, g.scalar, g.tensor
-    cnt, waited, seen = {}, {}, {}
+    calls, makes, writes, reads, lastpe = [], [], {}, {}, {}
 
     def A(name, lo=0, hi=None, step=1, rows=None):
         if hi is None:
@@ -54,126 +109,114 @@ def rank_program(g, core, T, topo):
         elif name in ("kt", "dt", "ynb"):
             lo, hi = lo + B, hi + B
         ap = T[name][slice(None) if rows is None else rows, lo:hi:step] if step > 1 else T[name][slice(None) if rows is None else rows, lo:hi]
-        return (ap, [(name, lo, hi)])
+        return (ap, (name, lo, hi), None, (hi - lo + step - 1) // step)
 
     def IX(win, off):
-        return (win[0].indirect(off[0]), win[1], off[1])
+        return (win[0].indirect(off[0]), win[1], off[1], 16 * off[3])
 
-    def need(eng, sem, val):
-        if waited.get((eng, sem), 0) < val:
-            E[eng].wait_ge(T.sem[sem], val)
-            waited[(eng, sem)] = val
+    def HBM(ap):
+        return (ap, None, None, 0)
 
-    def ranges(ins, outs):
-        rd, wr = [], []
-        for x in ins:
-            if isinstance(x, tuple):
-                rd += x[1] + (x[2] if len(x) > 2 else [])
-        for x in outs:
-            wr += x[1]
-            rd += x[2] if len(x) > 2 else []
-        return [r + (False,) for r in rd] + [r + (True,) for r in wr]
+    def psum(x):
+        return SCRATCH[x[1][0]][0] == "psum"
 
-    def psum(name):
-        return len(name) == 2 and name[0] == "b"
+    def size(x):
+        return 2 if SCRATCH[x[1][0]][2] in (_H, _B, _U) else 4
 
-    def order(eng, acc):
-        todo = {}
-        for name, lo, hi, w in acc:
-            for l, h, pw, pe, sem, val in seen.get(name, []):
-                if pe == eng == "t":
-                    continue
-                if (psum(name) and pe != eng) or (l < hi and lo < h and (w or pw)):
-                    todo[sem] = max(todo.get(sem, 0), val)
-        for s in todo:
-            need(eng, s, todo[s])
+    def call(q, busy, took, make, ins, outs, also=()):
+        ins = [x for x in ins if isinstance(x, tuple) and x[1]]
+        outs = [x for x in outs if x[1]]
+        rd = {x[1] for x in ins} | {x[2] for x in ins + outs if x[2]}
+        wr = {x[1] for x in outs}
+        me, pre = len(calls), set(also)
+        for name, lo, hi in rd:
+            pre |= {i for l, h, i in writes.get(name, []) if l < hi and lo < h}
+        raw = set(pre)
+        for name, lo, hi in wr:
+            pre |= {i for l, h, i in writes.get(name, []) if l < hi and lo < h}
+        for name, lo, hi in wr:
+            pre |= {i for l, h, i in reads.get(name, []) if l < hi and lo < h}
+        for name, lo, hi in wr:
+            for d in (writes, reads):
+                d[name] = [e for e in d.get(name, []) if not (lo <= e[0] and e[1] <= hi)]
+            writes[name].append((lo, hi, me))
+        for name, lo, hi in rd:
+            reads.setdefault(name, []).append((lo, hi, me))
+        banks = sorted({x[1][0] for x in ins + outs if psum(x)})
+        if q == "t":
+            pre |= {lastpe[b] for b in banks if b in lastpe}
+            lastpe.update({b: me for b in banks})
+        free = {i for i in pre if calls[i][0] == q and (q == "t" or (CFG["soft"] and busy == took and calls[i][1] == calls[i][2] and i not in raw))}
+        calls.append((q, busy, took, sorted(pre), banks, free))
+        makes.append(make)
+        return me
 
-    def record(acc, eng, sem, val):
-        for name, lo, hi, w in acc:
-            old = seen.get(name, [])
-            if psum(name):
-                old = [e for e in old if e[3] == eng]
-            seen[name] = [e for e in old if not (lo <= e[0] and e[1] <= hi and (w or (not e[2] and e[4] == sem)))] + [(lo, hi, w, eng, sem, val)]
+    def op(q, ns, fn, ins, outs):
+        call(q, ns, ns, ("c" + q, 1, lambda sem: fn().then_inc(sem, 1)), ins, outs)
 
-    held = []
+    nd = [0, 0.0]
 
-    def issue(eng, fn):
-        if held:
-            held[-1].append((eng, fn))
-        else:
-            fn()
-
-    def chain(*parts):
-        held.append([])
-        for p in parts:
-            p[0](*p[1:])
-        out = [[]]
-        for e in held.pop():
-            if e[0] == "v" and any(x[0] == "v" for x in out[-1]):
-                out.append([])
-            out[-1].append(e)
-        return out
-
-    def weave(*chains):
-        for k in range(max(len(c) for c in chains)):
-            for c in chains:
-                for e in (c[k] if k < len(c) else []):
-                    issue(*e)
-
-    def op(eng, fn, ins, outs):
-        def go():
-            acc = ranges(ins, outs)
-            order(eng, acc)
-            sem = "c" + eng
-            cnt[sem] = cnt.get(sem, 0) + 1
-            fn().then_inc(T.sem[sem], 1)
-            record(acc, eng, sem, cnt[sem])
-        issue(eng, go)
-
-    nd = [0]
-
-    def dma(eng, *pairs):
-        def go():
-            sem = "ld%d" % nd[0]
-            nd[0] += 1
-            acc = ranges(pairs[1::2], pairs[0::2])
-            order(eng, acc)
-            cnt[sem] = 8 * len(pairs)
+    def dma(q, *pairs):
+        def make(sem):
             for out, in_ in zip(pairs[0::2], pairs[1::2]):
-                E[eng].dma_start(out[0], in_[0]).then_inc(T.sem[sem], 16)
-            record(acc, "d", sem, cnt[sem])
-        issue(eng, go)
+                E[q].dma_start(out[0], in_[0]).then_inc(sem, 16)
+        nb = sum(128 * x[3] * size(x) * (1 if x[0].shape[0] == 128 else 1 / 16) for x in pairs if x[1]) / (2 if all(x[1] for x in pairs) else 1)
+        nd[0] += 1
+        if not pairs[1][1]:
+            nd[1] += nb
+            nb = nd[1]
+        call(q, 60.0, LOCAL[0] + nb / LOCAL[1], ("ld%d" % nd[0], 8 * len(pairs), make), pairs[1::2], pairs[0::2])
+
+    dst = T.cores[(rank + 1) % len(T.cores)]
+    src = T.cores[(rank - 1) % len(T.cores)]
+
+    def remote(out, in_, arr, snt):
+        rid, pid, _se = topo.addr(dst)
+        ns = CFG["rrow"] + 128 * in_[3] * size(in_) / REMOTE[1]
+        me = call("g", CFG["riss"], REMOTE[0], (snt, len(topo.engines(core, dst)),
+                                                lambda sem: g.remote_dma(out[0], in_[0], T.sem[arr], sem, pid, rid, topo.mask(core, dst))), [in_], [])
+        call("r", ns, ns, (arr, len(topo.engines(src, core)), None), [], [out], [me])
 
     def ap(x):
         return x[0] if isinstance(x, tuple) else x
 
+    def vec(out, ins, k):
+        if out[2] or ins[0][2]:
+            return 50.0 + out[3] * CYCLE * (SCATTER if out[2] else GATHER)
+        return max(64.0, out[3] * k) * CYCLE + CFG["vfix"]
+
+    def half(*x):
+        return 0.5 if all(size(a) == 2 for a in x) else 1.0
+
     def ts(out, a, s1, o0, s2=None, o1=None):
         if o1 is None:
-            op("v", lambda: V.tensor_scalar(out[0], a[0], ap(s1), None, o0), [a, s1], [out])
+            op("v", vec(out, [a], half(out, a)), lambda: V.tensor_scalar(out[0], a[0], ap(s1), None, o0), [a, s1], [out])
         else:
-            op("v", lambda: V.tensor_scalar(out[0], a[0], ap(s1), ap(s2), o0, o1), [a, s1, s2], [out])
+            op("v", vec(out, [a], half(out, a)), lambda: V.tensor_scalar(out[0], a[0], ap(s1), ap(s2), o0, o1), [a, s1, s2], [out])
 
     def tt(out, a, b, alu):
-        op("v", lambda: V.tensor_tensor(out[0], a[0], b[0], alu), [a, b], [out])
+        op("v", vec(out, [a], 1.0 if psum(a) or psum(b) else 2.0), lambda: V.tensor_tensor(out[0], a[0], b[0], alu), [a, b], [out])
 
     def cp(out, a):
-        op("v", lambda: V.tensor_copy(out[0], a[0]), [a], [out])
+        op("v", vec(out, [a], half(out, a)), lambda: V.tensor_copy(out[0], a[0]), [a], [out])
 
     def scan(out, a, b, init, o0, o1):
-        op("v", lambda: V.tensor_tensor_scan(out[0], a[0], b[0], ap(init), o0, o1), [a, b, init], [out])
+        op("v", vec(out, [a], half(out, a, b)), lambda: V.tensor_tensor_scan(out[0], a[0], b[0], ap(init), o0, o1), [a, b, init], [out])
 
     def fill(out, pattern, base, cm=0):
-        op("g", lambda: g.iota(out[0], pattern, base, cm, allow_small_or_imprecise_dtypes=True), [], [out])
+        op("g", 130.0 + 2 * CYCLE * out[3], lambda: g.iota(out[0], pattern, base, cm, allow_small_or_imprecise_dtypes=True), [], [out])
 
     def act(out, a, func=AF.Copy, bias=0.0, scale=1.0):
-        op("s", lambda: S.activation(out[0], a[0], func, bias=ap(bias), scale=ap(scale)), [a, bias, scale], [out])
+        op("s", CFG["afix"] + out[3] * CYCLE * (GATHER if a[2] else 1.0), lambda: S.activation(out[0], a[0], func, bias=ap(bias), scale=ap(scale)),
+           [a, bias, scale], [out])
 
     def mm(items, group=True, start=True, stop=True):
         def f():
             for i, (o, l, r) in enumerate(items):
                 x = PE.matmul(o[0], l[0], r[0], (start and i == 0) or not group, (stop and i == len(items) - 1) or not group)
             return x
-        op("t", f, [x for it in items for x in it[1:]], [it[0] for it in items])
+        op("t", sum(max(64, r[3]) * (4 if size(r) == 4 else 1) for o, l, r in items) * PE_CYCLE + CFG["pefix"] * len(items), f,
+           [x for it in items for x in it[1:]], [it[0] for it in items])
 
     def M(n):
         i = MATS.index(n)
@@ -206,14 +249,14 @@ def rank_program(g, core, T, topo):
         return A("b%d" % p, lo, hi)
 
     for k in range(4):
-        dma("y", A("tb", 768 * k, 768 * k + 768), (T.tab[:, 768 * k:768 * k + 768], []))
-    dma("s", A("dn", 0, 192), (T.suf[:, :], []))
-    dma("s", A("dn", 192, 384), (T.lnk[:, :], []))
-    dma("s", A("ca"), (T.cx[:, :], []))
-    dma("s", A("vr", 0, SP * LN), (T.vv[:, 0:SP * LN], []))
-    dma("y", A("vr", SP * LN, RO * SP * LN), (T.vv[:, SP * LN:RO * SP * LN], []))
+        dma("y", A("tb", 768 * k, 768 * k + 768), HBM(T.tab[:, 768 * k:768 * k + 768]))
+        if k == 0:
+            dma("y", A("dn", 0, 192), HBM(T.suf[:, :]), A("dn", 192, 384), HBM(T.lnk[:, :]))
+        if k == 1:
+            dma("y", A("ca"), HBM(T.cx[:, :]), A("vr", 0, SP * LN), HBM(T.vv[:, 0:SP * LN]))
+    dma("y", A("vr", SP * LN, RO * SP * LN), HBM(T.vv[:, SP * LN:RO * SP * LN]))
 
-    PGC, PRC, PFC, P16, PM1, PP1, N15, N0, T1, C15, CW, PS, PB, LS, R23, PM2, PM15, J0 = range(18)
+    PGC, PRC, PFC, P16, PM1, PP1, N15, N0, T1, C15, PS, PB, LS, R23, PM2, PM15, J0, R0, R192 = range(19)
 
     def col(i):
         return A("pc", i, i + 1)
@@ -228,155 +271,152 @@ def rank_program(g, core, T, topo):
     fill(A("xr"), [[0, 16], [1, 16]], 0)
     fill(A("c32k"), [[0, 96]], BASE)
     fill(A("zer"), [[0, 96]], 0)
-    fill(A("c1k"), [[0, W // 16]], 1024)
+    fill(A("c1k"), [[0, W0 // 16]], 1024)
     fill(A("lf", 0, W0), [[0, W0]], 0)
     fill(A("dt", W0, PG + W0), [[0, PG]], 0)
     fill(A("h0"), [[0, 8]], 0)
-    fill(A("pw", 0, CAP), [[0, CAP]], 0)
     fill(A("rb3", CAP, CAP + 16), [[0, 16]], 0)
+    fill(A("pw", LOW, LOW + CAP), [[0, CAP]], 0)
 
-    def places():
-        ts(A("pi", 0, 1), A("iop"), 4, OP.arith_shift_right)
-        ts(A("pi", 1, 2), A("iop"), 15, OP.bitwise_and)
-        ts(col(T1), col(PFC), 16.0, OP.mult, 16.0, OP.add)
-        cp(A("pc", PGC, PRC + 1), A("pi"))
-        for i, k in ((PP1, 1.0), (PM15, -15.0), (PM1, -1.0), (PM2, -2.0)):
-            ts(col(i), col(PFC), k, OP.add)
-        ts(A("oh16"), A("xf", 0, 16), col(PRC), OP.is_equal)
-        ts(M("blk"), A("xg"), col(PGC), OP.is_equal)
-        ts(A("m31"), A("oh16"), 31.0 / 32, OP.mult)
-        for r in range(16):
-            act(A("expa", 128 * r, 128 * r + 128), M("blk"), scale=A("m31", r, r + 1))
-        ts(SEL("vsel"), A("xf"), col(T1), OP.is_equal)
-        ts(M("id"), xm, col(PFC), OP.is_equal)
-        ts(col(P16), col(PGC), 16.0, OP.mult, 16.0, OP.add)
-        ts(col(N15), oh(15), -1.0, OP.mult, 1.0, OP.add)
-        ts(col(C15), oh(15), 1.0 / 4096, OP.mult)
-        ts(M("low"), A("xr", 0, 128), col(PRC), OP.is_gt)
-        ts(SEL("selt"), A("xf"), col(P16), OP.is_equal)
-        ts(M("u1"), xm, col(PP1), OP.is_equal, col(N15), OP.mult)
-        tt(M("low"), M("low"), M("blk"), OP.mult)
-        ts(M("nid"), M("id"), -1.0, OP.mult)
-        tt(A("f32m", 256, 384), M("id"), M("u1"), OP.subtract)
-        ts(M("m150"), xm, col(PM15), OP.is_equal, col(C15), OP.mult)
-        ts(M("mdf"), A("f32m", 256, 384), 1.0 / 4096, OP.mult)
-        ts(M("ntri"), M("low"), -1.0, OP.mult)
-        ts(M("i14"), M("id"), 2.0 ** 14, OP.mult)
-        ts(M("e15"), M("blk"), oh(15), OP.mult, 2.0 ** 13, OP.mult)
-
-    def lanes():
-        cp(A("cl"), A("ca"))
-        ts(A("cf"), A("ca"), float(MID), OP.subtract, 1.0 / 4096, OP.mult)
+    ts(A("pi", 0, 1), A("iop"), 4, OP.arith_shift_right)
+    ts(A("pi", 1, 2), A("iop"), 15, OP.bitwise_and)
+    cp(A("pc", PGC, PRC + 1), A("pi"))
+    ts(col(T1), col(PFC), 16.0, OP.mult, 16.0, OP.add)
+    for i, k in ((PP1, 1.0), (PM15, -15.0), (PM1, -1.0), (PM2, -2.0)):
+        ts(col(i), col(PFC), k, OP.add)
+    ts(A("oh16"), A("xf", 0, 16), col(PRC), OP.is_equal)
+    ts(A("m31"), A("oh16"), 31.0 / 32, OP.mult)
+    ts(col(P16), col(PGC), 16.0, OP.mult, 16.0, OP.add)
+    ts(col(N15), oh(15), -1.0, OP.mult, 1.0, OP.add)
+    ts(col(N0), oh(0), -1.0, OP.mult, 1.0, OP.add)
+    ts(col(C15), oh(15), 1.0 / 65536, OP.mult)
+    ts(col(R0), oh(0), -BIG / 65536, OP.mult)
+    ts(col(R192), col(R0), 192.0, OP.add)
+    ts(col(J0), col(PRC), float(CAP), OP.add, SU, OP.mult)
+    ts(col(LS), oh(0), 1.0 / 64, OP.mult, oh(1), OP.add)
+    ts(col(R23), oh(2), oh(3), OP.add)
+    ts(col(PS), oh(0), 32.0 / 31 / 4096, OP.mult)
+    ts(col(PB), oh(15), 1024.0, OP.mult)
+    ts(M("id"), xm, col(PFC), OP.is_equal)
+    ts(M("blk"), A("xg"), col(PGC), OP.is_equal)
+    ts(M("low"), A("xr", 0, 128), col(PRC), OP.is_gt)
+    tt(M("low"), M("low"), M("blk"), OP.mult)
+    ts(M("u1"), xm, col(PP1), OP.is_equal, col(N15), OP.mult)
+    ts(M("l1"), xm, col(PM1), OP.is_equal, col(N0), OP.mult)
+    ts(M("l2"), xm, col(PM2), OP.is_equal)
+    ts(A("f32m", 512, 640), xm, col(PM15), OP.is_equal, col(C15), OP.mult)
+    for r in range(16):
+        act(A("expa", 128 * r, 128 * r + 128), M("blk"), scale=A("m31", r, r + 1))
+    cp(A("f32m", 0, 128), M("id"))
+    tt(A("f32m", 256, 384), M("id"), M("u1"), OP.subtract)
+    for n, a, k in (("nid", M("id"), -1.0), ("ntri", M("low"), -1.0), ("i14", M("id"), 2.0 ** 14), ("i31", M("id"), 31.0), ("i512", M("id"), 512.0),
+                    ("blk2", M("blk"), 2.0), ("blks", M("blk"), 2.0 ** -37)):
+        ts(M(n), a, k, OP.mult)
+    ts(A("f32m", 384, 512), A("f32m", 256, 384), 1.0 / 65536, OP.mult)
+    tt(A("f32m", 128, 256), M("ntri"), M("id"), OP.subtract)
+    ts(M("e15"), M("blk"), oh(15), OP.mult, 2.0 ** 13, OP.mult)
+    tt(M("moh"), M("id"), M("l1"), OP.subtract)
+    tt(M("l2"), M("l2"), M("id"), OP.add)
+    ts(M("mv"), M("l2"), col(R23), OP.mult)
+    for n, k in (("slt", -2.0 ** 13), ("slq", 2.0 ** 13)):
+        ts(M(n), M("id"), k, OP.mult)
+        tt(M(n), M(n), M("low"), OP.add)
+        ts(M(n), M(n), 2.0 ** -37, OP.mult)
+    ts(SEL("vsel"), A("xf"), col(T1), OP.is_equal)
+    ts(SEL("selt"), A("xf"), col(P16), OP.is_equal)
+    for n, k in (("sel2", oh(2)), ("sel3", oh(3)), ("lsel", col(LS)), ("seln", BASE / 16.0)):
+        ts(SEL(n), SEL("selt"), k, OP.mult)
+    ts(SEL("nsel"), SEL("selt"), oh(0), OP.mult, -1.0 / 64, OP.mult)
+    ts(A("th0"), A("xr"), 0.0, OP.is_gt, 0.5, OP.mult)
+    ts(A("th1"), A("xr"), 0.0, OP.is_equal, 2.0, OP.mult)
+    scan(A("thr"), A("th0"), A("th1"), 0.0, OP.mult, OP.add)
+    tt(A("th2"), A("thr", 0, 16), A("oh16"), OP.mult)
+    scan(A("th3"), A("th2"), A("zer", 0, 16), 0.0, OP.add, OP.add)
+    ts(M("blkw"), M("blk"), A("th3", 15, 16), OP.mult, 0.5, OP.mult)
+    ts(A("inc", 0, 8), A("zer", 0, 8), 0.5, OP.add)
+    ts(A("jg", 0, 160), A("xf"), 16 * SU, OP.mult, col(J0), OP.add)
+    for t in range(1, RO):
+        act(A("jg", 160 * t, 160 * t + 160), A("jg", 0, 160), bias=t * CAP * SU)
+    act(A("jq"), A("jg", 0, LOW // 16), bias=1.0 - (LOW + CAP) * SU)
+    for h in range(2):
+        act(A("dj", 8 * h, 8 * h + 8), A("jg", 0, 8), bias=float(-B - MID - CAP), scale=1 / SU)
 
     def targets_list(st):
         if st < RO * SP:
             mm([(BK(7, 0, 160), SEL("vsel", r, slice(0, 8)), A("vr", st * LN + r, (st + 1) * LN, 16)) for r in range(16)])
             act(A("v8", 160 * st, 160 * st + 160), BK(7, 0, 160), scale=0.125)
 
+    cp(A("cl"), A("ca"))
+    ts(A("cf"), A("ca"), float(MID), OP.subtract, 1.0 / 4096, OP.mult)
+    targets_list(0)
+    ts(A("dg", 384, 576), A("dn", 192, 384), float(4096 - MID), OP.add)
+    ts(A("dg", 0, 192), A("dg", 384, 576), 63, OP.bitwise_and)
+    ts(A("dg", 192, 384), A("dg", 384, 576), 6, OP.arith_shift_right, 63, OP.bitwise_and)
+    ts(A("dgb"), A("dg", 0, 384), 1.0 / 64, OP.mult)
+    dma("y", A("lf", 0, W0, rows=slice(2, 128, 16)), A("dgb", 0, 192), A("lf", 0, W0, rows=slice(3, 128, 16)), A("dgb", 192, 384))
+    ts(A("fd"), A("dn", 0, 192), float(MID), OP.subtract, 1.0 / 4096, OP.mult)
+    dma("y", A("dt", PG, PG + W0, rows=slice(0, 128, 16)), A("fd"), A("dt", PG, PG + W0, rows=slice(15, 128, 16)), A("c1k"))
+
     def counts_table(k):
-        c = A("ci", 768 * (k // 3), 768 * (k // 3) + 768)
+        c = A("ci", 768 * (k % 2), 768 * (k % 2) + 768)
         q = A("kt", 768 * k, 768 * k + 768)
         ts(c, A("tb", 768 * k, 768 * k + 768), 15, OP.bitwise_and)
         ts(q, c, 31.0, OP.mult, 1.0, OP.max)
         act(q, q, bias=-1.0 - EPS)
 
     def pointer_table(k):
-        c = A("ci", 768, 1536)
         o = 768 * (k % 2)
-        ts(c, A("tb", 768 * k, 768 * k + 768), 4, OP.arith_shift_right)
-        ts(A("s16", o, o + 768), c, float(MID), OP.subtract)
+        ts(A("ag", o, o + 768), A("tb", 768 * k, 768 * k + 768), 7.5 + 16 * MID, OP.subtract, BIG, OP.add)
         if k == 0:
-            mm([(BK(1, 0, 1), M("m150"), A("s16", 0, 1))])
+            mm([(BK(1, 0, 1), A("f32m", 512, 640), A("ag", 0, 1))])
+            act(A("dt", PG, PG + 1), BK(1, 0, 1), AF.Identity, bias=col(R0))
         for h in range(2):
-            mm([(BK(2 + h, 0, 384), M("mdf"), A("s16", o + 384 * h, o + 384 * h + 384))])
-            act(A("rb", 384 * h, 384 * h + 384), BK(2 + h, 0, 384), bias=192.0)
-
-    def pointer_rest(k):
-        for h in range(2):
-            o = 768 * (k % 2) + 384 * h
-            bk = BK(4 - 4 * h, 0, 384)
-            mm([(bk, M("mdf"), A("s16", o, o + 384)), (bk, M("nid"), A("rb", 384 * h, 384 * h + 384))])
-            act(A("dt", 768 * k + 384 * h, 768 * k + 384 * h + 384), bk, bias=192.0)
-
-    def escape_page():
-        ts(A("fd"), A("dn", 0, 192), float(MID), OP.subtract, 1.0 / 4096, OP.mult)
-        dma("y", A("dt", PG, PG + W0, rows=slice(0, 128, 16)), A("fd"), A("dt", PG, PG + W0, rows=slice(15, 128, 16)), A("c1k", 0, W0 // 16))
-
-    def root_page():
-        act(A("dt", PG, PG + 1), BK(1, 0, 1))
-
-    def link_digits():
-        ts(A("dg", 384, 576), A("dn", 192, 384), float(4096 - MID), OP.add)
-        cp(A("fl"), A("dn", 0, 192))
-        ts(A("dg", 0, 192), A("dg", 384, 576), 63, OP.bitwise_and)
-        ts(A("dg", 192, 384), A("dg", 384, 576), 6, OP.arith_shift_right, 63, OP.bitwise_and)
-        ts(A("dgb"), A("dg", 0, 384), 1.0 / 64, OP.mult)
-        dma("y", A("lf", 0, W0, rows=slice(2, 128, 16)), A("dgb", 0, 192), A("lf", 0, W0, rows=slice(3, 128, 16)), A("dgb", 192, 384))
-
-    def suffix_links(h, call):
-        call(A("pw", LN + 1536 * h, LN + 1536 * h + 1536), IX(A("lf", 0, W0), A("fl", 96 * h, 96 * h + 96)))
-
-    def suffix_links_back():
-        mm(tolist(BK(7, 0, 192), "sel2", "pw", LN, LN + W0))
-        mm(tolist(BK(7, 192, 384), "sel3", "pw", LN, LN + W0))
-        act(A("lfd"), BK(7, 0, 384))
-        dma("y", A("lf", 0, W0, rows=slice(0, 128, 16)), A("lfd", 0, 192), A("lf", 0, W0, rows=slice(1, 128, 16)), A("lfd", 192, 384))
-
-    def hop_constants():
-        op("v", lambda: V.memset(T.inc[:, 0:8], 0.5), [], [A("inc", 0, 8)])
-        ts(M("slt"), M("id"), -2.0 ** 13, OP.mult)
-        ts(col(J0), col(PRC), float(CAP), OP.add, SU, OP.mult)
-        ts(col(LS), oh(0), 1.0 / 64, OP.mult, oh(1), OP.add)
-        tt(M("slt"), M("slt"), M("low"), OP.add)
-        ts(A("jg", 0, 160), A("xf"), 16 * SU, OP.mult, col(J0), OP.add)
-        ts(M("blks"), M("blk"), 2.0 ** -37, OP.mult)
-        ts(M("slt"), M("slt"), 2.0 ** -37, OP.mult)
-        ts(A("jg", 480, 640), A("jg", 0, 160), 3 * CAP * SU, OP.add)
-        ts(SEL("lsel"), SEL("selt"), col(LS), OP.mult)
-        ts(SEL("nsel"), SEL("selt"), oh(0), OP.mult, -1.0 / 64, OP.mult)
-
-    def link_selectors():
-        ts(SEL("sel2"), SEL("selt"), oh(2), OP.mult)
-        ts(SEL("sel3"), SEL("selt"), oh(3), OP.mult)
-
-    def write_back_constants():
-        ts(A("th0"), A("xr"), 0.0, OP.is_gt, 0.5, OP.mult)
-        ts(A("th1"), A("xr"), 0.0, OP.is_equal, 2.0, OP.mult)
-        ts(col(N0), oh(0), -1.0, OP.mult, 1.0, OP.add)
-        scan(A("thr"), A("th0"), A("th1"), 0.0, OP.mult, OP.add)
-        ts(M("l1"), xm, col(PM1), OP.is_equal, col(N0), OP.mult)
-        tt(A("th2"), A("thr", 0, 16), A("oh16"), OP.mult)
-        tt(M("moh"), M("id"), M("l1"), OP.subtract)
-        scan(A("th3"), A("th2"), A("zer", 0, 16), 0.0, OP.add, OP.add)
-        ts(col(R23), oh(2), oh(3), OP.add)
-        ts(M("blkw"), M("blk"), A("th3", 15, 16), OP.mult, 0.5, OP.mult)
-        ts(M("l1"), xm, col(PM2), OP.is_equal)
-        ts(col(PS), oh(0), 32.0 / 31 / 4096, OP.mult)
-        tt(M("l1"), M("l1"), M("id"), OP.add)
-        ts(col(PB), oh(15), 1024.0, OP.mult)
-        tt(A("f32m", 128, 256), M("ntri"), M("id"), OP.subtract)
-        ts(M("mv"), M("l1"), col(R23), OP.mult)
-        ts(M("blk2"), M("blk"), 2.0, OP.mult)
-        ts(M("i31"), M("id"), 31.0, OP.mult)
-        ts(M("i512"), M("id"), 512.0, OP.mult)
-        ts(SEL("seln"), SEL("selt"), BASE / 16.0, OP.mult)
-        cp(A("f32m", 0, 128), M("id"))
-
-    def late_constants():
-        for h in range(2):
-            act(A("dj", 8 * h, 8 * h + 8), A("jg", 0, 8), bias=float(-B - MID - CAP), scale=1 / SU)
-        for t in (1, 2):
-            act(A("jg", 160 * t, 160 * t + 160), A("jg", 0, 160), bias=t * CAP * SU)
+            s, rb, bk = A("ag", o + 384 * h, o + 384 * h + 384), A("rb", 384 * h, 384 * h + 384), BK(4 - 4 * h, 0, 384)
+            mm([(BK(2 + h, 0, 384), A("f32m", 384, 512), s)])
+            if 2 * k + h in CFG["modv"]:
+                r = A("ag", 1536 + 384 * h, 1920 + 384 * h)
+                ts(r, BK(2 + h, 0, 384), MAGIC, OP.add, MAGIC, OP.subtract)
+                tt(A("dt", 768 * k + 384 * h, 768 * k + 384 * h + 384), BK(2 + h, 0, 384), r, OP.subtract)
+                continue
+            act(rb, BK(2 + h, 0, 384), AF.Identity, bias=col(R192))
+            mm([(bk, A("f32m", 384, 512), s)], stop=False)
+            mm([(bk, M("nid"), rb)], start=False)
+            act(A("dt", 768 * k + 384 * h, 768 * k + 384 * h + 384), bk, AF.Identity, bias=col(R192))
+    for f, k in ((counts_table, 0), (pointer_table, 0), (counts_table, 1), (pointer_table, 1), (counts_table, 2), (counts_table, 3),
+                 (pointer_table, 2), (pointer_table, 3)):
+        f(k)
+    cp(A("fl"), A("dn", 0, 192))
+    for h in range(4):
+        (cp if h // 2 in CFG["lpv"] else act)(A("pw", LN + 768 * h, LN + 768 * h + 768), IX(A("lf", 0, W0), A("fl", 48 * h, 48 * h + 48)))
+    targets_list(1)
+    for k, n in enumerate(("sel2", "sel3")):
+        mm(tolist(BK(7, 192 * k, 192 * k + 192), n, "pw", LN, LN + W0))
+    act(A("lfd"), BK(7, 0, 384))
+    dma("y", A("lf", 0, W0, rows=slice(0, 128, 16)), A("lfd", 0, 192), A("lf", 0, W0, rows=slice(1, 128, 16)), A("lfd", 192, 384))
 
     def counts(t, s, x):
-        for p in PIECES[x]:
-            kw = IX(A("kt", 0, W0 + B * t), L("cl", p))
+        shared = [p for p in PIECES[x] if t + s > 0 and p in CFG["shared1" if s else "shared"]]
+        own = [p for p in PIECES[x] if p not in shared]
+        for lo, hi in ([(own[0], own[-1] + 1)] if CFG["merge"] else [(p, p + 1) for p in own]):
+            kw = IX(A("kt", 0, W0 + B * t), A("cl", 32 * lo, 32 * hi))
             if t + s == 0:
-                cp(P("kap", p), kw)
+                cp(A("kap", 512 * lo, 512 * hi), kw)
             else:
-                tt(P("kap", p), kw, P("ne", p), OP.mult)
+                tt(A("kap", 512 * lo, 512 * hi), kw, A("ne", 512 * lo, 512 * hi), OP.mult)
+        for p in shared:
+            if s == 0:
+                mm([(BK(p), M("id"), P("ne", p))])
+            act(P("ag", p), IX(A("kt", 0, W0 + B * t), L("cl", p)))
+            tt(P("kap", p), BK(p), P("ag", p), OP.mult)
         n = CH[x][1] - CH[x][0]
         mm([(TX(x, 0), M("id"), A("c32k", 0, n))] + tolist(TX(x, 0), "selt", "kap", 16 * CH[x][0], 16 * CH[x][1]))
+
+    def two(first, rest):
+        if CFG["early"]:
+            mm(first, stop=False)
+            mm(rest, start=False)
+        else:
+            mm(first + rest)
 
     def targets(st, x):
         s = TX(x, 0)
@@ -384,126 +424,117 @@ def rank_program(g, core, T, topo):
         tt(s, s, X("r32", x), OP.subtract)
         tt(s, s, X("v8", x, 160 * st), OP.mult)
         ts(X("qq", x), s, -1.0, OP.mult, BASE - 127.5 / 8, OP.add)
-
-    def page(x):
-        s = TX(x, 0)
         tt(s, X("qq", x), X("r32", x), OP.is_ge)
         tt(X("yy", x), s, X("cf", x), OP.add)
         ts(X("c2", x), X("yy", x), 4096.0, OP.mult, float(MID), OP.add)
 
     ESC = 1.0 - (MID - 0.5) / 4096
 
-    def compare(p):
-        mm([(BK(p), M("ntri"), P("kap", p))] + spread("b%d" % p, 0, 32, L("qq", p)))
-        act(P("cd", p), BK(p), AF.Sigmoid, bias=-16.0 * (BASE // 32 * 31 - 8), scale=16.0)
+    def compare(s, p):
+        two([(BK(p), M("ntri"), P("kap", p))], spread("b%d" % p, 0, 32, L("qq", p)))
+        act(BK(p) if p in CFG["late" if s else "late0"] else P("cd", p), BK(p), AF.Sigmoid, bias=-16.0 * (BASE // 32 * 31 - 8), scale=16.0)
 
-    def pointer(t, p):
-        tt(P("ds", p), IX(A("dt", 0, PG + W0 + B * t), L("c2", p)), P("cd", p), OP.mult)
-
-    def pointer_sum(x):
+    def pointers(t, s, x):
+        for p in PIECES[x]:
+            dw = IX(A("dt", 0, PG + W0 + B * t), L("c2", p))
+            if p in CFG["late" if s else "late0"]:
+                act(P("ag", p), dw)
+                tt(P("ds", p), BK(p), P("ag", p), OP.mult)
+            else:
+                tt(P("ds", p), dw, P("cd", p), OP.mult)
+            if s == 0:
+                two([(BK(p), M("i14"), P("kap", p))], [(BK(p), M("e15"), P("ds", p))])
+                act(BK(p) if p in CFG["shared1"] else P("ne", p), BK(p), AF.Sigmoid, bias=256.0 * (2.0 ** 23 - 0.5), scale=-256.0)
         mm(tolist(TX(x, 1), "selt", "ds", 16 * CH[x][0], 16 * CH[x][1]))
+        context(x, 1, "cl")
 
-    def context(x, k):
+    def context(x, k, out):
         s = TX(x, k)
         ts(X("rr", x), s, MAGIC, OP.add, MAGIC, OP.subtract)
         tt(X("cf", x), s, X("rr", x), OP.subtract)
-        ts(X("cl", x), X("cf", x), 4096.0, OP.mult, float(MID), OP.add)
-
-    def marks0(p):
-        mm([(BK(p), M("i14"), P("kap", p)), (BK(p), M("e15"), P("ds", p))])
-        act(P("ne", p), BK(p), AF.Sigmoid, bias=256.0 * (2.0 ** 23 - 0.5), scale=-256.0)
-
-    def marks1(p):
-        mm([(BK(p), M("i14"), P("kap", p))] + spread("b%d" % p, 0, 32, L("es", p)))
-        act(P("win", p, OWN), BK(p), AF.Sigmoid, bias=256.0 * (31 * 2.0 ** 18 - 0.5), scale=-256.0)
+        ts(X(out, x), X("cf", x), 4096.0, OP.mult, float(MID), OP.add)
 
     H = ["h0", "h1"]
 
-    def no_f():
-        act(A("hz"), A(H[0]), AF.Relu, bias=1.0, scale=-8.0)
-
     def first_escape():
         old, new = H
+        act(A("hz"), A(old), AF.Relu, bias=1.0, scale=-8.0)
         ts(A("e8"), A("yy", 0, 8), ESC, OP.is_gt)
         tt(A("ht"), A("hz"), A("yy", 0, 8), OP.mult)
         tt(A("ht"), A("ht"), A(old), OP.add)
         tt(A(new), A("ht"), A("e8"), OP.mult)
         H.reverse()
 
-    def escapes(x):
-        ts(X("es", x), X("yy", x), ESC, OP.is_gt, 2.0 ** 23, OP.mult)
-        mm([(TX(x, 2), M("slt"), X("es", x))])
-        mm([(TX(x, 3), M("blks"), X("es", x))])
-
-    def slots(x):
+    def slots(t, x):
         lo, hi = CH[x]
+        ts(X("es", x), X("yy", x), ESC, OP.is_gt, 2.0 ** 23, OP.mult)
+        mm([(TX(x, 3), M("blks"), X("es", x))])
+        mm([(TX(x, 2), M("slt"), X("es", x))])
         scan(X("inc", x, 8), TX(x, 3), A("zer", 0, hi - lo), A("inc", 7 + lo, 8 + lo), OP.add, OP.add)
         tt(X("sa", x), TX(x, 2), X("inc", x, 7), OP.add)
-        tt(TX(x, 3), X("sa", x), X("jg", x, 160 * (RO - 1)), OP.min)
-        ts(X("sl", x), TX(x, 3), 1 / SU, OP.mult)
+        k = max(lo, LOW // 16)
+        o = A(TB[x], 3 * (hi - lo), 3 * (hi - lo) + hi - k)
+        tt(o, A("sa", k, hi), A("jg", 160 * (RO - 1) + k, 160 * (RO - 1) + hi), OP.min)
+        ts(A("sl", k, hi), o, 1 / SU, OP.mult)
+        if lo == 0:
+            o = BK(5, 5 * hi, 5 * hi + LOW // 16)
+            mm([(o, M("slq"), A("es", 0, LOW // 16))])
+            tt(o, o, A("inc", 7, 7 + LOW // 16), OP.add)
+            tt(o, o, A("jq"), OP.max)
+            ts(A("sl", 0, LOW // 16), o, 1.0 - LOW * SU, OP.subtract, 1 / SU, OP.mult)
+        for p in PIECES[x]:
+            act(P("lg", p), IX(A("lf", 0, W0 + B * t), L("cl", p)))
+            if t < RO - 1:
+                two([(BK(p), M("i14"), P("kap", p))], spread("b%d" % p, 0, 32, L("es", p)))
+                act(P("win", p, OWN), BK(p), AF.Sigmoid, bias=256.0 * (31 * 2.0 ** 18 - 0.5), scale=-256.0)
 
-    dst = T.cores[(rank + 1) % len(T.cores)]
-    src = T.cores[(rank - 1) % len(T.cores)]
-
-    def remote(out, in_, arr, snt):
-        def go():
-            acc = ranges([in_], [])
-            order("g", acc)
-            rid, pid, _se = topo.addr(dst)
-            g.remote_dma(out[0], in_[0], T.sem[arr], T.sem[snt], pid, rid, topo.mask(core, dst))
-            cnt[snt] = len(topo.engines(core, dst))
-            cnt[arr] = len(topo.engines(src, core))
-            record(acc, "r", snt, cnt[snt])
-            record(ranges([], [out]), "r", arr, cnt[arr])
-        issue("g", go)
-
-    def landing(t):
-        return A("rb3", 0, CAP) if t == RO - 1 else A("win", OWN - CAP * (t + 1), OWN - CAP * t)
-
-    def links(t, x):
-        act(A("lg", 16 * CH[x][0], 16 * CH[x][1]), IX(A("lf", 0, W0 + B * t), X("cl", x)))
-
-    def scatter(t, p):
-        o = IX(A("pw"), L("sl", p))
+    def scatter(t, lo, hi):
+        o = IX(A("pw", 0, LOW + hi) if lo < LOW else A("pw", LOW, LOW + W0 + LN), A("sl", lo // 16, hi // 16))
         if t < RO - 1:
-            tt(o, P("lg", p), P("win", p, OWN), OP.add)
+            tt(o, A("lg", lo, hi), A("win", OWN + lo, OWN + hi), OP.add)
         else:
-            cp(o, P("lg", p))
+            cp(o, A("lg", lo, hi))
 
-    def reading_list(t, x):
-        if x == "A":
-            ts(A("nsf"), A("nsi", 4 * t + 3, 4 * t + 4), 0.5, OP.subtract, CAP * SU, OP.min)
-        ts(TX(x, 0), X("sa", x), A("nsf"), OP.is_ge)
-        tt(TX(x, 2), TX(x, 0), X("sa", x), OP.add)
-        if t < RO - 1:
-            tt(X("sx", x), TX(x, 2), X("jg", x, 160 * t), OP.min)
-            ts(X("rl", x), X("sx", x), 1 / SU, OP.mult)
-        else:
-            ts(X("rl", x), TX(x, 2), CAP * SU, OP.min, 1 / SU, OP.mult)
+    def payload_out(t, lo, hi, arr, snt):
+        at = 0 if t == RO - 1 else OWN - CAP * (t + 1)
+        remote(A("rb3" if t == RO - 1 else "win", at + lo, at + hi), A("pw", LOW + lo, LOW + hi), arr + str(t), snt + str(t))
 
-    def receive(t, p, call):
-        win = A("rb3") if t == RO - 1 else A("win", OWN - CAP * (t + 1), OWN + LN)
-        call(P("val", p), IX(win, L("rl", p)))
+    def send(t):
+        remote(A("nsi", 4 * t, 4 * t + 4), A("inc", 164, 168), "nar%d" % t, "nsn%d" % t)
+        cuts = CFG["cuts"]
+        for lo, hi in zip(cuts, cuts[1:]):
+            scatter(t, lo, hi)
+        payload_out(t, LOW, CAP, "har", "hsn")
+        mid = CFG["mid"]
+        if mid:
+            scatter(t, mid, LOW)
+            payload_out(t, mid, LOW, "mar", "msn")
+        scatter(t, 0, mid or LOW)
+        payload_out(t, 0, mid or LOW, "arr", "snt")
 
-    def flags(t, x):
+    def receive(t, x):
         last = t == RO - 1
         lo, hi = 16 * CH[x][0], 16 * CH[x][1]
-        mm(tolist(TX(x, 4), "lsel", "val", lo, hi), stop=last)
+        ts(TX(x, 0), X("sa", x), A("nsf"), OP.is_ge)
+        tt(TX(x, 2), TX(x, 0), X("sa", x), OP.add)
+        if last:
+            ts(X("rl", x), TX(x, 2), CAP * SU, OP.min, 1 / SU, OP.mult)
+        else:
+            tt(TX(x, 2), TX(x, 2), X("jg", x, 160 * t), OP.min)
+            ts(X("rl", x), TX(x, 2), 1 / SU, OP.mult)
+        tt(X("cw", x), TX(x, 0), X("cf", x), OP.mult)
+        if x == "A" and not last:
+            tt(A(H[0]), A(H[0]), TX("A", 0, 8), OP.mult)
+        for p in PIECES[x]:
+            (cp if p in CFG["recvv"] or (last and p % 2 == 0) else act)(P("val", p), IX(A("rb3") if last else A("win", OWN - CAP * (t + 1), OWN + LN), L("rl", p)))
+        own = [(TX(x, 4), A("f32m", 0, 128), X("cw", x))]
+        mm(tolist(TX(x, 4), "lsel", "val", lo, hi) + (own if last else []), stop=last)
         if not last:
             ts(A("ne", lo, hi), A("val", lo, hi), 1.0, OP.is_ge)
-            mm(tolist(TX(x, 4), "nsel", "ne", lo, hi), start=False)
+            mm(own + tolist(TX(x, 4), "nsel", "ne", lo, hi), start=False)
+        context(x, 4, "yo" if last else "cl")
 
-    def link_context(t, x):
-        s = TX(x, 4)
-        tt(s, s, X("cw", x), OP.add)
-        if t < RO - 1:
-            context(x, 4)
-        else:
-            ts(X("rr", x), s, MAGIC, OP.add, MAGIC, OP.subtract)
-            tt(X("cf", x), s, X("rr", x), OP.subtract)
-            ts(X("yo", x), X("cf", x), 4096.0, OP.mult, float(MID), OP.add)
-
-    def wb_keys(t):
+    def wb_first(t):
         new, old = H
         tt(A("cnd"), A(old), A(new), OP.is_gt)
         tt(A("ka", 0, 8), A("ka", 0, 8), A("cnd"), OP.mult)
@@ -513,268 +544,145 @@ def rank_program(g, core, T, topo):
         ts(A("k32"), A("k16", 0, 16), 31.0 / 32, OP.mult)
         ts(A("fdu"), A("k16", 0, 16), float(MID), OP.add, float(W0 + B * t - 1), OP.min)
         ts(A("nc"), A("k16", 0, 16), 2048.0, OP.is_equal, 4.0, OP.mult)
-
-    def wb_onehot(t):
-        o = BK(1, 0, B)
-        mm([(o, M("moh"), A("cd", 0, B))])
-        act(A("ohb"), o)
-        if t < RO - 1:
-            act(A("ohf"), o)
-            act(A("up"), o, bias=1024.0, scale=30.0 - EPS - 1024.0)
-            act(A("lo"), o, bias=-1.0, scale=31.0 - EPS)
-            act(A("cap"), o, bias=1024.0, scale=433.0 - EPS - 1024.0)
-        else:
-            act(A("nob"), o, bias=1.0, scale=-1.0)
-            act(A("cap"), o, bias=16.0, scale=-2.0)
-
-    def wb_grow(t):
-        if t < RO - 1:
-            o = BK(1, 0, B)
-            mm([(o, M("i31"), A("ohb")), (o, M("nid"), A("zr"))])
-            act(A("gro"), o, AF.Relu)
-
-    def wb_equal():
         mm([(BK(0, 0, 256), M("nid"), A("thr"))] + spread("b0", 0, 16, A("nc")), stop=False)
-        for i in range(16):
-            k, p = divmod(i, 8)
-            ts(A("eq", B * i + 16 * p, B * i + B), BK(7, B * k + 16 * p, B * k + B), A("k32", i, i + 1), OP.is_equal)
-            if p == 7:
-                it = []
-                for p in range(8):
-                    e = B * (8 * k + p) + 16 * p
-                    it.append((BK(0, B * k + 16 * p, B * k + 16 * p + 16), M("blkw"), A("eq", e, e + 16)))
-                    if p < 7:
-                        it.append((BK(0, B * k + 16 * p + 16, B * k + B), M("blk2"), A("eq", e + 16, e + B - 16 * p)))
-                mm(it, start=False, stop=k == 1)
-
-    def wb_first(t):
+        for k in range(2):
+            it = []
+            for p in range(8):
+                e, o = B * (8 * k + p) + 16 * p, B * k + 16 * p
+                ts(A("eq", e, e + B - 16 * p), BK(7, o, B * k + B), A("k32", 8 * k + p, 8 * k + p + 1), OP.is_equal)
+                it.append((BK(0, o, o + 16), M("blkw"), A("eq", e, e + 16)))
+                if p < 7:
+                    it.append((BK(0, o + 16, B * k + B), M("blk2"), A("eq", e + 16, e + B - 16 * p)))
+            mm(it, start=False, stop=k == 1)
         act(A("kr"), BK(0, 0, 256), AF.Sigmoid, scale=-2.0 ** 23)
         o = BK(0, 256, 272)
         mm([(o, M("nid"), A("c32k", 0, 16)), (o, M("id"), A("k16", 0, 16))] + tolist(o, "seln", "kr", 0, 256))
-
-    def wb_places():
-        tt(A("fy"), BK(0, 256, 272), A("dj"), OP.max)
+        tt(A("fy"), o, A("dj"), OP.max)
         ts(A("lw"), A("fy"), float(MID + B), OP.add)
 
-    def wb_new(t):
+    def write_back(t):
         wn = W0 + B * t
-        l8 = A("cl", 0, 8)
+        l8, lf, ld = A("cl", 0, 8), A("fdu", 0, 8), A("fdu", 8, 16)
+        o = BK(1, 0, B)
+        if t == RO - 1 and CFG["mini"]:
+            l8, o, s = A("c8"), BK(7, 256, 384), BK(7, 384, 392)
+            tt(A("d8"), IX(A("dt", 0, PG + wn), A("c2", 0, 8)), A("cd", 0, B), OP.mult)
+            mm(tolist(s, "selt", "d8", 0, B))
+            ts(A("ht"), s, MAGIC, OP.add, MAGIC, OP.subtract)
+            tt(A("ht"), s, A("ht"), OP.subtract)
+            ts(l8, A("ht"), 4096.0, OP.mult, float(MID), OP.add)
+        mm([(o, M("moh"), A("cd", 0, B))])
+        act(A("ohb"), o)
         if t == RO - 1:
+            act(A("nob"), o, bias=1.0, scale=-1.0)
+            act(A("cap"), o, bias=16.0, scale=-2.0)
             act(A("hx"), IX(A("ynb", 0, wn), l8), bias=128.25, scale=0.5)
-            return
-        act(A("hx"), IX(A("kt", 0, wn), l8), bias=128.25 + 1.0 / 62, scale=1.0 / 62)
-        act(A("dt", wn, wn + B), IX(A("dt", 0, wn), l8))
-        ts(A("k16", 16, 24), A("cf", 0, 8), 4096.0, OP.mult)
-
-    def wb_new_rows(t):
-        if t < RO - 1:
-            act(A("g1"), IX(A("lf", 0, W0 + B * t), A("cl", 0, 8)))
-            mm(spread("b1", 0, 8, A("k16", 16, 24)), False)
-            mm([(BK(1, B, 2 * B), M("mv"), A("g1"))])
-
-    def wb_new_counts(t):
-        wn = W0 + B * t
-        o = BK(1, 2 * B, 3 * B)
-        mm([(o, M("id" if t == RO - 1 else "i31"), A("hx")), (o, M("i512"), A("kr", 0, B))])
-        if t == RO - 1:
+            mm([(o, M("id"), A("hx")), (o, M("i512"), A("kr", 0, B))])
             act(A("ynb", wn, wn + B), o, AF.Relu, bias=-640.0)
+            tt(A("xb"), IX(A("ynb", 0, wn), lf), A("nob"), OP.mult)
+            tt(IX(A("ynb", -B, wn), A("lw", 0, 8)), A("xb"), A("ohb"), OP.add)
+            tt(A("xb"), IX(A("ynb", 0, wn), ld), A("cap"), OP.min)
+            tt(IX(A("ynb", -B, wn), A("lw", 8, 16)), A("xb"), A("ohb"), OP.add)
+            return
+        act(A("up"), o, bias=1024.0, scale=30.0 - 1024.0)
+        act(A("lo"), o, bias=-1.0, scale=31.0)
+        act(A("cap"), o, bias=1024.0, scale=433.0 - 1024.0)
+        wr = A("wr", B * t, B * t + B)
+        act(wr, xm, bias=(wn - MID) / 4096.0, scale=1.0 / 4096)
+        act(A("af"), IX(A("dt", 0, wn), lf))
+        mm([(BK(1, 384, 512), A("f32m", 0, 128), wr), (BK(1, 384, 512), A("f32m", 128, 256), A("af"))])
+        tt(A("dl"), BK(1, 384, 512), A("ohb"), OP.mult)
+        act(A("zr"), IX(A("kt", 0, wn), ld), AF.Relu, scale=-1 / EPS)
+        mm([(o, M("i31"), A("ohb")), (o, M("nid"), A("zr"))])
+        act(A("gro"), o, AF.Relu)
+        act(A("hx"), IX(A("kt", 0, wn), l8), bias=128.25 + 1.0 / 62, scale=1.0 / 62)
+        o = BK(1, 2 * B, 3 * B)
+        mm([(o, M("i31"), A("hx")), (o, M("i512"), A("kr", 0, B))])
+        if CFG["hyv"]:
+            ts(A("kt", wn, wn + B), o, 3969.0 + 512.0, OP.subtract, -EPS, OP.max)
         else:
             act(A("hy"), o, AF.Relu, bias=-3969.0 - 512.0)
             act(A("kt", wn, wn + B), A("hy"), bias=-EPS)
-
-    def wb_new_pages(t):
-        wn = W0 + B * t
-        if t < RO - 1:
-            act(A("dt", PG + wn, PG + wn + B), BK(1, 0, B), AF.Identity, bias=col(PB), scale=col(PS))
-            act(A("lf", wn, wn + B), BK(1, B, 2 * B))
-
-    def wb_counts(t):
-        wn = W0 + B * t
-        if t == RO - 1:
-            tt(A("xb"), IX(A("ynb", 0, wn), A("fdu", 0, 8)), A("nob"), OP.mult)
-            tt(IX(A("ynb", -B, wn), A("lw", 0, 8)), A("xb"), A("ohb"), OP.add)
-            tt(A("xb"), IX(A("ynb", 0, wn), A("fdu", 8, 16)), A("cap"), OP.min)
-            tt(IX(A("ynb", -B, wn), A("lw", 8, 16)), A("xb"), A("ohb"), OP.add)
-            return
-        tt(A("xa"), IX(A("kt", 0, wn), A("fdu", 0, 8)), A("up"), OP.min)
-        tt(IX(A("kt", -B, wn), A("lw", 0, 8)), A("xa"), A("lo"), OP.max)
-        tt(A("xa"), IX(A("kt", 0, wn), A("fdu", 8, 16)), A("cap"), OP.min)
-        tt(IX(A("kt", -B, wn), A("lw", 8, 16)), A("xa"), A("gro"), OP.add)
-
-    def wb_shift(t):
-        wn = W0 + B * t
-        if t == RO - 1:
-            return
-        act(A("wr"), xm, bias=(wn - MID) / 4096.0, scale=1.0 / 4096)
-        act(A("af"), IX(A("dt", 0, wn), A("fdu", 0, 8)))
-        act(A("zr"), IX(A("kt", 0, wn), A("fdu", 8, 16)), AF.Relu, scale=-1 / EPS)
-        mm([(BK(1, 384, 512), A("f32m", 0, 128), A("wr")), (BK(1, 384, 512), A("f32m", 128, 256), A("af"))])
-
-    def wb_shifted(t):
-        if t == RO - 1:
-            return
-        tt(A("dl"), BK(1, 384, 512), A("ohf"), OP.mult)
+        act(A("dt", wn, wn + B), IX(A("dt", 0, wn), l8))
+        act(A("g1"), IX(A("lf", 0, wn), l8))
+        ts(A("k16", 16, 24), A("cf", 0, 8), 4096.0, OP.mult)
         o = BK(7, 384, 512)
         mm([(o, A("f32m", 0, 128), A("af")), (o, A("f32m", 256, 384), A("dl"))])
-
-    def wb_reduce(t):
-        if t == RO - 1:
-            return
-        o = BK(7, 384, 512)
         act(A("ax"), o)
-        act(A("ar"), o, bias=MAGIC)
-        act(A("ar"), A("ar"), bias=-MAGIC)
+        if CFG["arv"]:
+            ts(A("ar"), o, MAGIC, OP.add, MAGIC, OP.subtract)
+        else:
+            act(A("ar"), o, bias=MAGIC)
+            act(A("ar"), A("ar"), bias=-MAGIC)
+        mm(spread("b0", 0, 8, A("k16", 16, 24)), False)
+        mm([(BK(0, B, 2 * B), M("mv"), A("g1"))])
+        act(A("dt", PG + wn, PG + wn + B), BK(0, 0, B), AF.Identity, bias=col(PB), scale=col(PS))
+        act(A("lf", wn, wn + B), BK(0, B, 2 * B))
+        tt(A("xa"), IX(A("kt", 0, wn), lf), A("up"), OP.min)
+        tt(IX(A("kt", -B, wn), A("lw", 0, 8)), A("xa"), A("lo"), OP.max)
+        tt(A("xa"), IX(A("kt", 0, wn), ld), A("cap"), OP.min)
+        tt(IX(A("kt", -B, wn), A("lw", 8, 16)), A("xa"), A("gro"), OP.add)
+        tt(IX(A("dt", -B, wn), A("lw", 0, 8)), A("ax"), A("ar"), OP.subtract)
 
-    def wb_pointers(t):
-        tt(IX(A("dt", -B, W0 + B * t), A("lw", 0, 8)), A("ax"), A("ar"), OP.subtract)
-
-    def counts_out(h):
-        n = (W - B) // 2
-        q = A("ynb", n * h, n * (h + 1))
-        act(q, A("kt", n * h, n * (h + 1)), bias=128.0 + 1.0 / 31, scale=1.0 / 31)
-        act(q, q, bias=-128.0)
-
-    def compares(x):
-        for p in PIECES[x]:
-            compare(p)
-
-    def pointers(t, x, marks, first=0):
-        for p in PIECES[x][first:]:
-            pointer(t, p)
-            if p == PIECES[x][-1]:
-                pointer_sum(x)
-            if marks:
-                marks0(p)
-
-    def marks(t, x):
-        if t < RO - 1:
-            for p in PIECES[x]:
-                marks1(p)
-
-    def count_out(t):
-        remote(A("nsi", 4 * t, 4 * t + 4), A("inc", 164, 168), "nar%d" % t, "nsn%d" % t)
-
-    def payload_out(t):
-        remote(landing(t), A("pw", 0, CAP), "arr%d" % t, "snt%d" % t)
-
-    def twos(c):
-        return [sum(c[k:k + 2], []) for k in range(0, len(c), 2)]
-
-    def scatters(t, ps):
-        for p in ps:
-            scatter(t, p)
-
-    def own_context(x):
-        tt(X("cw", x), TX(x, 0), X("cf", x), OP.mult)
-
-    def compares_late(t):
-        for p in PIECES["B"]:
-            mm([(BK(p), M("ntri"), P("kap", p))] + spread("b%d" % p, 0, 32, L("qq", p)))
-            act(BK(p), BK(p), AF.Sigmoid, bias=-16.0 * (BASE // 32 * 31 - 8), scale=16.0)
-
-    def gathers_late(t, x):
-        act(A("ag", 16 * CH[x][0], 16 * CH[x][1]), IX(A("dt", 0, PG + W0 + B * t), X("c2", x)))
-
-    def products_late(x):
-        for p in PIECES[x]:
-            tt(P("ds", p), BK(p), P("ag", p), OP.mult)
-        pointer_sum(x)
-
-    def drop_f():
-        tt(A(H[0]), A(H[0]), TX("A", 0, 8), OP.mult)
-        no_f()
-
-    places()
-    weave(chain((link_digits,), (escape_page,)), chain((lanes,), (link_selectors,)))
-    targets_list(0)
-    for k in range(2):
-        weave(chain((counts_table, k)), chain((pointer_table, k), (pointer_rest, k)))
-    weave(chain((counts_table, 2)), chain((counts_table, 3)))
-    pointer_table(2)
-    suffix_links(0, cp)
-    spare = chain((hop_constants,), (write_back_constants,))
-
-    def some(n):
-        out = [sum(spare[:n], [])]
-        del spare[:n]
-        return out
     for t in range(RO):
         last = t == RO - 1
-        s0, s1 = 2 * t, 2 * t + 1
-        if t == 0:
-            no_f()
-            pointer_rest(2)
-            counts(t, 0, "A")
-            pointer_table(3)
-            pointer_rest(3)
-            root_page()
-            suffix_links(1, act)
-            weave(chain((counts, t, 0, "B")), chain((targets, s0, "A"), (compares, "A")))
-        else:
-            weave(chain((counts, t, 0, "A"), (targets_list, s1)), chain((flags, t - 1, "B")))
-            link_context(t - 1, "B")
-            if last:
-                counts_out(0)
-            weave(chain((counts, t, 0, "B")), chain((targets, s0, "A"), (compares, "A")))
-            wb_pointers(t - 1)
-        weave(chain((page, "A"), (first_escape,)), some(6) + chain((targets, s0, "B"), (compares, "B"), (page, "B")))
-        if t == 0:
-            suffix_links_back()
-        weave(some(8))
-        pointers(t, "A", True)
-        weave(chain((pointers, t, "B", True)), [[]] + chain((context, "A", 1)))
-        if t == 0:
-            targets_list(s1)
-        weave(some(6))
-        weave(chain((counts, t, 1, "A")), twos(chain((context, "B", 1))))
-        no_f()
-        act(A("ka", 0, 8), A(H[0]), bias=-1.5)
-        act(A("ka", 8, 16), A("cf", 0, 8), bias=-0.5)
-        links(t, "A")
-        targets_list(s1 + 1)
-        links(t, "B")
-        weave(chain((counts, t, 1, "B")), chain((targets, s1, "A")))
-        weave(chain((page, "A"), (escapes, "A"), (marks, t, "A")), some(6) + chain((targets, s1, "B")))
-        weave(chain((page, "B"), (escapes, "B"), (marks, t, "B")), chain((slots, "A")))
-        weave(some(len(spare)))
-        if t == 0:
-            late_constants()
         if last:
-            counts_out(1)
-        sb = chain((slots, "B"), (count_out, t), (compares, "A"), (compares_late, t), (wb_onehot, t), (gathers_late, t, "B"))
-        ks = chain((first_escape,), (wb_keys, t))
-        weave(sb[:1], ks[:1])
-        weave(sb[1:], ks[1:6], chain((scatters, t, range(5)), (payload_out, t)))
-        weave(ks[6:], chain((pointers, t, "A", False)))
-        wb_shift(t)
-        wb_equal()
-        wb_shifted(t)
-        weave(chain((context, "A", 1), (wb_new, t), (wb_first, t), (wb_grow, t), (wb_new_rows, t)), chain((reading_list, t, "A")), [[]] + chain((reading_list, t, "B")))
-        if last:
-            wb_new_counts(t)
-            products_late("B")
-            wb_places()
-            weave(chain((wb_counts, t)), chain((own_context, "A"), (context, "B", 1), (own_context, "B")))
-            for h in range(2):
-                dma("y", (T.yn[:, W // 2 * h:W // 2 * (h + 1)], []), A("ynb", W // 2 * h, W // 2 * (h + 1)))
+            n = (W - B) // 6
+            for h in range(6):
+                q = A("ynb", n * h, n * (h + 1))
+                act(q, A("kt", n * h, n * (h + 1)), bias=128.0 + 1.0 / 31, scale=1.0 / 31)
+                if h in CFG["ynv"]:
+                    ts(q, q, 128.0, OP.subtract)
+                else:
+                    act(q, q, bias=-128.0)
+        for s in range(SP):
+            for x in "AB":
+                counts(t, s, x)
+                targets(SP * t + s, x)
+            if t + s > 0:
+                targets_list(SP * t + s + 1)
+            if s == 1:
+                act(A("ka", 0, 8), A(H[0]), bias=-1.5)
+                act(A("ka", 8, 16), A("cf", 0, 8), bias=-0.5)
+                slots(t, "A")
+                slots(t, "B")
+                send(t)
+            first_escape()
             for p in range(5):
-                receive(t, p, cp if p > 2 else act)
-                if p % 3 == 1:
-                    flags(t, "AB"[p // 3])
-            link_context(t, "A")
-            link_context(t, "B")
-        else:
-            for p in range(4):
-                receive(t, p, act)
-                if p == 1:
-                    wb_new_counts(t)
-            weave(chain((products_late, "B")), chain((own_context, "A"), (drop_f,), (wb_places,)))
-            wb_reduce(t)
-            wb_new_pages(t)
-            weave(chain((wb_counts, t)), [[], []] + chain((context, "B", 1)))
-            flags(t, "A")
-            receive(t, 4, cp)
-            weave(chain((link_context, t, "A")), chain((own_context, "B")))
-    dma("y", (T.yc[:, :], []), A("yo"))
+                compare(s, p)
+            if s == 1:
+                wb_first(t)
+            for x in "AB":
+                pointers(t, s, x)
+        write_back(t)
+        if last:
+            dma("y", HBM(T.yn[:, :]), A("ynb", 0, W))
+        ts(A("nsf"), A("nsi", 4 * t + 3, 4 * t + 4), 0.5, OP.subtract, CAP * SU, OP.min)
+        receive(t, "A")
+        receive(t, "B")
+    dma("y", HBM(T.yc[:, :]), A("yo"))
+
+    cnt, waited, got, bank = {}, {}, {}, {}
+
+    def need(q, sem, val):
+        if waited.get((q, sem), 0) < val:
+            E[q].wait_ge(T.sem[sem], val)
+            waited[(q, sem)] = val
+    if len(calls) not in ORDER:
+        ORDER[len(calls)] = in_order(calls)
+    for i in ORDER[len(calls)]:
+        q, pre, banks = calls[i][0], calls[i][3], calls[i][4]
+        sem, n, make = makes[i]
+        if make:
+            todo = {}
+            for k in pre + [bank[b] for b in banks if b in bank and calls[bank[b]][0] != q]:
+                if k not in calls[i][5]:
+                    todo[got[k][0]] = max(todo.get(got[k][0], 0), got[k][1])
+            for s in sorted(todo):
+                need(q, s, todo[s])
+            make(T.sem[sem])
+        cnt[sem] = cnt.get(sem, 0) + n
+        got[i] = (sem, cnt[sem])
+        bank.update({b: i for b in banks})
     for s in sorted(cnt):
         need("g", s, cnt[s])

@@ -8,29 +8,30 @@ W0, B, LN, RO, SP, CAP = 3072, 128, 2560, 4, 2, 768
 W = W0 + RO * B
 PG = 4096
 MID = 1792
+ESC = 1.0 - (MID - 0.5) / 4096
 BASE = 33024
 SU = 2.0 ** -14
 LOW = 512
 OWN = (RO - 1) * CAP
 CH = {"A": (0, 96), "B": (96, 160)}
 PIECES = {"A": (0, 1, 2), "B": (3, 4)}
-TB = {"A": "b5", "B": "b6"}
-CYCLE, PE_CYCLE, GATHER, SCATTER, WAKE, LOCAL, REMOTE = 0.83, 0.42, 1.3, 2.5, 250.0, (2000.0, 250.0), (3500.0, 50.0)
-CFG = dict(late=(1, 2, 3, 4), late0=(), shared=(2, 4), shared1=(2,), flagv="AB", recvv=(2, 4), lpv=(), turns=3, pefix=0.0, vfix=0.0, afix=100.0, cuts=(512, 1024, 1536, 2560), early=True, merge=False, mini=False, modv=(1, 3, 5, 7), rrow=300.0, riss=600.0, mid=0, soft=False, hyv=True, arv=False, ynv=(0, 2, 4), tries=40, amp=400.0)
+TB = {"A": ("b5", 0), "B": ("b6", 0)}
+CYCLE, PE_CYCLE, GATHER, SCATTER, WAKE, LOCAL, REMOTE = 0.83, 0.42, 1.3, 2.5, 250.0, (2000.0, 250.0), (3000.0, 60.0)
+CFG = dict(late=(1, 2, 3, 4), late0=(), shared=(2, 4), shared1=(2,), flagv="AB", recvv=(2, 4), lpv=(), turns=3, pefix=0.0, vfix=0.0, afix=100.0, cuts=(512, 1024, 1536, 2560), early=True, merge=False, mini=True, modv=(1, 3, 5, 7), rrow=300.0, riss=600.0, mid=0, soft=False, parts=False, ne1=False, ord=("AB", "AB", "AB", "AB", "AB"), hyv=True, arv=False, ynv=(0, 2, 4), tries=300, amp=300.0, near=12000.0)
 ORDER = {}
 
 _F, _H, _I, _B, _U = "float32", "float16", "int32", "bfloat16", "uint16"
-MATS = ["id", "nid", "blk", "ntri", "i14", "e15", "slt", "blks", "moh", "blkw", "blk2", "i31", "i512", "mv", "u1", "l1", "l2", "low", "slq"]
+MATS = ["id", "nid", "blk", "ntri", "i14", "e15", "slt", "blks", "moh", "blkw", "blk2", "i31", "i512", "mv", "u1", "l1", "l2", "low", "slq", "nslt"]
 SELS = ["selt", "vsel", "seln", "lsel", "nsel", "sel2", "sel3"]
 SCRATCH = {}
 for _n, _w, _d in (
         ("tb", W0, _I), ("kt", B + W, _F), ("dt", B + PG + W, _F), ("lf", W, _B), ("ynb", B + W, _B), ("ci", 1536, _I), ("rb", 768, _B),
-        ("dn", 384, _I), ("dg", 576, _I), ("dgb", 384, _B), ("lfd", 384, _B), ("fd", 192, _F), ("fl", 192, _U), ("c1k", W0 // 16, _F),
-        ("v8", 1280, _F), ("iop", 1, _I), ("pi", 2, _I), ("xf", 160, _B), ("xg", 128, _B), ("xr", 256, _B), ("pc", 32, _F), ("oh16", 16, _F), ("m31", 16, _F),
+        ("dn", 384, _I), ("dg", 384, _I), ("dgb", 384, _B), ("lfd", 384, _B), ("fd", 192, _F), ("fl", 192, _U), ("c1k", W0 // 16, _F),
+        ("v8", 640, _B), ("tk", 320, _F), ("iop", 1, _I), ("pi", 2, _I), ("xf", 160, _B), ("xg", 128, _B), ("xr", 256, _B), ("pc", 32, _F), ("oh16", 16, _F), ("m31", 16, _F),
         ("mats", 128 * len(MATS), _B), ("sels", 160 * len(SELS), _B), ("f32m", 640, _F), ("expa", 2048, _B), ("c32k", 96, _B),
         ("th0", 256, _B), ("th1", 256, _B), ("th2", 16, _F), ("th3", 16, _F), ("thr", 256, _B), ("jg", 640, _F), ("dj", 16, _F),
-        ("ca", 160, _I), ("cl", 160, _U), ("c2", 160, _U), ("cf", 160, _F), ("r32", 160, _H), ("qq", 160, _H), ("yy", 160, _F), ("rr", 160, _F),
-        ("es", 160, _B), ("inc", 168, _F), ("zer", 96, _F), ("sa", 160, _F), ("sl", 160, _U), ("rl", 160, _U),
+        ("ca", 160, _I), ("cl", 160, _U), ("c2", 160, _U), ("cf", 160, _F), ("r32", 160, _H), ("cq", 160, _F), ("r0", 160, _B), ("qq", 320, _H), ("yy", 160, _F), ("rr", 160, _F),
+        ("es", 160, _B), ("inc", 328, _F), ("zer", 192, _F), ("sl", 160, _U), ("rl", 160, _U),
         ("cw", 160, _F), ("yo", 160, _F), ("nsi", 4 * RO, _F), ("nsf", 1, _F),
         ("kap", LN, _H), ("ds", LN, _H), ("cd", LN, _B), ("ne", LN, _B), ("val", LN, _B), ("lg", LN, _B), ("ag", LN, _F),
         ("win", OWN + LN, _B), ("rb3", CAP + 16, _B), ("pw", LOW + W0 + LN, _B), ("jq", LOW // 16, _F),
@@ -87,9 +88,11 @@ def in_order(calls):
     best = there_and_back([-i for i in range(n)])
     for k in range(CFG["tries"]):
         way = [0.0] * n
+        amp, mid = CFG["amp"] * (1 + k % 3), best[0] * ((k * 0.618) % 1)
         for i in range(n - 1, -1, -1):
-            way[i] = max([best[2][i] + CFG["amp"] * math.sin((i + 1) * (k + 1) * 12.9898)] + [way[j] + 1.0 for j, gap in after[i]])
-        best = min(best, there_and_back(way), key=lambda b: b[0])
+            near = abs(best[1][i] - mid) < CFG["near"]
+            way[i] = max([best[2][i] + near * amp * math.sin((i + 1) * (k + 1) * 12.9898)] + [way[j] + 1.0 for j, gap in after[i]])
+        best = min(there_and_back(way), best, key=lambda b: b[0])
     CFG["span"] = best[0]
     loads = [i for i in range(n) if calls[i][0] in "ys" and not calls[i][3]]
     return loads + sorted(set(range(n)) - set(loads), key=lambda i: (best[1][i] - calls[i][1], i))
@@ -237,7 +240,7 @@ def rank_program(g, core, T, topo):
 
     def TX(x, k, m=None):
         n = CH[x][1] - CH[x][0]
-        return A(TB[x], n * k, n * k + (m or n))
+        return A(TB[x][0], TB[x][1] + n * k, TB[x][1] + n * k + (m or n))
 
     def P(name, p, base=0):
         return A(name, base + 512 * p, base + 512 * p + 512)
@@ -270,7 +273,9 @@ def rank_program(g, core, T, topo):
     fill(A("xg"), [[1, 8], [0, 16]], 0)
     fill(A("xr"), [[0, 16], [1, 16]], 0)
     fill(A("c32k"), [[0, 96]], BASE)
-    fill(A("zer"), [[0, 96]], 0)
+    fill(A("zer"), [[0, 192]], 0)
+    fill(A("v8"), [[0, 640]], 0)
+    fill(A("tk"), [[0, 320]], BASE)
     fill(A("c1k"), [[0, W0 // 16]], 1024)
     fill(A("lf", 0, W0), [[0, W0]], 0)
     fill(A("dt", W0, PG + W0), [[0, PG]], 0)
@@ -322,11 +327,12 @@ def rank_program(g, core, T, topo):
         ts(M(n), M("id"), k, OP.mult)
         tt(M(n), M(n), M("low"), OP.add)
         ts(M(n), M(n), 2.0 ** -37, OP.mult)
+    ts(M("nslt"), M("slt"), -1.0, OP.mult)
     ts(SEL("vsel"), A("xf"), col(T1), OP.is_equal)
     ts(SEL("selt"), A("xf"), col(P16), OP.is_equal)
     for n, k in (("sel2", oh(2)), ("sel3", oh(3)), ("lsel", col(LS)), ("seln", BASE / 16.0)):
         ts(SEL(n), SEL("selt"), k, OP.mult)
-    ts(SEL("nsel"), SEL("selt"), oh(0), OP.mult, -1.0 / 64, OP.mult)
+    ts(SEL("nsel"), SEL("lsel"), -1.0, OP.mult)
     ts(A("th0"), A("xr"), 0.0, OP.is_gt, 0.5, OP.mult)
     ts(A("th1"), A("xr"), 0.0, OP.is_equal, 2.0, OP.mult)
     scan(A("thr"), A("th0"), A("th1"), 0.0, OP.mult, OP.add)
@@ -334,6 +340,7 @@ def rank_program(g, core, T, topo):
     scan(A("th3"), A("th2"), A("zer", 0, 16), 0.0, OP.add, OP.add)
     ts(M("blkw"), M("blk"), A("th3", 15, 16), OP.mult, 0.5, OP.mult)
     ts(A("inc", 0, 8), A("zer", 0, 8), 0.5, OP.add)
+    act(A("tk"), A("tk"), bias=-127.5 / 8)
     ts(A("jg", 0, 160), A("xf"), 16 * SU, OP.mult, col(J0), OP.add)
     for t in range(1, RO):
         act(A("jg", 160 * t, 160 * t + 160), A("jg", 0, 160), bias=t * CAP * SU)
@@ -344,14 +351,13 @@ def rank_program(g, core, T, topo):
     def targets_list(st):
         if st < RO * SP:
             mm([(BK(7, 0, 160), SEL("vsel", r, slice(0, 8)), A("vr", st * LN + r, (st + 1) * LN, 16)) for r in range(16)])
-            act(A("v8", 160 * st, 160 * st + 160), BK(7, 0, 160), scale=0.125)
+            act(A("v8", 320 * (st % 2) + 1, 320 * (st % 2) + 320, 2), BK(7, 0, 160), scale=-0.125)
 
     cp(A("cl"), A("ca"))
     ts(A("cf"), A("ca"), float(MID), OP.subtract, 1.0 / 4096, OP.mult)
     targets_list(0)
-    ts(A("dg", 384, 576), A("dn", 192, 384), float(4096 - MID), OP.add)
-    ts(A("dg", 0, 192), A("dg", 384, 576), 63, OP.bitwise_and)
-    ts(A("dg", 192, 384), A("dg", 384, 576), 6, OP.arith_shift_right, 63, OP.bitwise_and)
+    ts(A("dg", 0, 192), A("dn", 192, 384), 63, OP.bitwise_and)
+    ts(A("dg", 192, 384), A("dn", 192, 384), 6, OP.arith_shift_right)
     ts(A("dgb"), A("dg", 0, 384), 1.0 / 64, OP.mult)
     dma("y", A("lf", 0, W0, rows=slice(2, 128, 16)), A("dgb", 0, 192), A("lf", 0, W0, rows=slice(3, 128, 16)), A("dgb", 192, 384))
     ts(A("fd"), A("dn", 0, 192), float(MID), OP.subtract, 1.0 / 4096, OP.mult)
@@ -408,8 +414,14 @@ def rank_program(g, core, T, topo):
                 mm([(BK(p), M("id"), P("ne", p))])
             act(P("ag", p), IX(A("kt", 0, W0 + B * t), L("cl", p)))
             tt(P("kap", p), BK(p), P("ag", p), OP.mult)
-        n = CH[x][1] - CH[x][0]
-        mm([(TX(x, 0), M("id"), A("c32k", 0, n))] + tolist(TX(x, 0), "selt", "kap", 16 * CH[x][0], 16 * CH[x][1]))
+        for lo, hi, o in parts(x, 0):
+            mm([(o, M("id"), A("c32k", 0, hi - lo))] + tolist(o, "selt", "kap", 16 * lo, 16 * hi))
+
+    def parts(x, k):
+        lo, hi = CH[x]
+        at = TB[x][1] + (hi - lo) * k - lo
+        step = 64 if CFG["parts"] else 96
+        return [(a, min(a + step, hi), A(TB[x][0], at + a, at + min(a + step, hi))) for a in range(lo, hi, step)]
 
     def two(first, rest):
         if CFG["early"]:
@@ -421,17 +433,18 @@ def rank_program(g, core, T, topo):
     def targets(st, x):
         s = TX(x, 0)
         ts(X("r32", x), s, 32.0 / 31, OP.mult, BASE - BASE * 32.0 / 31 + 8.25, OP.add)
-        tt(s, s, X("r32", x), OP.subtract)
-        tt(s, s, X("v8", x, 160 * st), OP.mult)
-        ts(X("qq", x), s, -1.0, OP.mult, BASE - 127.5 / 8, OP.add)
-        tt(s, X("qq", x), X("r32", x), OP.is_ge)
+        lo, hi = 2 * CH[x][0], 2 * CH[x][1]
+        tt(A("tk", lo, hi, 2), s, X("r32", x), OP.subtract)
+        scan(A("qq", lo, hi), A("v8", 320 * (st % 2) + lo, 320 * (st % 2) + hi), A("tk", lo, hi), 0.0, OP.mult, OP.add)
+        tt(s, A("qq", lo + 1, hi, 2), X("r32", x), OP.is_ge)
+        if st % 2:
+            ts(X("r0", x), X("cf", x), ESC - 1.0, OP.is_gt, 2.0 ** 23, OP.mult)
+            tt(X("es", x), s, X("r0", x), OP.mult)
         tt(X("yy", x), s, X("cf", x), OP.add)
         ts(X("c2", x), X("yy", x), 4096.0, OP.mult, float(MID), OP.add)
 
-    ESC = 1.0 - (MID - 0.5) / 4096
-
     def compare(s, p):
-        two([(BK(p), M("ntri"), P("kap", p))], spread("b%d" % p, 0, 32, L("qq", p)))
+        two([(BK(p), M("ntri"), P("kap", p))], spread("b%d" % p, 0, 32, A("qq", 64 * p + 1, 64 * p + 64, 2)))
         act(BK(p) if p in CFG["late" if s else "late0"] else P("cd", p), BK(p), AF.Sigmoid, bias=-16.0 * (BASE // 32 * 31 - 8), scale=16.0)
 
     def pointers(t, s, x):
@@ -445,7 +458,8 @@ def rank_program(g, core, T, topo):
             if s == 0:
                 two([(BK(p), M("i14"), P("kap", p))], [(BK(p), M("e15"), P("ds", p))])
                 act(BK(p) if p in CFG["shared1"] else P("ne", p), BK(p), AF.Sigmoid, bias=256.0 * (2.0 ** 23 - 0.5), scale=-256.0)
-        mm(tolist(TX(x, 1), "selt", "ds", 16 * CH[x][0], 16 * CH[x][1]))
+        for lo, hi, o in parts(x, 1):
+            mm(tolist(o, "selt", "ds", 16 * lo, 16 * hi))
         context(x, 1, "cl")
 
     def context(x, k, out):
@@ -467,19 +481,20 @@ def rank_program(g, core, T, topo):
 
     def slots(t, x):
         lo, hi = CH[x]
-        ts(X("es", x), X("yy", x), ESC, OP.is_gt, 2.0 ** 23, OP.mult)
-        mm([(TX(x, 3), M("blks"), X("es", x))])
-        mm([(TX(x, 2), M("slt"), X("es", x))])
-        scan(X("inc", x, 8), TX(x, 3), A("zer", 0, hi - lo), A("inc", 7 + lo, 8 + lo), OP.add, OP.add)
-        tt(X("sa", x), TX(x, 2), X("inc", x, 7), OP.add)
+        b, at = TB[x][0], TB[x][1] + 2 * (hi - lo)
+        even, odd = A(b, at, at + 2 * (hi - lo), 2), A(b, at + 1, at + 2 * (hi - lo), 2)
+        mm([(even, M("slt"), X("es", x))])
+        mm([(odd, M("blks"), X("es", x)), (odd, M("nslt"), X("es", x))])
+        scan(A("inc", 8 + 2 * lo, 8 + 2 * hi), TX(x, 2, 2 * (hi - lo)), A("zer", 0, 2 * (hi - lo)), A("inc", 7 + 2 * lo, 8 + 2 * lo), OP.add, OP.add)
         k = max(lo, LOW // 16)
-        o = A(TB[x], 3 * (hi - lo), 3 * (hi - lo) + hi - k)
-        tt(o, A("sa", k, hi), A("jg", 160 * (RO - 1) + k, 160 * (RO - 1) + hi), OP.min)
-        ts(A("sl", k, hi), o, 1 / SU, OP.mult)
+        if k < hi:
+            o = TX(x, 1, hi - k)
+            tt(o, A("inc", 8 + 2 * k, 8 + 2 * hi, 2), A("jg", 160 * (RO - 1) + k, 160 * (RO - 1) + hi), OP.min)
+            ts(A("sl", k, hi), o, 1 / SU, OP.mult)
         if lo == 0:
             o = BK(5, 5 * hi, 5 * hi + LOW // 16)
             mm([(o, M("slq"), A("es", 0, LOW // 16))])
-            tt(o, o, A("inc", 7, 7 + LOW // 16), OP.add)
+            tt(o, o, A("inc", 7, 7 + LOW // 8, 2), OP.add)
             tt(o, o, A("jq"), OP.max)
             ts(A("sl", 0, LOW // 16), o, 1.0 - LOW * SU, OP.subtract, 1 / SU, OP.mult)
         for p in PIECES[x]:
@@ -500,7 +515,7 @@ def rank_program(g, core, T, topo):
         remote(A("rb3" if t == RO - 1 else "win", at + lo, at + hi), A("pw", LOW + lo, LOW + hi), arr + str(t), snt + str(t))
 
     def send(t):
-        remote(A("nsi", 4 * t, 4 * t + 4), A("inc", 164, 168), "nar%d" % t, "nsn%d" % t)
+        remote(A("nsi", 4 * t, 4 * t + 4), A("inc", 324, 328), "nar%d" % t, "nsn%d" % t)
         cuts = CFG["cuts"]
         for lo, hi in zip(cuts, cuts[1:]):
             scatter(t, lo, hi)
@@ -515,24 +530,31 @@ def rank_program(g, core, T, topo):
     def receive(t, x):
         last = t == RO - 1
         lo, hi = 16 * CH[x][0], 16 * CH[x][1]
-        ts(TX(x, 0), X("sa", x), A("nsf"), OP.is_ge)
-        tt(TX(x, 2), TX(x, 0), X("sa", x), OP.add)
+        sa = A("inc", 8 + 2 * CH[x][0], 8 + 2 * CH[x][1], 2)
+        ts(TX(x, 0), sa, A("nsf"), OP.is_ge)
+        tt(TX(x, 2), TX(x, 0), sa, OP.add)
         if last:
             ts(X("rl", x), TX(x, 2), CAP * SU, OP.min, 1 / SU, OP.mult)
         else:
             tt(TX(x, 2), TX(x, 2), X("jg", x, 160 * t), OP.min)
             ts(X("rl", x), TX(x, 2), 1 / SU, OP.mult)
-        tt(X("cw", x), TX(x, 0), X("cf", x), OP.mult)
+        ts(X("cq", x), X("cf", x), MID / 4096.0, OP.add)
+        tt(X("cw", x), TX(x, 0), X("cq", x), OP.mult)
         if x == "A" and not last:
             tt(A(H[0]), A(H[0]), TX("A", 0, 8), OP.mult)
         for p in PIECES[x]:
             (cp if p in CFG["recvv"] or (last and p % 2 == 0) else act)(P("val", p), IX(A("rb3") if last else A("win", OWN - CAP * (t + 1), OWN + LN), L("rl", p)))
-        own = [(TX(x, 4), A("f32m", 0, 128), X("cw", x))]
-        mm(tolist(TX(x, 4), "lsel", "val", lo, hi) + (own if last else []), stop=last)
         if not last:
-            ts(A("ne", lo, hi), A("val", lo, hi), 1.0, OP.is_ge)
-            mm(own + tolist(TX(x, 4), "nsel", "ne", lo, hi), start=False)
-        context(x, 4, "yo" if last else "cl")
+            for p in PIECES[x]:
+                ts(P("ne", p), P("val", p), 1.0, OP.is_ge)
+        for a, b, o in parts(x, 4):
+            mm(tolist(o, "lsel", "val", 16 * a, 16 * b), stop=False)
+            mm([(o, A("f32m", 0, 128), A("cw", a, b))], start=False, stop=last)
+            if not last:
+                mm(tolist(o, "nsel", "ne", 16 * a, 16 * b), start=False)
+        ts(X("yo" if last else "cl", x), TX(x, 4), 4096.0, OP.mult)
+        if not last:
+            ts(X("cf", x), TX(x, 4), MID / 4096.0, OP.subtract)
 
     def wb_first(t):
         new, old = H
@@ -636,7 +658,7 @@ def rank_program(g, core, T, topo):
                 else:
                     act(q, q, bias=-128.0)
         for s in range(SP):
-            for x in "AB":
+            for x in CFG["ord"][s]:
                 counts(t, s, x)
                 targets(SP * t + s, x)
             if t + s > 0:
@@ -644,22 +666,22 @@ def rank_program(g, core, T, topo):
             if s == 1:
                 act(A("ka", 0, 8), A(H[0]), bias=-1.5)
                 act(A("ka", 8, 16), A("cf", 0, 8), bias=-0.5)
-                slots(t, "A")
-                slots(t, "B")
+                for x in CH:
+                    slots(t, x)
                 send(t)
             first_escape()
             for p in range(5):
                 compare(s, p)
             if s == 1:
                 wb_first(t)
-            for x in "AB":
+            for x in CFG["ord"][2 + s]:
                 pointers(t, s, x)
         write_back(t)
         if last:
             dma("y", HBM(T.yn[:, :]), A("ynb", 0, W))
         ts(A("nsf"), A("nsi", 4 * t + 3, 4 * t + 4), 0.5, OP.subtract, CAP * SU, OP.min)
-        receive(t, "A")
-        receive(t, "B")
+        for x in CFG["ord"][4]:
+            receive(t, x)
     dma("y", HBM(T.yc[:, :]), A("yo"))
 
     cnt, waited, got, bank = {}, {}, {}, {}

@@ -1,98 +1,143 @@
 import math
 from concourse.mybir import AluOpType as OP, ActivationFunctionType as AF
 
-EPS = 2.0 ** -14
+EPS = 2.0 ** -13
 MAGIC = 1.5 * 2.0 ** 23
 BIG = 1.5 * 2.0 ** 27
 W0, B, LN, RO, SP, CAP = 3072, 128, 2560, 4, 2, 768
 W = W0 + RO * B
+NK, NS = LN // 16, CAP // 16
 PG = 4096
 MID = 1792
 ESC = 1.0 - (MID - 0.5) / 4096
 BASE = 33024
-SU = 2.0 ** -14
-LOW = 512
+MARK = 256
+CEN = (LN + NK) // 2
+FAR = 8192.0
 OWN = (RO - 1) * CAP
+FREE = OWN + LN
 CH = {"A": (0, 96), "B": (96, 160)}
 PIECES = {"A": (0, 1, 2), "B": (3, 4)}
 TB = {"A": ("b5", 0), "B": ("b6", 0)}
+LKB = {"A": ("b7", 160), "B": ("b7", 256)}
+PBK = [0, 1, 2, 3, 4]
 CYCLE, PE_CYCLE, GATHER, SCATTER, WAKE, LOCAL, REMOTE = 0.83, 0.42, 1.3, 2.5, 250.0, (2000.0, 250.0), (3000.0, 60.0)
-CFG = dict(late=(1, 2, 3, 4), late0=(), shared=(2, 4), shared1=(2,), flagv="AB", recvv=(2, 4), lpv=(), turns=3, pefix=0.0, vfix=0.0, afix=100.0, cuts=(512, 1024, 1536, 2560), early=True, merge=False, mini=True, modv=(1, 3, 5, 7), rrow=300.0, riss=600.0, mid=0, soft=False, parts=False, ne1=False, ord=("AB", "AB", "AB", "AB", "AB"), hyv=True, arv=False, ynv=(0, 2, 4), tries=300, amp=300.0, near=12000.0)
+CFG = dict(late=(1, 2, 3, 4), late0=(), shared=(), shared1=(), first=(), recvv=(), payv=(), lpv=(), pefix=0.0, vfix=0.0, afix=100.0,
+           parts=(0, 384, 768), lparts=(0, 768), modv=(1, 3, 5, 7), rrow=300.0, riss=600.0,
+           hb=("b6", 336, "b6", 384, "b6", 432), sb=(3, 4), cqs=False, msgs=False, k16s=True, wbx="A", lgv=(), rrs=(), arv=False,
+           wb=(7, 0, 1, 0, 7), tl=(7, 0), eqg=4, wake=WAKE, linkat=1, split=False, tries=2500, amp=300.0, near=6000.0, shake=0.15, back=0.3, jump=800.0)
 ORDER = {}
 
 _F, _H, _I, _B, _U = "float32", "float16", "int32", "bfloat16", "uint16"
-MATS = ["id", "nid", "blk", "ntri", "i14", "e15", "slt", "blks", "moh", "blkw", "blk2", "i31", "i512", "mv", "u1", "l1", "l2", "low", "slq", "nslt"]
-SELS = ["selt", "vsel", "seln", "lsel", "nsel", "sel2", "sel3"]
+MATS = ["id", "nid", "blk", "ntri", "i13", "e15", "slt", "nslt", "moh", "blkw", "blk2", "i34", "i18", "i512", "u1", "l1", "low", "nb4", "omat", "r1", "nfar",
+        "p00", "p01", "p10", "p11"]
+SELS = ["selt", "seln", "sel0", "sel1", "selw"]
 SCRATCH = {}
 for _n, _w, _d in (
-        ("tb", W0, _I), ("kt", B + W, _F), ("dt", B + PG + W, _F), ("lf", W, _B), ("ynb", B + W, _B), ("ci", 1536, _I), ("rb", 768, _B),
-        ("dn", 384, _I), ("dg", 384, _I), ("dgb", 384, _B), ("lfd", 384, _B), ("fd", 192, _F), ("fl", 192, _U), ("c1k", W0 // 16, _F),
-        ("v8", 640, _B), ("tk", 320, _F), ("iop", 1, _I), ("pi", 2, _I), ("xf", 160, _B), ("xg", 128, _B), ("xr", 256, _B), ("pc", 32, _F), ("oh16", 16, _F), ("m31", 16, _F),
-        ("mats", 128 * len(MATS), _B), ("sels", 160 * len(SELS), _B), ("f32m", 640, _F), ("expa", 2048, _B), ("c32k", 96, _B),
-        ("th0", 256, _B), ("th1", 256, _B), ("th2", 16, _F), ("th3", 16, _F), ("thr", 256, _B), ("jg", 640, _F), ("dj", 16, _F),
-        ("ca", 160, _I), ("cl", 160, _U), ("c2", 160, _U), ("cf", 160, _F), ("r32", 160, _H), ("cq", 160, _F), ("r0", 160, _B), ("qq", 320, _H), ("yy", 160, _F), ("rr", 160, _F),
-        ("es", 160, _B), ("inc", 328, _F), ("zer", 192, _F), ("sl", 160, _U), ("rl", 160, _U),
-        ("cw", 160, _F), ("yo", 160, _F), ("nsi", 4 * RO, _F), ("nsf", 1, _F),
-        ("kap", LN, _H), ("ds", LN, _H), ("cd", LN, _B), ("ne", LN, _B), ("val", LN, _B), ("lg", LN, _B), ("ag", LN, _F),
-        ("win", OWN + LN, _B), ("rb3", CAP + 16, _B), ("pw", LOW + W0 + LN, _B), ("jq", LOW // 16, _F),
-        ("h0", 8, _F), ("h1", 8, _F), ("ht", 8, _F), ("hz", 8, _F), ("c8", 8, _U), ("d8", B, _H), ("e8", 8, _F), ("cnd", 8, _F), ("ka", 16, _F), ("k32", 16, _F), ("k16", 24, _H),
+        ("tb", W0, _I), ("kt", B + W, _F), ("dt", B + PG + W, _F), ("lf", W, _F), ("ynb", B + W, _B), ("ci", 1536, _I), ("cb", 1536, _B), ("rb", 768, _B),
+        ("dn", 384, _I), ("fh", 192, _H), ("ft", 192, _H), ("ld", 192, _F), ("fl", 192, _U), ("vd", 1280, _B), ("vt", 1280, _B),
+        ("v8", 640, _B), ("tk", 320, _F), ("iop", 1, _I), ("pi", 3, _I), ("xf", 160, _B), ("xg", 128, _B), ("xr", 256, _B), ("pc", 32, _F), ("oh16", 16, _F),
+        ("mats", 128 * len(MATS), _B), ("sels", 160 * len(SELS), _B), ("f32m", 768, _F), ("expa", 2048, _B), ("c32k", 96, _B),
+        ("th0", 256, _B), ("th1", 256, _B), ("th2", 16, _F), ("th3", 16, _F), ("thr", 256, _B), ("jg", 480, _F), ("dj", 16, _F),
+        ("ca", NK, _I), ("cl", NK, _U), ("c2", NK, _U), ("cf", NK, _F), ("r32", NK, _H), ("cq", NK, _F), ("r0", NK, _B), ("qq", 320, _H), ("yy", NK, _F),
+        ("rr", NK, _F), ("lk", 2 * NK, _F), ("r33", NK, _F), ("nsi", 4 * RO, _F), ("lg", LN, _H), ("es", NK, _B), ("inc", 328, _F), ("pat", 192, _F), ("zer", CAP, _B), ("rl", NK, _U), ("yo", NK, _F), ("nsf", 1, _F),
+        ("spr", NK, _F), ("ue", 2 * NK, _H), ("ol", 20, _U), ("kw", LN + NK, _B), ("kr2", CAP, _B), ("kl", NS, _U), ("k16b", NS, _B), ("mrow", CAP, _F),
+        ("oh", CAP, _B), ("lo16", CAP, _H), ("il", NS, _U), ("pay", CAP, _B), ("msg", NS, _H), ("mi", NS * RO, _H), ("sc", CAP, _F),
+        ("rcv", NK, _F), ("xs", NK, _F), ("gu", NK, _F),
+        ("kap", LN, _B), ("ds", LN, _H), ("cd", LN, _B), ("ne", LN, _B), ("ag", LN, _F), ("win", FREE + 16, _B),
+        ("h0", 8, _F), ("h1", 8, _F), ("ht", 8, _F), ("hz", 8, _F), ("c8", 8, _U), ("d8", B, _H), ("e8", 8, _F), ("cnd", 8, _F), ("ka", 16, _F), ("k32", 16, _F), ("k16", 16, _H),
         ("nc", 16, _H), ("fdu", 16, _U), ("fy", 16, _F), ("lw", 16, _U), ("eq", 16 * B, _B), ("kr", 256, _B),
-        ("ohb", B, _B), ("up", B, _F), ("lo", B, _F), ("cap", B, _F), ("gro", B, _F), ("zr", B, _B), ("hx", B, _B), ("hy", B, _F),
-        ("xa", B, _F), ("xb", B, _B), ("nob", B, _B), ("g1", B, _B), ("af", B, _F), ("wr", 3 * B, _F), ("dl", B, _F), ("ax", B, _F), ("ar", B, _F)):
+        ("ohb", B, _B), ("up", B, _F), ("lo", B, _F), ("cap", B, _F), ("gro", B, _F), ("zr", B, _B), ("z0", B, _B), ("hx", B, _B),
+        ("xa", B, _F), ("xb", B, _B), ("nob", B, _B), ("g1", B, _H), ("af", B, _F), ("wr", 3 * B, _F), ("dl", B, _F), ("ax", B, _F), ("ar", B, _F)):
     SCRATCH[_n] = ("sbuf", [128, _w], _d)
-SCRATCH["vr"] = ("sbuf", [8, RO * SP * LN], _B)
 for _k in range(8):
     SCRATCH["b%d" % _k] = ("psum", [128, 512], _F)
-SEMAPHORES = (["cv", "ct", "cs", "cg"] + ["ld%d" % k for k in range(20)]
-              + [n + str(k) for k in range(RO) for n in ("arr", "snt", "nar", "nsn", "har", "hsn", "mar", "msn")])
+SEMAPHORES = (["cv", "ct", "cs", "cg"] + ["ld%d" % k for k in range(16)]
+              + [n + str(k) + str(h) for k in range(RO) for n in ("arr", "snt") for h in range(4)])
 
 
 def in_order(calls):
-    n = len(calls)
-    before = [[(p, calls[p][2] - calls[p][1] + (0.0 if p in c[5] else WAKE)) for p in c[3]] for c in calls]
+    n, wake = len(calls), CFG["wake"]
+    tail = [c[2] - c[1] for c in calls]
+    before = [[(p, 0.0 if p in c[5] else tail[p] + wake) for p in c[3]] for c in calls]
     after = [[] for _ in range(n)]
     for i in range(n):
         for p, gap in before[i]:
             after[p].append((i, gap))
 
     def lay(order, needs):
-        end, held = [0.0] * n, {}
+        end, why, held = [0.0] * n, [None] * n, {r: [] for c in calls for r in [c[0]] + c[4]}
         for i in order:
-            q, busy, banks = calls[i][0], calls[i][1], calls[i][4]
-            t = max([end[p] + gap for p, gap in needs[i]], default=0.0)
+            q, d, banks, t, w = calls[i][0], calls[i][1], calls[i][4], 0.0, None
+            for p, gap in needs[i]:
+                if end[p] + gap > t:
+                    t, w = end[p] + gap, (p, False)
             moved = True
             while moved:
                 moved = False
-                for r in [q] + banks:
-                    pad = 0.0 if r == q else WAKE
-                    h = held.setdefault(r, [])
+                h = held[q]
+                at = len(h)
+                while at and h[at - 1][1] > t:
+                    at -= 1
+                while at < len(h) and h[at][0] < t + d:
+                    t, w = h[at][1], (h[at][3], True)
+                    at += 1
+                for r in banks:
+                    h = held[r]
                     k = len(h)
-                    while k and h[k - 1][0] > t - 9000.0:
+                    while k and h[k - 1][1] + wake > t:
                         k -= 1
-                    for a, b, who in h[k:]:
-                        if a - pad >= t + busy and a - pad > t:
-                            break
-                        if b + pad > t and (r == q or who != q):
-                            t, moved = b + pad, True
-            end[i] = t + busy
-            for r in [q] + banks:
-                held[r].append((t, t + busy, q))
-                held[r].sort()
-        return end
+                    while k < len(h) and h[k][0] - wake < t + d:
+                        if h[k][2] != q and h[k][1] + wake > t:
+                            t, moved, w = h[k][1] + wake, True, (h[k][3], True)
+                        k += 1
+            end[i], why[i] = t + d, w
+            held[q].insert(at, (t, t + d, q, i))
+            for r in banks:
+                h = held[r]
+                k = len(h)
+                while k and h[k - 1][0] > t:
+                    k -= 1
+                h.insert(k, (t, t + d, q, i))
+        return end, why
+
+    def forth(way):
+        end, why = lay(sorted(range(n), key=lambda i: (-way[i], i)), before)
+        return max(end[i] + tail[i] for i in range(n)), end, way, why
 
     def there_and_back(way):
-        end = lay(sorted(range(n), key=lambda i: (-way[i], i)), before)
-        way = lay(sorted(range(n), key=lambda i: (-end[i], -i)), after)
-        end = lay(sorted(range(n), key=lambda i: (-way[i], i)), before)
-        return max(end[i] + calls[i][2] - calls[i][1] for i in range(n)), end, way
+        end = forth(way)[1]
+        return forth(lay(sorted(range(n), key=lambda i: (-end[i], -i)), after)[0])
+
+    def chance(x):
+        return (math.sin(x * 12.9898) * 43758.5453) % 1
     best = there_and_back([-i for i in range(n)])
-    for k in range(CFG["tries"]):
-        way = [0.0] * n
-        amp, mid = CFG["amp"] * (1 + k % 3), best[0] * ((k * 0.618) % 1)
+    for k in range(1, CFG["tries"] + 1):
+        way, shake = list(best[2]), chance(k + 0.1) < CFG["shake"]
+        if shake:
+            amp, mid = CFG["amp"] * (1 + k % 3), best[0] * ((k * 0.618) % 1)
+            way = [way[i] + (amp * math.sin((i + 1) * (k + 1) * 12.9898) if abs(best[1][i] - mid) < CFG["near"] else 0.0) for i in range(n)]
+        else:
+            i, pairs = max(range(n), key=lambda i: best[1][i] + tail[i]), []
+            while best[3][i]:
+                if best[3][i][1]:
+                    pairs.append((i, best[3][i][0]))
+                i = best[3][i][0]
+            i, j = pairs[int(chance(k + 0.37) * len(pairs))]
+            jump = 10 + CFG["jump"] * chance(k + 0.71)
+            if chance(k + 0.53) < 0.5:
+                way[i] = max(way[i], way[j]) + jump
+            else:
+                way[j] = min(way[i], way[j]) - jump
+                for a in range(j, n):
+                    for p, gap in before[a]:
+                        if way[a] >= way[p]:
+                            way[a] = way[p] - 1.0
         for i in range(n - 1, -1, -1):
-            near = abs(best[1][i] - mid) < CFG["near"]
-            way[i] = max([best[2][i] + near * amp * math.sin((i + 1) * (k + 1) * 12.9898)] + [way[j] + 1.0 for j, gap in after[i]])
-        best = min(there_and_back(way), best, key=lambda b: b[0])
+            for j, gap in after[i]:
+                if way[j] + 1.0 > way[i]:
+                    way[i] = way[j] + 1.0
+        best = min((there_and_back if shake or chance(k + 0.91) < CFG["back"] else forth)(way), best, key=lambda b: b[0])
     CFG["span"] = best[0]
     loads = [i for i in range(n) if calls[i][0] in "ys" and not calls[i][3]]
     return loads + sorted(set(range(n)) - set(loads), key=lambda i: (best[1][i] - calls[i][1], i))
@@ -111,6 +156,7 @@ def rank_program(g, core, T, topo):
             hi = T[name].shape[1]
         elif name in ("kt", "dt", "ynb"):
             lo, hi = lo + B, hi + B
+        hi -= (hi - lo - 1) % step
         ap = T[name][slice(None) if rows is None else rows, lo:hi:step] if step > 1 else T[name][slice(None) if rows is None else rows, lo:hi]
         return (ap, (name, lo, hi), None, (hi - lo + step - 1) // step)
 
@@ -132,10 +178,7 @@ def rank_program(g, core, T, topo):
         rd = {x[1] for x in ins} | {x[2] for x in ins + outs if x[2]}
         wr = {x[1] for x in outs}
         me, pre = len(calls), set(also)
-        for name, lo, hi in rd:
-            pre |= {i for l, h, i in writes.get(name, []) if l < hi and lo < h}
-        raw = set(pre)
-        for name, lo, hi in wr:
+        for name, lo, hi in rd | wr:
             pre |= {i for l, h, i in writes.get(name, []) if l < hi and lo < h}
         for name, lo, hi in wr:
             pre |= {i for l, h, i in reads.get(name, []) if l < hi and lo < h}
@@ -149,7 +192,7 @@ def rank_program(g, core, T, topo):
         if q == "t":
             pre |= {lastpe[b] for b in banks if b in lastpe}
             lastpe.update({b: me for b in banks})
-        free = {i for i in pre if calls[i][0] == q and (q == "t" or (CFG["soft"] and busy == took and calls[i][1] == calls[i][2] and i not in raw))}
+        free = {i for i in pre if calls[i][0] == q == "t"}
         calls.append((q, busy, took, sorted(pre), banks, free))
         makes.append(make)
         return me
@@ -173,12 +216,17 @@ def rank_program(g, core, T, topo):
     dst = T.cores[(rank + 1) % len(T.cores)]
     src = T.cores[(rank - 1) % len(T.cores)]
 
-    def remote(out, in_, arr, snt):
+    wire = []
+
+    def remote(out, in_, tag):
         rid, pid, _se = topo.addr(dst)
         ns = CFG["rrow"] + 128 * in_[3] * size(in_) / REMOTE[1]
-        me = call("g", CFG["riss"], REMOTE[0], (snt, len(topo.engines(core, dst)),
-                                                lambda sem: g.remote_dma(out[0], in_[0], T.sem[arr], sem, pid, rid, topo.mask(core, dst))), [in_], [])
-        call("r", ns, ns, (arr, len(topo.engines(src, core)), None), [], [out], [me])
+        me = call("g", CFG["riss"], REMOTE[0], ("snt" + tag, len(topo.engines(core, dst)),
+                                                lambda sem: g.remote_dma(out[0], in_[0], T.sem["arr" + tag], sem, pid, rid, topo.mask(core, dst))), [in_], [])
+        calls[me] = calls[me][:3] + (sorted(set(calls[me][3]) | set(wire[:1])), [], set(wire[:1]))
+        land = call("r", ns, ns, ("arr" + tag, len(topo.engines(src, core)), None), [], [out], [me] + wire[1:])
+        calls[land] = calls[land][:5] + (set(wire[1:]),)
+        wire[:] = [me, land]
 
     def ap(x):
         return x[0] if isinstance(x, tuple) else x
@@ -203,6 +251,9 @@ def rank_program(g, core, T, topo):
     def cp(out, a):
         op("v", vec(out, [a], half(out, a)), lambda: V.tensor_copy(out[0], a[0]), [a], [out])
 
+    def turn(out, a):
+        op("v", vec(out, [a], half(out, a)), lambda: V.transpose(out[0], a[0]), [a], [out])
+
     def scan(out, a, b, init, o0, o1):
         op("v", vec(out, [a], half(out, a, b)), lambda: V.tensor_tensor_scan(out[0], a[0], b[0], ap(init), o0, o1), [a, b, init], [out])
 
@@ -213,10 +264,18 @@ def rank_program(g, core, T, topo):
         op("s", CFG["afix"] + out[3] * CYCLE * (GATHER if a[2] else 1.0), lambda: S.activation(out[0], a[0], func, bias=ap(bias), scale=ap(scale)),
            [a, bias, scale], [out])
 
-    def mm(items, group=True, start=True, stop=True):
+    def lin(on_s, out, a, scale, bias):
+        if on_s:
+            act(out, a, bias=bias, scale=scale)
+        else:
+            ts(out, a, scale, OP.mult, bias, OP.add)
+
+    def mm(items, group=0, start=True, stop=True):
+        k = group or len(items)
+
         def f():
             for i, (o, l, r) in enumerate(items):
-                x = PE.matmul(o[0], l[0], r[0], (start and i == 0) or not group, (stop and i == len(items) - 1) or not group)
+                x = PE.matmul(o[0], l[0], r[0], start and i % k == 0, stop and i % k == k - 1)
             return x
         op("t", sum(max(64, r[3]) * (4 if size(r) == 4 else 1) for o, l, r in items) * PE_CYCLE + CFG["pefix"] * len(items), f,
            [x for it in items for x in it[1:]], [it[0] for it in items])
@@ -225,9 +284,12 @@ def rank_program(g, core, T, topo):
         i = MATS.index(n)
         return A("mats", 128 * i, 128 * i + 128)
 
-    def SEL(n, r=None, rows=None):
+    def F32(i):
+        return A("f32m", 128 * i, 128 * i + 128)
+
+    def SEL(n, r=None):
         i = 160 * SELS.index(n)
-        return A("sels", i, i + 160) if r is None else A("sels", i + 16 - r, i + 144 - r, rows=rows)
+        return A("sels", i, i + 160) if r is None else A("sels", i + 16 - r, i + 144 - r)
 
     def tolist(out, sel, name, lo, hi):
         return [(out, SEL(sel, r), A(name, lo + r, hi, 16)) for r in range(16)]
@@ -237,6 +299,9 @@ def rank_program(g, core, T, topo):
 
     def X(name, x, base=0):
         return A(name, base + CH[x][0], base + CH[x][1])
+
+    def X2(name, x, base=0):
+        return A(name, base + 2 * CH[x][0], base + 2 * CH[x][1], 2)
 
     def TX(x, k, m=None):
         n = CH[x][1] - CH[x][0]
@@ -251,15 +316,18 @@ def rank_program(g, core, T, topo):
     def BK(p, lo=0, hi=512):
         return A("b%d" % p, lo, hi)
 
+    def HB(k, lo, hi):
+        return A(CFG["hb"][2 * k], CFG["hb"][2 * k + 1] + lo, CFG["hb"][2 * k + 1] + hi)
+
     for k in range(4):
         dma("y", A("tb", 768 * k, 768 * k + 768), HBM(T.tab[:, 768 * k:768 * k + 768]))
         if k == 0:
             dma("y", A("dn", 0, 192), HBM(T.suf[:, :]), A("dn", 192, 384), HBM(T.lnk[:, :]))
         if k == 1:
-            dma("y", A("ca"), HBM(T.cx[:, :]), A("vr", 0, SP * LN), HBM(T.vv[:, 0:SP * LN]))
-    dma("y", A("vr", SP * LN, RO * SP * LN), HBM(T.vv[:, SP * LN:RO * SP * LN]))
+            dma("y", A("ca"), HBM(T.cx[:, :]))
+    dma("y", A("vd"), HBM(T.vv[:, :]))
 
-    PGC, PRC, PFC, P16, PM1, PP1, N15, N0, T1, C15, PS, PB, LS, R23, PM2, PM15, J0, R0, R192 = range(19)
+    PGC, PRC, PAR, PFC, P16, PM1, PP1, N15, N0, C15, PS, PB, PM15, J0, R0, R192, NPAR, PP16, PM16, LB = range(20)
 
     def col(i):
         return A("pc", i, i + 1)
@@ -269,204 +337,203 @@ def rank_program(g, core, T, topo):
     xm = A("xf", 0, 128)
     fill(A("iop"), [[1, 1]], 0, 1)
     fill(col(PFC), [[1, 1]], 0, 1)
-    fill(A("xf"), [[1, 160]], 0)
+    fill(A("xf"), [[1, NK]], 0)
     fill(A("xg"), [[1, 8], [0, 16]], 0)
     fill(A("xr"), [[0, 16], [1, 16]], 0)
+    fill(A("lf", 0, W0), [[1, W0]], -MID)
     fill(A("c32k"), [[0, 96]], BASE)
-    fill(A("zer"), [[0, 192]], 0)
     fill(A("v8"), [[0, 640]], 0)
     fill(A("tk"), [[0, 320]], BASE)
-    fill(A("c1k"), [[0, W0 // 16]], 1024)
-    fill(A("lf", 0, W0), [[0, W0]], 0)
-    fill(A("dt", W0, PG + W0), [[0, PG]], 0)
+    fill(A("dt", W0, PG), [[0, PG - W0]], 0)
     fill(A("h0"), [[0, 8]], 0)
-    fill(A("rb3", CAP, CAP + 16), [[0, 16]], 0)
-    fill(A("pw", LOW, LOW + CAP), [[0, CAP]], 0)
+    fill(A("zer"), [[0, CAP]], 0)
+    fill(A("lk"), [[0, 2 * NK]], 0)
+    fill(A("pat"), [[0, 96], [-2 * int(FAR), 2]], int(FAR))
+    fill(A("inc", 0, 8), [[0, 8]], -CEN)
+    fill(A("spr"), [[1, NK]], LN - CEN)
+    fill(A("mrow"), [[1, CAP]], -CEN)
+    fill(A("win", FREE, FREE + 16), [[0, 16]], -1)
 
     ts(A("pi", 0, 1), A("iop"), 4, OP.arith_shift_right)
     ts(A("pi", 1, 2), A("iop"), 15, OP.bitwise_and)
-    cp(A("pc", PGC, PRC + 1), A("pi"))
-    ts(col(T1), col(PFC), 16.0, OP.mult, 16.0, OP.add)
-    for i, k in ((PP1, 1.0), (PM15, -15.0), (PM1, -1.0), (PM2, -2.0)):
+    ts(A("pi", 2, 3), A("iop"), 4, OP.arith_shift_right, 1, OP.bitwise_and)
+    cp(A("pc", PGC, PAR + 1), A("pi"))
+    for i, k in ((PP1, 1.0), (PM15, -15.0), (PM1, -1.0), (PP16, 16.0), (PM16, -16.0)):
         ts(col(i), col(PFC), k, OP.add)
     ts(A("oh16"), A("xf", 0, 16), col(PRC), OP.is_equal)
-    ts(A("m31"), A("oh16"), 31.0 / 32, OP.mult)
     ts(col(P16), col(PGC), 16.0, OP.mult, 16.0, OP.add)
-    ts(col(N15), oh(15), -1.0, OP.mult, 1.0, OP.add)
-    ts(col(N0), oh(0), -1.0, OP.mult, 1.0, OP.add)
+    for i, c in ((N15, oh(15)), (N0, oh(0)), (NPAR, col(PAR))):
+        ts(col(i), c, -1.0, OP.mult, 1.0, OP.add)
     ts(col(C15), oh(15), 1.0 / 65536, OP.mult)
     ts(col(R0), oh(0), -BIG / 65536, OP.mult)
     ts(col(R192), col(R0), 192.0, OP.add)
-    ts(col(J0), col(PRC), float(CAP), OP.add, SU, OP.mult)
-    ts(col(LS), oh(0), 1.0 / 64, OP.mult, oh(1), OP.add)
-    ts(col(R23), oh(2), oh(3), OP.add)
-    ts(col(PS), oh(0), 32.0 / 31 / 4096, OP.mult)
-    ts(col(PB), oh(15), 1024.0, OP.mult)
+    ts(col(J0), col(PRC), CAP - CEN + FAR, OP.add)
+    ts(col(PS), oh(0), 1.0 / 4096, OP.mult, oh(1), OP.add)
+    ts(col(PB), oh(15), float(MARK), OP.mult)
+    ts(col(LB), col(PRC), -256.0, OP.mult, -128.0, OP.add)
     ts(M("id"), xm, col(PFC), OP.is_equal)
     ts(M("blk"), A("xg"), col(PGC), OP.is_equal)
-    ts(M("low"), A("xr", 0, 128), col(PRC), OP.is_gt)
+    act(M("low"), A("xr", 0, 128), AF.Sigmoid, bias=col(LB), scale=256.0)
     tt(M("low"), M("low"), M("blk"), OP.mult)
     ts(M("u1"), xm, col(PP1), OP.is_equal, col(N15), OP.mult)
     ts(M("l1"), xm, col(PM1), OP.is_equal, col(N0), OP.mult)
-    ts(M("l2"), xm, col(PM2), OP.is_equal)
-    ts(A("f32m", 512, 640), xm, col(PM15), OP.is_equal, col(C15), OP.mult)
+    for n, c, m in (("p00", PFC, NPAR), ("p11", PFC, PAR), ("p01", PP16, NPAR), ("p10", PM16, PAR)):
+        ts(M(n), xm, col(c), OP.is_equal, col(m), OP.mult)
+    ts(F32(4), xm, col(PM15), OP.is_equal, col(C15), OP.mult)
     for r in range(16):
-        act(A("expa", 128 * r, 128 * r + 128), M("blk"), scale=A("m31", r, r + 1))
-    cp(A("f32m", 0, 128), M("id"))
-    tt(A("f32m", 256, 384), M("id"), M("u1"), OP.subtract)
-    for n, a, k in (("nid", M("id"), -1.0), ("ntri", M("low"), -1.0), ("i14", M("id"), 2.0 ** 14), ("i31", M("id"), 31.0), ("i512", M("id"), 512.0),
-                    ("blk2", M("blk"), 2.0), ("blks", M("blk"), 2.0 ** -37)):
+        act(A("expa", 128 * r, 128 * r + 128), M("blk"), scale=oh(r))
+    cp(F32(0), M("id"))
+    tt(F32(2), M("id"), M("u1"), OP.subtract)
+    for n, a, k in (("nid", M("id"), -1.0), ("ntri", M("low"), -15.0 / 16), ("i13", M("id"), 1 / EPS), ("i34", M("id"), 34.0), ("i18", M("id"), 18.0),
+                    ("i512", M("id"), 512.0), ("blk2", M("blk"), 2.0), ("nb4", M("blk"), -FAR / 2), ("omat", M("blk"), 1.5), ("slt", M("id"), -FAR),
+                    ("nfar", M("id"), -FAR), ("r1", M("id"), oh(1))):
         ts(M(n), a, k, OP.mult)
-    ts(A("f32m", 384, 512), A("f32m", 256, 384), 1.0 / 65536, OP.mult)
-    tt(A("f32m", 128, 256), M("ntri"), M("id"), OP.subtract)
-    ts(M("e15"), M("blk"), oh(15), OP.mult, 2.0 ** 13, OP.mult)
+    ts(F32(3), F32(2), 1.0 / 65536, OP.mult)
+    tt(F32(1), M("nid"), M("low"), OP.subtract)
+    ts(F32(5), M("id"), oh(0), OP.mult, 4096.0, OP.mult)
+    ts(M("e15"), M("blk"), oh(15), OP.mult, 2.0 ** 23 / MARK, OP.mult)
     tt(M("moh"), M("id"), M("l1"), OP.subtract)
-    tt(M("l2"), M("l2"), M("id"), OP.add)
-    ts(M("mv"), M("l2"), col(R23), OP.mult)
-    for n, k in (("slt", -2.0 ** 13), ("slq", 2.0 ** 13)):
-        ts(M(n), M("id"), k, OP.mult)
-        tt(M(n), M(n), M("low"), OP.add)
-        ts(M(n), M(n), 2.0 ** -37, OP.mult)
+    tt(M("omat"), M("omat"), M("id"), OP.subtract)
+    tt(M("slt"), M("slt"), M("low"), OP.add)
     ts(M("nslt"), M("slt"), -1.0, OP.mult)
-    ts(SEL("vsel"), A("xf"), col(T1), OP.is_equal)
     ts(SEL("selt"), A("xf"), col(P16), OP.is_equal)
-    for n, k in (("sel2", oh(2)), ("sel3", oh(3)), ("lsel", col(LS)), ("seln", BASE / 16.0)):
+    for n, k in (("sel0", oh(0)), ("sel1", oh(1)), ("selw", col(PRC)), ("seln", BASE / 16.0)):
         ts(SEL(n), SEL("selt"), k, OP.mult)
-    ts(SEL("nsel"), SEL("lsel"), -1.0, OP.mult)
     ts(A("th0"), A("xr"), 0.0, OP.is_gt, 0.5, OP.mult)
     ts(A("th1"), A("xr"), 0.0, OP.is_equal, 2.0, OP.mult)
     scan(A("thr"), A("th0"), A("th1"), 0.0, OP.mult, OP.add)
     tt(A("th2"), A("thr", 0, 16), A("oh16"), OP.mult)
     scan(A("th3"), A("th2"), A("zer", 0, 16), 0.0, OP.add, OP.add)
     ts(M("blkw"), M("blk"), A("th3", 15, 16), OP.mult, 0.5, OP.mult)
-    ts(A("inc", 0, 8), A("zer", 0, 8), 0.5, OP.add)
     act(A("tk"), A("tk"), bias=-127.5 / 8)
-    ts(A("jg", 0, 160), A("xf"), 16 * SU, OP.mult, col(J0), OP.add)
-    for t in range(1, RO):
-        act(A("jg", 160 * t, 160 * t + 160), A("jg", 0, 160), bias=t * CAP * SU)
-    act(A("jq"), A("jg", 0, LOW // 16), bias=1.0 - (LOW + CAP) * SU)
+    ts(A("jg", 0, NK), A("xf"), 16.0, OP.mult, col(J0), OP.add)
+    for t in range(1, RO - 1):
+        act(A("jg", NK * t, NK * t + NK), A("jg", 0, NK), bias=float(t * CAP))
     for h in range(2):
-        act(A("dj", 8 * h, 8 * h + 8), A("jg", 0, 8), bias=float(-B - MID - CAP), scale=1 / SU)
+        act(A("dj", 8 * h, 8 * h + 8), A("jg", 0, 8), bias=CEN - CAP - FAR - B - MID)
+
+    def unturn(out, lo, step, name, at, n):
+        return [(A(out, lo + h, lo + h + step[0] * n, step[0]), M("p%d%d" % (h, e)), A(name, at + 16 * e, at + 16 * e + step[1] * (n - 1) + 1, step[1]))
+                for h in range(2) for e in range(2)]
 
     def targets_list(st):
         if st < RO * SP:
-            mm([(BK(7, 0, 160), SEL("vsel", r, slice(0, 8)), A("vr", st * LN + r, (st + 1) * LN, 16)) for r in range(16)])
-            act(A("v8", 320 * (st % 2) + 1, 320 * (st % 2) + 320, 2), BK(7, 0, 160), scale=-0.125)
+            b, at = CFG["tl"]
+            mm(unturn("b%d" % b, at, (2, 32), "vt", 2 * st, 40) + unturn("b%d" % b, at + 80, (2, 32), "vt", 2 * st + 1, 40), 2)
+            act(A("v8", 320 * (st % 2) + 1, 320 * (st % 2) + 320, 2), BK(b, at, at + NK), scale=1.0 / 16)
 
     cp(A("cl"), A("ca"))
     ts(A("cf"), A("ca"), float(MID), OP.subtract, 1.0 / 4096, OP.mult)
+    turn(A("vt"), A("vd"))
     targets_list(0)
-    ts(A("dg", 0, 192), A("dn", 192, 384), 63, OP.bitwise_and)
-    ts(A("dg", 192, 384), A("dn", 192, 384), 6, OP.arith_shift_right)
-    ts(A("dgb"), A("dg", 0, 384), 1.0 / 64, OP.mult)
-    dma("y", A("lf", 0, W0, rows=slice(2, 128, 16)), A("dgb", 0, 192), A("lf", 0, W0, rows=slice(3, 128, 16)), A("dgb", 192, 384))
-    ts(A("fd"), A("dn", 0, 192), float(MID), OP.subtract, 1.0 / 4096, OP.mult)
-    dma("y", A("dt", PG, PG + W0, rows=slice(0, 128, 16)), A("fd"), A("dt", PG, PG + W0, rows=slice(15, 128, 16)), A("c1k"))
+    ts(A("ld"), A("dn", 192, 384), float(MID), OP.subtract)
+    dma("y", A("lf", 0, W0, rows=slice(1, 128, 16)), A("ld"))
+    ts(A("fh"), A("dn", 0, 192), float(MID), OP.subtract)
+    turn(A("ft"), A("fh"))
+    mm([it for b in range(6) for it in unturn("b7", 256 + 2 * b, (12, 1), "ft", 32 * b, 16)], 2)
+    ts(A("fl"), BK(7, 256, 448), float(MID), OP.add)
+    for h in range(4):
+        o, w = A("dt", PG + 768 * h, PG + 768 * h + 768), IX(A("lf", 0, W0), A("fl", 48 * h, 48 * h + 48))
+        if h in CFG["lpv"]:
+            ts(o, w, col(PS), OP.mult, col(PB), OP.add)
+        else:
+            act(o, w, AF.Identity, bias=col(PB), scale=col(PS))
 
     def counts_table(k):
-        c = A("ci", 768 * (k % 2), 768 * (k % 2) + 768)
-        q = A("kt", 768 * k, 768 * k + 768)
+        c, b = A("ci", 768 * (k % 2), 768 * (k % 2) + 768), A("cb", 768 * (k % 2), 768 * (k % 2) + 768)
         ts(c, A("tb", 768 * k, 768 * k + 768), 15, OP.bitwise_and)
-        ts(q, c, 31.0, OP.mult, 1.0, OP.max)
-        act(q, q, bias=-1.0 - EPS)
+        ts(b, c, 34.0, OP.mult, -542.0625, OP.add)
+        act(A("kt", 768 * k, 768 * k + 768), b, bias=544.0 - EPS)
 
     def pointer_table(k):
         o = 768 * (k % 2)
         ts(A("ag", o, o + 768), A("tb", 768 * k, 768 * k + 768), 7.5 + 16 * MID, OP.subtract, BIG, OP.add)
         if k == 0:
-            mm([(BK(1, 0, 1), A("f32m", 512, 640), A("ag", 0, 1))])
+            mm([(BK(1, 0, 1), F32(4), A("ag", 0, 1))])
             act(A("dt", PG, PG + 1), BK(1, 0, 1), AF.Identity, bias=col(R0))
         for h in range(2):
             s, rb, bk = A("ag", o + 384 * h, o + 384 * h + 384), A("rb", 384 * h, 384 * h + 384), BK(4 - 4 * h, 0, 384)
-            mm([(BK(2 + h, 0, 384), A("f32m", 384, 512), s)])
+            mm([(BK(2 + h, 0, 384), F32(3), s)])
             if 2 * k + h in CFG["modv"]:
                 r = A("ag", 1536 + 384 * h, 1920 + 384 * h)
                 ts(r, BK(2 + h, 0, 384), MAGIC, OP.add, MAGIC, OP.subtract)
                 tt(A("dt", 768 * k + 384 * h, 768 * k + 384 * h + 384), BK(2 + h, 0, 384), r, OP.subtract)
                 continue
             act(rb, BK(2 + h, 0, 384), AF.Identity, bias=col(R192))
-            mm([(bk, A("f32m", 384, 512), s)], stop=False)
+            mm([(bk, F32(3), s)], stop=False)
             mm([(bk, M("nid"), rb)], start=False)
             act(A("dt", 768 * k + 384 * h, 768 * k + 384 * h + 384), bk, AF.Identity, bias=col(R192))
     for f, k in ((counts_table, 0), (pointer_table, 0), (counts_table, 1), (pointer_table, 1), (counts_table, 2), (counts_table, 3),
                  (pointer_table, 2), (pointer_table, 3)):
         f(k)
-    cp(A("fl"), A("dn", 0, 192))
-    for h in range(4):
-        (cp if h // 2 in CFG["lpv"] else act)(A("pw", LN + 768 * h, LN + 768 * h + 768), IX(A("lf", 0, W0), A("fl", 48 * h, 48 * h + 48)))
     targets_list(1)
-    for k, n in enumerate(("sel2", "sel3")):
-        mm(tolist(BK(7, 192 * k, 192 * k + 192), n, "pw", LN, LN + W0))
-    act(A("lfd"), BK(7, 0, 384))
-    dma("y", A("lf", 0, W0, rows=slice(0, 128, 16)), A("lfd", 0, 192), A("lf", 0, W0, rows=slice(1, 128, 16)), A("lfd", 192, 384))
+
+    KAP = (("kap", 0), ("win", OWN))
 
     def counts(t, s, x):
-        shared = [p for p in PIECES[x] if t + s > 0 and p in CFG["shared1" if s else "shared"]]
-        own = [p for p in PIECES[x] if p not in shared]
-        for lo, hi in ([(own[0], own[-1] + 1)] if CFG["merge"] else [(p, p + 1) for p in own]):
-            kw = IX(A("kt", 0, W0 + B * t), A("cl", 32 * lo, 32 * hi))
+        name, at = KAP[s]
+        for p in PIECES[x]:
+            kw = IX(A("kt", 0, W0 + B * t), L("cl", p))
             if t + s == 0:
-                cp(A("kap", 512 * lo, 512 * hi), kw)
+                (act if p in CFG["first"] else cp)(P(name, p, at), kw)
+            elif p in CFG["shared1" if s else "shared"]:
+                if s == 0:
+                    mm([(BK(PBK[p]), M("id"), P("ne", p))])
+                act(P("ag", p), kw)
+                tt(P(name, p, at), BK(PBK[p]), P("ag", p), OP.mult)
             else:
-                tt(A("kap", 512 * lo, 512 * hi), kw, A("ne", 512 * lo, 512 * hi), OP.mult)
-        for p in shared:
-            if s == 0:
-                mm([(BK(p), M("id"), P("ne", p))])
-            act(P("ag", p), IX(A("kt", 0, W0 + B * t), L("cl", p)))
-            tt(P("kap", p), BK(p), P("ag", p), OP.mult)
+                tt(P(name, p, at), kw, P("ne", p), OP.mult)
         for lo, hi, o in parts(x, 0):
-            mm([(o, M("id"), A("c32k", 0, hi - lo))] + tolist(o, "selt", "kap", 16 * lo, 16 * hi))
+            two([(o, M("id"), A("c32k", 0, hi - lo))], tolist(o, "selt", name, at + 16 * lo, at + 16 * hi))
 
     def parts(x, k):
         lo, hi = CH[x]
+        cuts = (lo, hi - 32, hi) if CFG["split"] and hi - lo > 64 else (lo, hi)
         at = TB[x][1] + (hi - lo) * k - lo
-        step = 64 if CFG["parts"] else 96
-        return [(a, min(a + step, hi), A(TB[x][0], at + a, at + min(a + step, hi))) for a in range(lo, hi, step)]
+        return [(a, b, A(TB[x][0], at + a, at + b)) for a, b in zip(cuts, cuts[1:])]
 
     def two(first, rest):
-        if CFG["early"]:
-            mm(first, stop=False)
-            mm(rest, start=False)
-        else:
-            mm(first + rest)
+        mm(first, stop=False)
+        mm(rest, start=False)
 
     def targets(st, x):
         s = TX(x, 0)
-        ts(X("r32", x), s, 32.0 / 31, OP.mult, BASE - BASE * 32.0 / 31 + 8.25, OP.add)
+        lin(x in CFG["rrs"], X("r32", x), s, 16.0 / 17, BASE - (BASE + 16) * 16.0 / 17)
         lo, hi = 2 * CH[x][0], 2 * CH[x][1]
         tt(A("tk", lo, hi, 2), s, X("r32", x), OP.subtract)
         scan(A("qq", lo, hi), A("v8", 320 * (st % 2) + lo, 320 * (st % 2) + hi), A("tk", lo, hi), 0.0, OP.mult, OP.add)
-        tt(s, A("qq", lo + 1, hi, 2), X("r32", x), OP.is_ge)
         if st % 2:
-            ts(X("r0", x), X("cf", x), ESC - 1.0, OP.is_gt, 2.0 ** 23, OP.mult)
-            tt(X("es", x), s, X("r0", x), OP.mult)
+            ts(X("r0", x), X("cf", x), ESC - 1.0, OP.is_lt, 2 * FAR, OP.mult)
+            tt(X("r33", x), X("r32", x), X("r0", x), OP.add)
+            tt(X("es", x), A("qq", lo + 1, hi, 2), X("r33", x), OP.is_ge)
+        tt(s, A("qq", lo + 1, hi, 2), X("r32", x), OP.is_ge)
         tt(X("yy", x), s, X("cf", x), OP.add)
         ts(X("c2", x), X("yy", x), 4096.0, OP.mult, float(MID), OP.add)
 
     def compare(s, p):
-        two([(BK(p), M("ntri"), P("kap", p))], spread("b%d" % p, 0, 32, A("qq", 64 * p + 1, 64 * p + 64, 2)))
-        act(BK(p) if p in CFG["late" if s else "late0"] else P("cd", p), BK(p), AF.Sigmoid, bias=-16.0 * (BASE // 32 * 31 - 8), scale=16.0)
+        bk = BK(PBK[p])
+        two([(bk, M("ntri"), P(KAP[s][0], p, KAP[s][1]))], spread("b%d" % PBK[p], 0, 32, A("qq", 64 * p + 1, 64 * p + 64, 2)))
+        act(bk if p in CFG["late" if s else "late0"] else P("cd", p), bk, AF.Sigmoid, bias=-64.0 * (BASE - 29), scale=64.0)
 
     def pointers(t, s, x):
         for p in PIECES[x]:
-            dw = IX(A("dt", 0, PG + W0 + B * t), L("c2", p))
+            dw, bk = IX(A("dt", 0, PG + W0 + B * t), L("c2", p)), BK(PBK[p])
             if p in CFG["late" if s else "late0"]:
                 act(P("ag", p), dw)
-                tt(P("ds", p), BK(p), P("ag", p), OP.mult)
+                tt(P("ds", p), bk, P("ag", p), OP.mult)
             else:
                 tt(P("ds", p), dw, P("cd", p), OP.mult)
             if s == 0:
-                two([(BK(p), M("i14"), P("kap", p))], [(BK(p), M("e15"), P("ds", p))])
-                act(BK(p) if p in CFG["shared1"] else P("ne", p), BK(p), AF.Sigmoid, bias=256.0 * (2.0 ** 23 - 0.5), scale=-256.0)
+                two([(bk, M("i13"), P("kap", p))], [(bk, M("e15"), P("ds", p))])
+                act(bk if p in CFG["shared1"] else P("ne", p), bk, AF.Sigmoid, bias=256.0 * (2.0 ** 23 - 0.5), scale=-256.0)
         for lo, hi, o in parts(x, 1):
             mm(tolist(o, "selt", "ds", 16 * lo, 16 * hi))
-        context(x, 1, "cl")
-
-    def context(x, k, out):
-        s = TX(x, k)
-        ts(X("rr", x), s, MAGIC, OP.add, MAGIC, OP.subtract)
-        tt(X("cf", x), s, X("rr", x), OP.subtract)
-        ts(X(out, x), X("cf", x), 4096.0, OP.mult, float(MID), OP.add)
+        ts(X("rr", x), TX(x, 1), MAGIC, OP.add, MAGIC, OP.subtract)
+        tt(X("cf", x), TX(x, 1), X("rr", x), OP.subtract)
+        if s == 0:
+            ts(X("cl", x), X("cf", x), 4096.0, OP.mult, float(MID), OP.add)
+        elif x == "A" and t < RO - 1:
+            ts(A("c8"), A("cf", 0, 8), 4096.0, OP.mult, float(MID), OP.add)
 
     H = ["h0", "h1"]
 
@@ -481,113 +548,126 @@ def rank_program(g, core, T, topo):
 
     def slots(t, x):
         lo, hi = CH[x]
-        b, at = TB[x][0], TB[x][1] + 2 * (hi - lo)
-        even, odd = A(b, at, at + 2 * (hi - lo), 2), A(b, at + 1, at + 2 * (hi - lo), 2)
+        n = hi - lo
+        b, at = TB[x][0], TB[x][1] + 2 * n
+        even, odd = A(b, at, at + 2 * n, 2), A(b, at + 1, at + 2 * n, 2)
         mm([(even, M("slt"), X("es", x))])
-        mm([(odd, M("blks"), X("es", x)), (odd, M("nslt"), X("es", x))])
-        scan(A("inc", 8 + 2 * lo, 8 + 2 * hi), TX(x, 2, 2 * (hi - lo)), A("zer", 0, 2 * (hi - lo)), A("inc", 7 + 2 * lo, 8 + 2 * lo), OP.add, OP.add)
-        k = max(lo, LOW // 16)
-        if k < hi:
-            o = TX(x, 1, hi - k)
-            tt(o, A("inc", 8 + 2 * k, 8 + 2 * hi, 2), A("jg", 160 * (RO - 1) + k, 160 * (RO - 1) + hi), OP.min)
-            ts(A("sl", k, hi), o, 1 / SU, OP.mult)
-        if lo == 0:
-            o = BK(5, 5 * hi, 5 * hi + LOW // 16)
-            mm([(o, M("slq"), A("es", 0, LOW // 16))])
-            tt(o, o, A("inc", 7, 7 + LOW // 8, 2), OP.add)
-            tt(o, o, A("jq"), OP.max)
-            ts(A("sl", 0, LOW // 16), o, 1.0 - LOW * SU, OP.subtract, 1 / SU, OP.mult)
-        for p in PIECES[x]:
-            act(P("lg", p), IX(A("lf", 0, W0 + B * t), L("cl", p)))
-            if t < RO - 1:
-                two([(BK(p), M("i14"), P("kap", p))], spread("b%d" % p, 0, 32, L("es", p)))
-                act(P("win", p, OWN), BK(p), AF.Sigmoid, bias=256.0 * (31 * 2.0 ** 18 - 0.5), scale=-256.0)
-
-    def scatter(t, lo, hi):
-        o = IX(A("pw", 0, LOW + hi) if lo < LOW else A("pw", LOW, LOW + W0 + LN), A("sl", lo // 16, hi // 16))
-        if t < RO - 1:
-            tt(o, A("lg", lo, hi), A("win", OWN + lo, OWN + hi), OP.add)
-        else:
-            cp(o, A("lg", lo, hi))
-
-    def payload_out(t, lo, hi, arr, snt):
-        at = 0 if t == RO - 1 else OWN - CAP * (t + 1)
-        remote(A("rb3" if t == RO - 1 else "win", at + lo, at + hi), A("pw", LOW + lo, LOW + hi), arr + str(t), snt + str(t))
+        mm([(odd, M("blk"), X("es", x)), (odd, M("nslt"), X("es", x))])
+        two([(TX(x, 4), F32(0), X("spr", x))], [(TX(x, 4), M("nb4"), X("es", x))])
+        scan(A("inc", 8 + 2 * lo, 8 + 2 * hi), TX(x, 2, 2 * n), A("pat", 0, 2 * n), A("inc", 7 + 2 * lo, 8 + 2 * lo), OP.add, OP.add)
+        tt(A("ue", 2 * lo, 2 * lo + n), TX(x, 4), X2("inc", x, 7), OP.max)
+        ts(A("ue", 2 * lo + n, 2 * hi), X2("inc", x, 9), float(CAP - CEN), OP.min, -1.0, OP.add)
+        o = TX(x, 5, n // 8)
+        mm(tolist(o, "sel0", "ue", 2 * lo, 2 * hi))
+        ts(A("ol", lo // 8, hi // 8), o, float(CEN), OP.add)
+        cp(IX(A("kw"), A("ol", lo // 8, lo // 8 + n // 16)), X("xf", x))
 
     def send(t):
-        remote(A("nsi", 4 * t, 4 * t + 4), A("inc", 324, 328), "nar%d" % t, "nsn%d" % t)
-        cuts = CFG["cuts"]
+        last = t == RO - 1
+        scan(A("kr2"), A("kw", 0, CAP), A("zer"), 0.0, OP.max, OP.add)
+        mm(tolist(HB(0, 0, NS), "sel0", "kr2", 0, CAP))
+        ts(A("kl"), HB(0, 0, NS), 2.0, OP.mult)
+        if not last:
+            lin(CFG["k16s"], A("k16b"), HB(0, 0, NS), 16.0, 0.0)
+        cuts = CFG["parts"]
         for lo, hi in zip(cuts, cuts[1:]):
-            scatter(t, lo, hi)
-        payload_out(t, LOW, CAP, "har", "hsn")
-        mid = CFG["mid"]
-        if mid:
-            scatter(t, mid, LOW)
-            payload_out(t, mid, LOW, "mar", "msn")
-        scatter(t, 0, mid or LOW)
-        payload_out(t, 0, mid or LOW, "arr", "snt")
+            tt(A("oh", lo, hi), IX(A("inc", 8, 328), A("kl", lo // 16, hi // 16)), A("mrow", lo, hi), OP.is_equal)
+        for h, (lo, hi) in enumerate(zip(cuts + (0,), cuts[1:] + (0,))):
+            if h == min(CFG["linkat"], len(cuts) - 1):
+                send_links(t)
+            if not last and hi:
+                o = HB(2, lo // 16, hi // 16)
+                two([(o, M("id"), A("k16b", lo // 16, hi // 16))], tolist(o, "selw", "oh", lo, hi))
+                cp(A("il", lo // 16, hi // 16), o)
+                (cp if h in CFG["payv"] else act)(A("pay", lo, hi), IX(A("win", OWN, OWN + LN), A("il", lo // 16, hi // 16)))
+                at = OWN - CAP * (t + 1)
+                remote(A("win", at + lo, at + hi), A("pay", lo, hi), "%d%d" % (t, h))
+
+    def send_links(t):
+        cuts = CFG["lparts"]
+        for lo, hi in zip(cuts, cuts[1:]):
+            tt(A("lo16", lo, hi), IX(A("lk"), A("kl", lo // 16, hi // 16)), A("oh", lo, hi), OP.mult)
+        mm(tolist(HB(1, 0, NS), "selt", "lo16", 0, CAP))
+        lin(CFG["msgs"], A("msg"), HB(1, 0, NS), 1 / FAR, 0.0)
+        remote(A("mi", NS * t, NS * t + NS), A("msg"), "%d3" % t)
+
+    def own_links(t, x):
+        for p in PIECES[x]:
+            (cp if p in CFG["lgv"] else act)(P("lg", p), IX(A("dt", PG, PG + W0 + B * t), L("cl", p)))
+        o = A(LKB[x][0], LKB[x][1], LKB[x][1] + CH[x][1] - CH[x][0])
+        mm(tolist(o, "sel1", "lg", 16 * CH[x][0], 16 * CH[x][1]))
+        act(X2("lk", x), o)
+
+    def links_in(t):
+        for h in range(2):
+            lo, hi, bk = 384 * h, 384 * h + 384, CFG["sb"][h]
+            two([(BK(bk, 0, 384), M("omat"), A("oh", lo, hi))], spread("b%d" % bk, 0, 24, A("mi", NS * t + 24 * h, NS * t + 24 * h + 24)))
+            scan(A("sc", lo, hi), A("oh", lo, hi), BK(bk, 0, 384), A("sc", lo - 1, lo) if h else 0.0, OP.max, OP.min)
+        ts(A("nsf"), A("nsi", 4 * t + 3, 4 * t + 4), 0.5, OP.subtract, float(CAP - CEN), OP.min)
 
     def receive(t, x):
         last = t == RO - 1
-        lo, hi = 16 * CH[x][0], 16 * CH[x][1]
-        sa = A("inc", 8 + 2 * CH[x][0], 8 + 2 * CH[x][1], 2)
-        ts(TX(x, 0), sa, A("nsf"), OP.is_ge)
-        tt(TX(x, 2), TX(x, 0), sa, OP.add)
-        if last:
-            ts(X("rl", x), TX(x, 2), CAP * SU, OP.min, 1 / SU, OP.mult)
-        else:
-            tt(TX(x, 2), TX(x, 2), X("jg", x, 160 * t), OP.min)
-            ts(X("rl", x), TX(x, 2), 1 / SU, OP.mult)
-        ts(X("cq", x), X("cf", x), MID / 4096.0, OP.add)
-        tt(X("cw", x), TX(x, 0), X("cq", x), OP.mult)
+        lo, hi = CH[x]
+        sa = X2("inc", x, 8)
+        ts(TX(x, 0), sa, A("nsf"), OP.is_ge, FAR, OP.mult)
+        ts(X("rcv", x), sa, A("nsf"), OP.is_lt)
+        if not last:
+            two([(TX(x, 4), F32(0), X("jg", x, NK * t))], [(TX(x, 4), M("nfar"), X("es", x))])
+            tt(X("xs", x), TX(x, 0), sa, OP.add)
+            tt(TX(x, 4), TX(x, 4), X("xs", x), OP.min)
+            ts(X("rl", x), TX(x, 4), float(CAP * (t + 1) + LN - CEN), OP.min, float(CEN), OP.add)
+        lin(CFG["cqs"], X("cq", x), X("cf", x), 0.5 / FAR, 0.5 / FAR)
+        tt(TX(x, 2), TX(x, 0), X("cq", x), OP.mult)
         if x == "A" and not last:
-            tt(A(H[0]), A(H[0]), TX("A", 0, 8), OP.mult)
-        for p in PIECES[x]:
-            (cp if p in CFG["recvv"] or (last and p % 2 == 0) else act)(P("val", p), IX(A("rb3") if last else A("win", OWN - CAP * (t + 1), OWN + LN), L("rl", p)))
+            tt(A(H[0]), A(H[0]), TX("A", 0, 8), OP.min)
+        tt(X("gu", x), IX(A("sc"), A("ol", lo // 8 + (hi - lo) // 16, hi // 8)), X("rcv", x), OP.mult)
+        tt(TX(x, 2), TX(x, 2), X("gu", x), OP.add)
+        ts(X("yo" if last else "cl", x), TX(x, 2), FAR, OP.mult, MID - FAR / 2, OP.add)
         if not last:
+            lin(CFG["cqs"], X("cf", x), TX(x, 2), 2.0, -1.0)
             for p in PIECES[x]:
-                ts(P("ne", p), P("val", p), 1.0, OP.is_ge)
-        for a, b, o in parts(x, 4):
-            mm(tolist(o, "lsel", "val", 16 * a, 16 * b), stop=False)
-            mm([(o, A("f32m", 0, 128), A("cw", a, b))], start=False, stop=last)
-            if not last:
-                mm(tolist(o, "nsel", "ne", 16 * a, 16 * b), start=False)
-        ts(X("yo" if last else "cl", x), TX(x, 4), 4096.0, OP.mult)
-        if not last:
-            ts(X("cf", x), TX(x, 4), MID / 4096.0, OP.subtract)
+                w = IX(A("win", OWN - CAP * (t + 1), FREE + 16), L("rl", p))
+                if p in CFG["recvv"]:
+                    ts(P("ne", p), w, 0.0, OP.is_lt)
+                else:
+                    act(P("ne", p), w, AF.Sigmoid, bias=-128.0, scale=-256.0 / EPS)
 
     def wb_first(t):
         new, old = H
         tt(A("cnd"), A(old), A(new), OP.is_gt)
         tt(A("ka", 0, 8), A("ka", 0, 8), A("cnd"), OP.mult)
         tt(A("ka", 8, 16), A("ka", 8, 16), A("cnd"), OP.mult)
-        ts(A("k16", 0, 16), A("ka"), 4096.0, OP.mult, 2048.0, OP.add)
-        mm(spread("b7", 0, 16, A("k16", 0, 16)), False)
-        ts(A("k32"), A("k16", 0, 16), 31.0 / 32, OP.mult)
-        ts(A("fdu"), A("k16", 0, 16), float(MID), OP.add, float(W0 + B * t - 1), OP.min)
-        ts(A("nc"), A("k16", 0, 16), 2048.0, OP.is_equal, 4.0, OP.mult)
-        mm([(BK(0, 0, 256), M("nid"), A("thr"))] + spread("b0", 0, 16, A("nc")), stop=False)
+        ts(A("k16"), A("ka"), 4096.0, OP.mult, 2048.0, OP.add)
+        wa, wb = CFG["wb"][:2]
+        mm(spread("b%d" % wa, 0, 16, A("k16")), 1)
+        lin(CFG["cqs"], A("k32"), A("ka"), 4096.0, 2048.0)
+        ts(A("fdu"), A("k16"), float(MID), OP.add, float(W0 + B * t - 1), OP.min)
+        ts(A("nc"), A("k16"), 2048.0, OP.is_equal, 4.0, OP.mult)
+        mm([(BK(wb, 0, 256), M("nid"), A("thr"))] + spread("b%d" % wb, 0, 16, A("nc")), stop=False)
+        it = []
         for k in range(2):
-            it = []
             for p in range(8):
                 e, o = B * (8 * k + p) + 16 * p, B * k + 16 * p
-                ts(A("eq", e, e + B - 16 * p), BK(7, o, B * k + B), A("k32", 8 * k + p, 8 * k + p + 1), OP.is_equal)
-                it.append((BK(0, o, o + 16), M("blkw"), A("eq", e, e + 16)))
+                ts(A("eq", e, e + B - 16 * p), BK(wa, o, B * k + B), A("k32", 8 * k + p, 8 * k + p + 1), OP.is_equal)
+                it.append((BK(wb, o, o + 16), M("blkw"), A("eq", e, e + 16)))
                 if p < 7:
-                    it.append((BK(0, o + 16, B * k + B), M("blk2"), A("eq", e + 16, e + B - 16 * p)))
-            mm(it, start=False, stop=k == 1)
-        act(A("kr"), BK(0, 0, 256), AF.Sigmoid, scale=-2.0 ** 23)
-        o = BK(0, 256, 272)
-        mm([(o, M("nid"), A("c32k", 0, 16)), (o, M("id"), A("k16", 0, 16))] + tolist(o, "seln", "kr", 0, 256))
+                    it.append((BK(wb, o + 16, B * k + B), M("blk2"), A("eq", e + 16, e + B - 16 * p)))
+                if (p + 1) % CFG["eqg"] == 0:
+                    mm(it, start=False, stop=k == 1 and p == 7)
+                    it = []
+        act(A("kr"), BK(wb, 0, 256), AF.Sigmoid, scale=-2.0 ** 23)
+        o = BK(wb, 256, 272)
+        mm([(o, M("nid"), A("c32k", 0, 16)), (o, M("id"), A("k16"))] + tolist(o, "seln", "kr", 0, 256))
         tt(A("fy"), o, A("dj"), OP.max)
         ts(A("lw"), A("fy"), float(MID + B), OP.add)
 
     def write_back(t):
         wn = W0 + B * t
-        l8, lf, ld = A("cl", 0, 8), A("fdu", 0, 8), A("fdu", 8, 16)
-        o = BK(1, 0, B)
-        if t == RO - 1 and CFG["mini"]:
-            l8, o, s = A("c8"), BK(7, 256, 384), BK(7, 384, 392)
+        l8, lf, ld = A("c8"), A("fdu", 0, 8), A("fdu", 8, 16)
+        wc, wd, we = CFG["wb"][2:]
+        o = BK(wc, 0, B)
+        if t == RO - 1:
+            o, s = BK(we, 256, 384), BK(we, 384, 392)
             tt(A("d8"), IX(A("dt", 0, PG + wn), A("c2", 0, 8)), A("cd", 0, B), OP.mult)
             mm(tolist(s, "selt", "d8", 0, B))
             ts(A("ht"), s, MAGIC, OP.add, MAGIC, OP.subtract)
@@ -606,40 +686,36 @@ def rank_program(g, core, T, topo):
             tt(A("xb"), IX(A("ynb", 0, wn), ld), A("cap"), OP.min)
             tt(IX(A("ynb", -B, wn), A("lw", 8, 16)), A("xb"), A("ohb"), OP.add)
             return
-        act(A("up"), o, bias=1024.0, scale=30.0 - 1024.0)
-        act(A("lo"), o, bias=-1.0, scale=31.0)
-        act(A("cap"), o, bias=1024.0, scale=433.0 - 1024.0)
+        act(A("up"), A("ohb"), bias=1024.0, scale=36.0 - 1024.0)
+        act(A("lo"), A("ohb"), bias=-1.0, scale=37.0)
+        act(A("cap"), A("ohb"), bias=1024.0, scale=478.0 - 1024.0)
         wr = A("wr", B * t, B * t + B)
         act(wr, xm, bias=(wn - MID) / 4096.0, scale=1.0 / 4096)
         act(A("af"), IX(A("dt", 0, wn), lf))
-        mm([(BK(1, 384, 512), A("f32m", 0, 128), wr), (BK(1, 384, 512), A("f32m", 128, 256), A("af"))])
-        tt(A("dl"), BK(1, 384, 512), A("ohb"), OP.mult)
+        mm([(BK(wc, 384, 512), F32(0), wr), (BK(wc, 384, 512), F32(1), A("af"))])
+        tt(A("dl"), BK(wc, 384, 512), A("ohb"), OP.mult)
         act(A("zr"), IX(A("kt", 0, wn), ld), AF.Relu, scale=-1 / EPS)
-        mm([(o, M("i31"), A("ohb")), (o, M("nid"), A("zr"))])
-        act(A("gro"), o, AF.Relu)
-        act(A("hx"), IX(A("kt", 0, wn), l8), bias=128.25 + 1.0 / 62, scale=1.0 / 62)
-        o = BK(1, 2 * B, 3 * B)
-        mm([(o, M("i31"), A("hx")), (o, M("i512"), A("kr", 0, B))])
-        if CFG["hyv"]:
-            ts(A("kt", wn, wn + B), o, 3969.0 + 512.0, OP.subtract, -EPS, OP.max)
-        else:
-            act(A("hy"), o, AF.Relu, bias=-3969.0 - 512.0)
-            act(A("kt", wn, wn + B), A("hy"), bias=-EPS)
+        mm([(o, M("i18"), A("ohb")), (o, M("id"), A("zr"))])
+        act(A("gro"), o, AF.Relu, bias=-2.0, scale=2.0)
+        act(A("hx"), IX(A("kt", 0, wn), l8), bias=128.25 - 1.0 / 34, scale=1.0 / 68)
+        act(A("z0"), IX(A("kt", 0, wn), l8), AF.Relu, scale=-4 / EPS)
+        o = BK(wc, 2 * B, 3 * B)
+        mm([(o, M("i34"), A("hx")), (o, M("nid"), A("z0")), (o, M("i512"), A("kr", 0, B))])
+        ts(A("kt", wn, wn + B), o, 34.0 * 128 - 2 + 512, OP.subtract, -EPS, OP.max)
         act(A("dt", wn, wn + B), IX(A("dt", 0, wn), l8))
+        act(A("dt", PG + wn, PG + wn + B), IX(A("lf", 0, wn), l8), AF.Identity, bias=col(PB), scale=col(PS))
         act(A("g1"), IX(A("lf", 0, wn), l8))
-        ts(A("k16", 16, 24), A("cf", 0, 8), 4096.0, OP.mult)
-        o = BK(7, 384, 512)
-        mm([(o, A("f32m", 0, 128), A("af")), (o, A("f32m", 256, 384), A("dl"))])
+        o = BK(wd, B, 2 * B)
+        two([(o, F32(5), wr)], [(o, M("r1"), A("g1"))])
+        act(A("lf", wn, wn + B), o)
+        o = BK(we, 384, 512)
+        mm([(o, F32(0), A("af")), (o, F32(2), A("dl"))])
         act(A("ax"), o)
         if CFG["arv"]:
             ts(A("ar"), o, MAGIC, OP.add, MAGIC, OP.subtract)
         else:
             act(A("ar"), o, bias=MAGIC)
             act(A("ar"), A("ar"), bias=-MAGIC)
-        mm(spread("b0", 0, 8, A("k16", 16, 24)), False)
-        mm([(BK(0, B, 2 * B), M("mv"), A("g1"))])
-        act(A("dt", PG + wn, PG + wn + B), BK(0, 0, B), AF.Identity, bias=col(PB), scale=col(PS))
-        act(A("lf", wn, wn + B), BK(0, B, 2 * B))
         tt(A("xa"), IX(A("kt", 0, wn), lf), A("up"), OP.min)
         tt(IX(A("kt", -B, wn), A("lw", 0, 8)), A("xa"), A("lo"), OP.max)
         tt(A("xa"), IX(A("kt", 0, wn), ld), A("cap"), OP.min)
@@ -648,17 +724,13 @@ def rank_program(g, core, T, topo):
 
     for t in range(RO):
         last = t == RO - 1
+        fill(A("kw", 0, CAP), [[0, CAP]], 0)
         if last:
             n = (W - B) // 6
             for h in range(6):
-                q = A("ynb", n * h, n * (h + 1))
-                act(q, A("kt", n * h, n * (h + 1)), bias=128.0 + 1.0 / 31, scale=1.0 / 31)
-                if h in CFG["ynv"]:
-                    ts(q, q, 128.0, OP.subtract)
-                else:
-                    act(q, q, bias=-128.0)
+                act(A("ynb", n * h, n * (h + 1)), A("kt", n * h, n * (h + 1)), AF.Relu, bias=-1.0 / 17, scale=1.0 / 34)
         for s in range(SP):
-            for x in CFG["ord"][s]:
+            for x in CH:
                 counts(t, s, x)
                 targets(SP * t + s, x)
             if t + s > 0:
@@ -667,20 +739,22 @@ def rank_program(g, core, T, topo):
                 act(A("ka", 0, 8), A(H[0]), bias=-1.5)
                 act(A("ka", 8, 16), A("cf", 0, 8), bias=-0.5)
                 for x in CH:
+                    own_links(t, x)
                     slots(t, x)
+                remote(A("nsi", 4 * t, 4 * t + 4), A("inc", 324, 328), "%d2" % t)
                 send(t)
             first_escape()
-            for p in range(5):
-                compare(s, p)
-            if s == 1:
-                wb_first(t)
-            for x in CFG["ord"][2 + s]:
+            for x in CH:
+                for p in PIECES[x]:
+                    compare(s, p)
                 pointers(t, s, x)
+                if s == 1 and x == CFG["wbx"]:
+                    wb_first(t)
         write_back(t)
         if last:
             dma("y", HBM(T.yn[:, :]), A("ynb", 0, W))
-        ts(A("nsf"), A("nsi", 4 * t + 3, 4 * t + 4), 0.5, OP.subtract, CAP * SU, OP.min)
-        for x in CFG["ord"][4]:
+        links_in(t)
+        for x in CH:
             receive(t, x)
     dma("y", HBM(T.yc[:, :]), A("yo"))
 

import math
from concourse.mybir import AluOpType as OP, ActivationFunctionType as AF

EPS = 2.0 ** -13
MAGIC = 1.5 * 2.0 ** 23
BIG = 1.5 * 2.0 ** 27
W0, B, LN, RO, SP, CAP = 3072, 128, 2560, 4, 2, 768
W = W0 + RO * B
NK, NS = LN // 16, CAP // 16
PG = 4096
MID = 1792
ESC = 1.0 - (MID - 0.5) / 4096
BASE = 33024
MARK = 256
CEN = (LN + NK) // 2
FAR = 8192.0
OWN = (RO - 1) * CAP
FREE = OWN + LN
CH = {"A": (0, 96), "B": (96, 160)}
PIECES = {"A": (0, 1, 2), "B": (3, 4)}
TB = {"A": ("b5", 0), "B": ("b6", 0)}
LKB = {"A": ("b7", 160), "B": ("b7", 256)}
PBK = [0, 1, 2, 3, 4]
CYCLE, PE_CYCLE, GATHER, SCATTER, WAKE, LOCAL, REMOTE = 0.83, 0.42, 1.3, 2.5, 250.0, (2000.0, 250.0), (3000.0, 60.0)
CFG = dict(late=(1, 2, 3, 4), late0=(), shared=(), shared1=(), first=(), recvv=(), payv=(), lpv=(), pefix=0.0, vfix=0.0, afix=100.0,
           parts=(0, 384, 768), lparts=(0, 768), modv=(1, 3, 5, 7), rrow=300.0, riss=600.0,
           hb=("b6", 336, "b6", 384, "b6", 432), sb=(3, 4), cqs=False, msgs=False, k16s=True, wbx="A", lgv=(), rrs=(), arv=False,
           wb=(7, 0, 1, 0, 7), tl=(7, 0), eqg=4, wake=WAKE, linkat=1, split=False, tries=2500, amp=300.0, near=6000.0, shake=0.15, back=0.3, jump=800.0)
ORDER = {}

_F, _H, _I, _B, _U = "float32", "float16", "int32", "bfloat16", "uint16"
MATS = ["id", "nid", "blk", "ntri", "i13", "e15", "slt", "nslt", "moh", "blkw", "blk2", "i34", "i18", "i512", "u1", "l1", "low", "nb4", "omat", "r1", "nfar",
        "p00", "p01", "p10", "p11"]
SELS = ["selt", "seln", "sel0", "sel1", "selw"]
SCRATCH = {}
for _n, _w, _d in (
        ("tb", W0, _I), ("kt", B + W, _F), ("dt", B + PG + W, _F), ("lf", W, _F), ("ynb", B + W, _B), ("ci", 1536, _I), ("cb", 1536, _B), ("rb", 768, _B),
        ("dn", 384, _I), ("fh", 192, _H), ("ft", 192, _H), ("ld", 192, _F), ("fl", 192, _U), ("vd", 1280, _B), ("vt", 1280, _B),
        ("v8", 640, _B), ("tk", 320, _F), ("iop", 1, _I), ("pi", 3, _I), ("xf", 160, _B), ("xg", 128, _B), ("xr", 256, _B), ("pc", 32, _F), ("oh16", 16, _F),
        ("mats", 128 * len(MATS), _B), ("sels", 160 * len(SELS), _B), ("f32m", 768, _F), ("expa", 2048, _B), ("c32k", 96, _B),
        ("th0", 256, _B), ("th1", 256, _B), ("th2", 16, _F), ("th3", 16, _F), ("thr", 256, _B), ("jg", 480, _F), ("dj", 16, _F),
        ("ca", NK, _I), ("cl", NK, _U), ("c2", NK, _U), ("cf", NK, _F), ("r32", NK, _H), ("cq", NK, _F), ("r0", NK, _B), ("qq", 320, _H), ("yy", NK, _F),
        ("rr", NK, _F), ("lk", 2 * NK, _F), ("r33", NK, _F), ("nsi", 4 * RO, _F), ("lg", LN, _H), ("es", NK, _B), ("inc", 328, _F), ("pat", 192, _F), ("zer", CAP, _B), ("rl", NK, _U), ("yo", NK, _F), ("nsf", 1, _F),
        ("spr", NK, _F), ("ue", 2 * NK, _H), ("ol", 20, _U), ("kw", LN + NK, _B), ("kr2", CAP, _B), ("kl", NS, _U), ("k16b", NS, _B), ("mrow", CAP, _F),
        ("oh", CAP, _B), ("lo16", CAP, _H), ("il", NS, _U), ("pay", CAP, _B), ("msg", NS, _H), ("mi", NS * RO, _H), ("sc", CAP, _F),
        ("rcv", NK, _F), ("xs", NK, _F), ("gu", NK, _F),
        ("kap", LN, _B), ("ds", LN, _H), ("cd", LN, _B), ("ne", LN, _B), ("ag", LN, _F), ("win", FREE + 16, _B),
        ("h0", 8, _F), ("h1", 8, _F), ("ht", 8, _F), ("hz", 8, _F), ("c8", 8, _U), ("d8", B, _H), ("e8", 8, _F), ("cnd", 8, _F), ("ka", 16, _F), ("k32", 16, _F), ("k16", 16, _H),
        ("nc", 16, _H), ("fdu", 16, _U), ("fy", 16, _F), ("lw", 16, _U), ("eq", 16 * B, _B), ("kr", 256, _B),
        ("ohb", B, _B), ("up", B, _F), ("lo", B, _F), ("cap", B, _F), ("gro", B, _F), ("zr", B, _B), ("z0", B, _B), ("hx", B, _B),
        ("xa", B, _F), ("xb", B, _B), ("nob", B, _B), ("g1", B, _H), ("af", B, _F), ("wr", 3 * B, _F), ("dl", B, _F), ("ax", B, _F), ("ar", B, _F)):
    SCRATCH[_n] = ("sbuf", [128, _w], _d)
for _k in range(8):
    SCRATCH["b%d" % _k] = ("psum", [128, 512], _F)
SEMAPHORES = (["cv", "ct", "cs", "cg"] + ["ld%d" % k for k in range(16)]
              + [n + str(k) + str(h) for k in range(RO) for n in ("arr", "snt") for h in range(4)])


def in_order(calls):
    n, wake = len(calls), CFG["wake"]
    tail = [c[2] - c[1] for c in calls]
    before = [[(p, 0.0 if p in c[5] else tail[p] + wake) for p in c[3]] for c in calls]
    after = [[] for _ in range(n)]
    for i in range(n):
        for p, gap in before[i]:
            after[p].append((i, gap))

    def lay(order, needs):
        end, why, held = [0.0] * n, [None] * n, {r: [] for c in calls for r in [c[0]] + c[4]}
        for i in order:
            q, d, banks, t, w = calls[i][0], calls[i][1], calls[i][4], 0.0, None
            for p, gap in needs[i]:
                if end[p] + gap > t:
                    t, w = end[p] + gap, (p, False)
            moved = True
            while moved:
                moved = False
                h = held[q]
                at = len(h)
                while at and h[at - 1][1] > t:
                    at -= 1
                while at < len(h) and h[at][0] < t + d:
                    t, w = h[at][1], (h[at][3], True)
                    at += 1
                for r in banks:
                    h = held[r]
                    k = len(h)
                    while k and h[k - 1][1] + wake > t:
                        k -= 1
                    while k < len(h) and h[k][0] - wake < t + d:
                        if h[k][2] != q and h[k][1] + wake > t:
                            t, moved, w = h[k][1] + wake, True, (h[k][3], True)
                        k += 1
            end[i], why[i] = t + d, w
            held[q].insert(at, (t, t + d, q, i))
            for r in banks:
                h = held[r]
                k = len(h)
                while k and h[k - 1][0] > t:
                    k -= 1
                h.insert(k, (t, t + d, q, i))
        return end, why

    def forth(way):
        end, why = lay(sorted(range(n), key=lambda i: (-way[i], i)), before)
        return max(end[i] + tail[i] for i in range(n)), end, way, why

    def there_and_back(way):
        end = forth(way)[1]
        return forth(lay(sorted(range(n), key=lambda i: (-end[i], -i)), after)[0])

    def chance(x):
        return (math.sin(x * 12.9898) * 43758.5453) % 1
    best = there_and_back([-i for i in range(n)])
    for k in range(1, CFG["tries"] + 1):
        way, shake = list(best[2]), chance(k + 0.1) < CFG["shake"]
        if shake:
            amp, mid = CFG["amp"] * (1 + k % 3), best[0] * ((k * 0.618) % 1)
            way = [way[i] + (amp * math.sin((i + 1) * (k + 1) * 12.9898) if abs(best[1][i] - mid) < CFG["near"] else 0.0) for i in range(n)]
        else:
            i, pairs = max(range(n), key=lambda i: best[1][i] + tail[i]), []
            while best[3][i]:
                if best[3][i][1]:
                    pairs.append((i, best[3][i][0]))
                i = best[3][i][0]
            i, j = pairs[int(chance(k + 0.37) * len(pairs))]
            jump = 10 + CFG["jump"] * chance(k + 0.71)
            if chance(k + 0.53) < 0.5:
                way[i] = max(way[i], way[j]) + jump
            else:
                way[j] = min(way[i], way[j]) - jump
                for a in range(j, n):
                    for p, gap in before[a]:
                        if way[a] >= way[p]:
                            way[a] = way[p] - 1.0
        for i in range(n - 1, -1, -1):
            for j, gap in after[i]:
                if way[j] + 1.0 > way[i]:
                    way[i] = way[j] + 1.0
        best = min((there_and_back if shake or chance(k + 0.91) < CFG["back"] else forth)(way), best, key=lambda b: b[0])
    CFG["span"] = best[0]
    loads = [i for i in range(n) if calls[i][0] in "ys" and not calls[i][3]]
    return loads + sorted(set(range(n)) - set(loads), key=lambda i: (best[1][i] - calls[i][1], i))


def rank_program(g, core, T, topo):
    rank = T.rank_of(core)
    if rank is None:
        return
    E = {"v": g.vector, "t": g.tensor, "s": g.scalar, "g": g, "y": g.sync}
    V, S, PE = g.vector, g.scalar, g.tensor
    calls, makes, writes, reads, lastpe = [], [], {}, {}, {}

    def A(name, lo=0, hi=None, step=1, rows=None):
        if hi is None:
            hi = T[name].shape[1]
        elif name in ("kt", "dt", "ynb"):
            lo, hi = lo + B, hi + B
        hi -= (hi - lo - 1) % step
        ap = T[name][slice(None) if rows is None else rows, lo:hi:step] if step > 1 else T[name][slice(None) if rows is None else rows, lo:hi]
        return (ap, (name, lo, hi), None, (hi - lo + step - 1) // step)

    def IX(win, off):
        return (win[0].indirect(off[0]), win[1], off[1], 16 * off[3])

    def HBM(ap):
        return (ap, None, None, 0)

    def psum(x):
        return SCRATCH[x[1][0]][0] == "psum"

    def size(x):
        return 2 if SCRATCH[x[1][0]][2] in (_H, _B, _U) else 4

    def call(q, busy, took, make, ins, outs, also=()):
        ins = [x for x in ins if isinstance(x, tuple) and x[1]]
        outs = [x for x in outs if x[1]]
        rd = {x[1] for x in ins} | {x[2] for x in ins + outs if x[2]}
        wr = {x[1] for x in outs}
        me, pre = len(calls), set(also)
        for name, lo, hi in rd | wr:
            pre |= {i for l, h, i in writes.get(name, []) if l < hi and lo < h}
        for name, lo, hi in wr:
            pre |= {i for l, h, i in reads.get(name, []) if l < hi and lo < h}
        for name, lo, hi in wr:
            for d in (writes, reads):
                d[name] = [e for e in d.get(name, []) if not (lo <= e[0] and e[1] <= hi)]
            writes[name].append((lo, hi, me))
        for name, lo, hi in rd:
            reads.setdefault(name, []).append((lo, hi, me))
        banks = sorted({x[1][0] for x in ins + outs if psum(x)})
        if q == "t":
            pre |= {lastpe[b] for b in banks if b in lastpe}
            lastpe.update({b: me for b in banks})
        free = {i for i in pre if calls[i][0] == q == "t"}
        calls.append((q, busy, took, sorted(pre), banks, free))
        makes.append(make)
        return me

    def op(q, ns, fn, ins, outs):
        call(q, ns, ns, ("c" + q, 1, lambda sem: fn().then_inc(sem, 1)), ins, outs)

    nd = [0, 0.0]

    def dma(q, *pairs):
        def make(sem):
            for out, in_ in zip(pairs[0::2], pairs[1::2]):
                E[q].dma_start(out[0], in_[0]).then_inc(sem, 16)
        nb = sum(128 * x[3] * size(x) * (1 if x[0].shape[0] == 128 else 1 / 16) for x in pairs if x[1]) / (2 if all(x[1] for x in pairs) else 1)
        nd[0] += 1
        if not pairs[1][1]:
            nd[1] += nb
            nb = nd[1]
        call(q, 60.0, LOCAL[0] + nb / LOCAL[1], ("ld%d" % nd[0], 8 * len(pairs), make), pairs[1::2], pairs[0::2])

    dst = T.cores[(rank + 1) % len(T.cores)]
    src = T.cores[(rank - 1) % len(T.cores)]

    wire = []

    def remote(out, in_, tag):
        rid, pid, _se = topo.addr(dst)
        ns = CFG["rrow"] + 128 * in_[3] * size(in_) / REMOTE[1]
        me = call("g", CFG["riss"], REMOTE[0], ("snt" + tag, len(topo.engines(core, dst)),
                                                lambda sem: g.remote_dma(out[0], in_[0], T.sem["arr" + tag], sem, pid, rid, topo.mask(core, dst))), [in_], [])
        calls[me] = calls[me][:3] + (sorted(set(calls[me][3]) | set(wire[:1])), [], set(wire[:1]))
        land = call("r", ns, ns, ("arr" + tag, len(topo.engines(src, core)), None), [], [out], [me] + wire[1:])
        calls[land] = calls[land][:5] + (set(wire[1:]),)
        wire[:] = [me, land]

    def ap(x):
        return x[0] if isinstance(x, tuple) else x

    def vec(out, ins, k):
        if out[2] or ins[0][2]:
            return 50.0 + out[3] * CYCLE * (SCATTER if out[2] else GATHER)
        return max(64.0, out[3] * k) * CYCLE + CFG["vfix"]

    def half(*x):
        return 0.5 if all(size(a) == 2 for a in x) else 1.0

    def ts(out, a, s1, o0, s2=None, o1=None):
        if o1 is None:
            op("v", vec(out, [a], half(out, a)), lambda: V.tensor_scalar(out[0], a[0], ap(s1), None, o0), [a, s1], [out])
        else:
            op("v", vec(out, [a], half(out, a)), lambda: V.tensor_scalar(out[0], a[0], ap(s1), ap(s2), o0, o1), [a, s1, s2], [out])

    def tt(out, a, b, alu):
        op("v", vec(out, [a], 1.0 if psum(a) or psum(b) else 2.0), lambda: V.tensor_tensor(out[0], a[0], b[0], alu), [a, b], [out])

    def cp(out, a):
        op("v", vec(out, [a], half(out, a)), lambda: V.tensor_copy(out[0], a[0]), [a], [out])

    def turn(out, a):
        op("v", vec(out, [a], half(out, a)), lambda: V.transpose(out[0], a[0]), [a], [out])

    def scan(out, a, b, init, o0, o1):
        op("v", vec(out, [a], half(out, a, b)), lambda: V.tensor_tensor_scan(out[0], a[0], b[0], ap(init), o0, o1), [a, b, init], [out])

    def fill(out, pattern, base, cm=0):
        op("g", 130.0 + 2 * CYCLE * out[3], lambda: g.iota(out[0], pattern, base, cm, allow_small_or_imprecise_dtypes=True), [], [out])

    def act(out, a, func=AF.Copy, bias=0.0, scale=1.0):
        op("s", CFG["afix"] + out[3] * CYCLE * (GATHER if a[2] else 1.0), lambda: S.activation(out[0], a[0], func, bias=ap(bias), scale=ap(scale)),
           [a, bias, scale], [out])

    def lin(on_s, out, a, scale, bias):
        if on_s:
            act(out, a, bias=bias, scale=scale)
        else:
            ts(out, a, scale, OP.mult, bias, OP.add)

    def mm(items, group=0, start=True, stop=True):
        k = group or len(items)

        def f():
            for i, (o, l, r) in enumerate(items):
                x = PE.matmul(o[0], l[0], r[0], start and i % k == 0, stop and i % k == k - 1)
            return x
        op("t", sum(max(64, r[3]) * (4 if size(r) == 4 else 1) for o, l, r in items) * PE_CYCLE + CFG["pefix"] * len(items), f,
           [x for it in items for x in it[1:]], [it[0] for it in items])

    def M(n):
        i = MATS.index(n)
        return A("mats", 128 * i, 128 * i + 128)

    def F32(i):
        return A("f32m", 128 * i, 128 * i + 128)

    def SEL(n, r=None):
        i = 160 * SELS.index(n)
        return A("sels", i, i + 160) if r is None else A("sels", i + 16 - r, i + 144 - r)

    def tolist(out, sel, name, lo, hi):
        return [(out, SEL(sel, r), A(name, lo + r, hi, 16)) for r in range(16)]

    def spread(bank, lo, n, src):
        return [(A(bank, lo + r, lo + 16 * n, 16), A("expa", 128 * r, 128 * r + 128), src) for r in range(16)]

    def X(name, x, base=0):
        return A(name, base + CH[x][0], base + CH[x][1])

    def X2(name, x, base=0):
        return A(name, base + 2 * CH[x][0], base + 2 * CH[x][1], 2)

    def TX(x, k, m=None):
        n = CH[x][1] - CH[x][0]
        return A(TB[x][0], TB[x][1] + n * k, TB[x][1] + n * k + (m or n))

    def P(name, p, base=0):
        return A(name, base + 512 * p, base + 512 * p + 512)

    def L(name, p):
        return A(name, 32 * p, 32 * p + 32)

    def BK(p, lo=0, hi=512):
        return A("b%d" % p, lo, hi)

    def HB(k, lo, hi):
        return A(CFG["hb"][2 * k], CFG["hb"][2 * k + 1] + lo, CFG["hb"][2 * k + 1] + hi)

    for k in range(4):
        dma("y", A("tb", 768 * k, 768 * k + 768), HBM(T.tab[:, 768 * k:768 * k + 768]))
        if k == 0:
            dma("y", A("dn", 0, 192), HBM(T.suf[:, :]), A("dn", 192, 384), HBM(T.lnk[:, :]))
        if k == 1:
            dma("y", A("ca"), HBM(T.cx[:, :]))
    dma("y", A("vd"), HBM(T.vv[:, :]))

    PGC, PRC, PAR, PFC, P16, PM1, PP1, N15, N0, C15, PS, PB, PM15, J0, R0, R192, NPAR, PP16, PM16, LB = range(20)

    def col(i):
        return A("pc", i, i + 1)

    def oh(i):
        return A("oh16", i, i + 1)
    xm = A("xf", 0, 128)
    fill(A("iop"), [[1, 1]], 0, 1)
    fill(col(PFC), [[1, 1]], 0, 1)
    fill(A("xf"), [[1, NK]], 0)
    fill(A("xg"), [[1, 8], [0, 16]], 0)
    fill(A("xr"), [[0, 16], [1, 16]], 0)
    fill(A("lf", 0, W0), [[1, W0]], -MID)
    fill(A("c32k"), [[0, 96]], BASE)
    fill(A("v8"), [[0, 640]], 0)
    fill(A("tk"), [[0, 320]], BASE)
    fill(A("dt", W0, PG), [[0, PG - W0]], 0)
    fill(A("h0"), [[0, 8]], 0)
    fill(A("zer"), [[0, CAP]], 0)
    fill(A("lk"), [[0, 2 * NK]], 0)
    fill(A("pat"), [[0, 96], [-2 * int(FAR), 2]], int(FAR))
    fill(A("inc", 0, 8), [[0, 8]], -CEN)
    fill(A("spr"), [[1, NK]], LN - CEN)
    fill(A("mrow"), [[1, CAP]], -CEN)
    fill(A("win", FREE, FREE + 16), [[0, 16]], -1)

    ts(A("pi", 0, 1), A("iop"), 4, OP.arith_shift_right)
    ts(A("pi", 1, 2), A("iop"), 15, OP.bitwise_and)
    ts(A("pi", 2, 3), A("iop"), 4, OP.arith_shift_right, 1, OP.bitwise_and)
    cp(A("pc", PGC, PAR + 1), A("pi"))
    for i, k in ((PP1, 1.0), (PM15, -15.0), (PM1, -1.0), (PP16, 16.0), (PM16, -16.0)):
        ts(col(i), col(PFC), k, OP.add)
    ts(A("oh16"), A("xf", 0, 16), col(PRC), OP.is_equal)
    ts(col(P16), col(PGC), 16.0, OP.mult, 16.0, OP.add)
    for i, c in ((N15, oh(15)), (N0, oh(0)), (NPAR, col(PAR))):
        ts(col(i), c, -1.0, OP.mult, 1.0, OP.add)
    ts(col(C15), oh(15), 1.0 / 65536, OP.mult)
    ts(col(R0), oh(0), -BIG / 65536, OP.mult)
    ts(col(R192), col(R0), 192.0, OP.add)
    ts(col(J0), col(PRC), CAP - CEN + FAR, OP.add)
    ts(col(PS), oh(0), 1.0 / 4096, OP.mult, oh(1), OP.add)
    ts(col(PB), oh(15), float(MARK), OP.mult)
    ts(col(LB), col(PRC), -256.0, OP.mult, -128.0, OP.add)
    ts(M("id"), xm, col(PFC), OP.is_equal)
    ts(M("blk"), A("xg"), col(PGC), OP.is_equal)
    act(M("low"), A("xr", 0, 128), AF.Sigmoid, bias=col(LB), scale=256.0)
    tt(M("low"), M("low"), M("blk"), OP.mult)
    ts(M("u1"), xm, col(PP1), OP.is_equal, col(N15), OP.mult)
    ts(M("l1"), xm, col(PM1), OP.is_equal, col(N0), OP.mult)
    for n, c, m in (("p00", PFC, NPAR), ("p11", PFC, PAR), ("p01", PP16, NPAR), ("p10", PM16, PAR)):
        ts(M(n), xm, col(c), OP.is_equal, col(m), OP.mult)
    ts(F32(4), xm, col(PM15), OP.is_equal, col(C15), OP.mult)
    for r in range(16):
        act(A("expa", 128 * r, 128 * r + 128), M("blk"), scale=oh(r))
    cp(F32(0), M("id"))
    tt(F32(2), M("id"), M("u1"), OP.subtract)
    for n, a, k in (("nid", M("id"), -1.0), ("ntri", M("low"), -15.0 / 16), ("i13", M("id"), 1 / EPS), ("i34", M("id"), 34.0), ("i18", M("id"), 18.0),
                    ("i512", M("id"), 512.0), ("blk2", M("blk"), 2.0), ("nb4", M("blk"), -FAR / 2), ("omat", M("blk"), 1.5), ("slt", M("id"), -FAR),
                    ("nfar", M("id"), -FAR), ("r1", M("id"), oh(1))):
        ts(M(n), a, k, OP.mult)
    ts(F32(3), F32(2), 1.0 / 65536, OP.mult)
    tt(F32(1), M("nid"), M("low"), OP.subtract)
    ts(F32(5), M("id"), oh(0), OP.mult, 4096.0, OP.mult)
    ts(M("e15"), M("blk"), oh(15), OP.mult, 2.0 ** 23 / MARK, OP.mult)
    tt(M("moh"), M("id"), M("l1"), OP.subtract)
    tt(M("omat"), M("omat"), M("id"), OP.subtract)
    tt(M("slt"), M("slt"), M("low"), OP.add)
    ts(M("nslt"), M("slt"), -1.0, OP.mult)
    ts(SEL("selt"), A("xf"), col(P16), OP.is_equal)
    for n, k in (("sel0", oh(0)), ("sel1", oh(1)), ("selw", col(PRC)), ("seln", BASE / 16.0)):
        ts(SEL(n), SEL("selt"), k, OP.mult)
    ts(A("th0"), A("xr"), 0.0, OP.is_gt, 0.5, OP.mult)
    ts(A("th1"), A("xr"), 0.0, OP.is_equal, 2.0, OP.mult)
    scan(A("thr"), A("th0"), A("th1"), 0.0, OP.mult, OP.add)
    tt(A("th2"), A("thr", 0, 16), A("oh16"), OP.mult)
    scan(A("th3"), A("th2"), A("zer", 0, 16), 0.0, OP.add, OP.add)
    ts(M("blkw"), M("blk"), A("th3", 15, 16), OP.mult, 0.5, OP.mult)
    act(A("tk"), A("tk"), bias=-127.5 / 8)
    ts(A("jg", 0, NK), A("xf"), 16.0, OP.mult, col(J0), OP.add)
    for t in range(1, RO - 1):
        act(A("jg", NK * t, NK * t + NK), A("jg", 0, NK), bias=float(t * CAP))
    for h in range(2):
        act(A("dj", 8 * h, 8 * h + 8), A("jg", 0, 8), bias=CEN - CAP - FAR - B - MID)

    def unturn(out, lo, step, name, at, n):
        return [(A(out, lo + h, lo + h + step[0] * n, step[0]), M("p%d%d" % (h, e)), A(name, at + 16 * e, at + 16 * e + step[1] * (n - 1) + 1, step[1]))
                for h in range(2) for e in range(2)]

    def targets_list(st):
        if st < RO * SP:
            b, at = CFG["tl"]
            mm(unturn("b%d" % b, at, (2, 32), "vt", 2 * st, 40) + unturn("b%d" % b, at + 80, (2, 32), "vt", 2 * st + 1, 40), 2)
            act(A("v8", 320 * (st % 2) + 1, 320 * (st % 2) + 320, 2), BK(b, at, at + NK), scale=1.0 / 16)

    cp(A("cl"), A("ca"))
    ts(A("cf"), A("ca"), float(MID), OP.subtract, 1.0 / 4096, OP.mult)
    turn(A("vt"), A("vd"))
    targets_list(0)
    ts(A("ld"), A("dn", 192, 384), float(MID), OP.subtract)
    dma("y", A("lf", 0, W0, rows=slice(1, 128, 16)), A("ld"))
    ts(A("fh"), A("dn", 0, 192), float(MID), OP.subtract)
    turn(A("ft"), A("fh"))
    mm([it for b in range(6) for it in unturn("b7", 256 + 2 * b, (12, 1), "ft", 32 * b, 16)], 2)
    ts(A("fl"), BK(7, 256, 448), float(MID), OP.add)
    for h in range(4):
        o, w = A("dt", PG + 768 * h, PG + 768 * h + 768), IX(A("lf", 0, W0), A("fl", 48 * h, 48 * h + 48))
        if h in CFG["lpv"]:
            ts(o, w, col(PS), OP.mult, col(PB), OP.add)
        else:
            act(o, w, AF.Identity, bias=col(PB), scale=col(PS))

    def counts_table(k):
        c, b = A("ci", 768 * (k % 2), 768 * (k % 2) + 768), A("cb", 768 * (k % 2), 768 * (k % 2) + 768)
        ts(c, A("tb", 768 * k, 768 * k + 768), 15, OP.bitwise_and)
        ts(b, c, 34.0, OP.mult, -542.0625, OP.add)
        act(A("kt", 768 * k, 768 * k + 768), b, bias=544.0 - EPS)

    def pointer_table(k):
        o = 768 * (k % 2)
        ts(A("ag", o, o + 768), A("tb", 768 * k, 768 * k + 768), 7.5 + 16 * MID, OP.subtract, BIG, OP.add)
        if k == 0:
            mm([(BK(1, 0, 1), F32(4), A("ag", 0, 1))])
            act(A("dt", PG, PG + 1), BK(1, 0, 1), AF.Identity, bias=col(R0))
        for h in range(2):
            s, rb, bk = A("ag", o + 384 * h, o + 384 * h + 384), A("rb", 384 * h, 384 * h + 384), BK(4 - 4 * h, 0, 384)
            mm([(BK(2 + h, 0, 384), F32(3), s)])
            if 2 * k + h in CFG["modv"]:
                r = A("ag", 1536 + 384 * h, 1920 + 384 * h)
                ts(r, BK(2 + h, 0, 384), MAGIC, OP.add, MAGIC, OP.subtract)
                tt(A("dt", 768 * k + 384 * h, 768 * k + 384 * h + 384), BK(2 + h, 0, 384), r, OP.subtract)
                continue
            act(rb, BK(2 + h, 0, 384), AF.Identity, bias=col(R192))
            mm([(bk, F32(3), s)], stop=False)
            mm([(bk, M("nid"), rb)], start=False)
            act(A("dt", 768 * k + 384 * h, 768 * k + 384 * h + 384), bk, AF.Identity, bias=col(R192))
    for f, k in ((counts_table, 0), (pointer_table, 0), (counts_table, 1), (pointer_table, 1), (counts_table, 2), (counts_table, 3),
                 (pointer_table, 2), (pointer_table, 3)):
        f(k)
    targets_list(1)

    KAP = (("kap", 0), ("win", OWN))

    def counts(t, s, x):
        name, at = KAP[s]
        for p in PIECES[x]:
            kw = IX(A("kt", 0, W0 + B * t), L("cl", p))
            if t + s == 0:
                (act if p in CFG["first"] else cp)(P(name, p, at), kw)
            elif p in CFG["shared1" if s else "shared"]:
                if s == 0:
                    mm([(BK(PBK[p]), M("id"), P("ne", p))])
                act(P("ag", p), kw)
                tt(P(name, p, at), BK(PBK[p]), P("ag", p), OP.mult)
            else:
                tt(P(name, p, at), kw, P("ne", p), OP.mult)
        for lo, hi, o in parts(x, 0):
            two([(o, M("id"), A("c32k", 0, hi - lo))], tolist(o, "selt", name, at + 16 * lo, at + 16 * hi))

    def parts(x, k):
        lo, hi = CH[x]
        cuts = (lo, hi - 32, hi) if CFG["split"] and hi - lo > 64 else (lo, hi)
        at = TB[x][1] + (hi - lo) * k - lo
        return [(a, b, A(TB[x][0], at + a, at + b)) for a, b in zip(cuts, cuts[1:])]

    def two(first, rest):
        mm(first, stop=False)
        mm(rest, start=False)

    def targets(st, x):
        s = TX(x, 0)
        lin(x in CFG["rrs"], X("r32", x), s, 16.0 / 17, BASE - (BASE + 16) * 16.0 / 17)
        lo, hi = 2 * CH[x][0], 2 * CH[x][1]
        tt(A("tk", lo, hi, 2), s, X("r32", x), OP.subtract)
        scan(A("qq", lo, hi), A("v8", 320 * (st % 2) + lo, 320 * (st % 2) + hi), A("tk", lo, hi), 0.0, OP.mult, OP.add)
        if st % 2:
            ts(X("r0", x), X("cf", x), ESC - 1.0, OP.is_lt, 2 * FAR, OP.mult)
            tt(X("r33", x), X("r32", x), X("r0", x), OP.add)
            tt(X("es", x), A("qq", lo + 1, hi, 2), X("r33", x), OP.is_ge)
        tt(s, A("qq", lo + 1, hi, 2), X("r32", x), OP.is_ge)
        tt(X("yy", x), s, X("cf", x), OP.add)
        ts(X("c2", x), X("yy", x), 4096.0, OP.mult, float(MID), OP.add)

    def compare(s, p):
        bk = BK(PBK[p])
        two([(bk, M("ntri"), P(KAP[s][0], p, KAP[s][1]))], spread("b%d" % PBK[p], 0, 32, A("qq", 64 * p + 1, 64 * p + 64, 2)))
        act(bk if p in CFG["late" if s else "late0"] else P("cd", p), bk, AF.Sigmoid, bias=-64.0 * (BASE - 29), scale=64.0)

    def pointers(t, s, x):
        for p in PIECES[x]:
            dw, bk = IX(A("dt", 0, PG + W0 + B * t), L("c2", p)), BK(PBK[p])
            if p in CFG["late" if s else "late0"]:
                act(P("ag", p), dw)
                tt(P("ds", p), bk, P("ag", p), OP.mult)
            else:
                tt(P("ds", p), dw, P("cd", p), OP.mult)
            if s == 0:
                two([(bk, M("i13"), P("kap", p))], [(bk, M("e15"), P("ds", p))])
                act(bk if p in CFG["shared1"] else P("ne", p), bk, AF.Sigmoid, bias=256.0 * (2.0 ** 23 - 0.5), scale=-256.0)
        for lo, hi, o in parts(x, 1):
            mm(tolist(o, "selt", "ds", 16 * lo, 16 * hi))
        ts(X("rr", x), TX(x, 1), MAGIC, OP.add, MAGIC, OP.subtract)
        tt(X("cf", x), TX(x, 1), X("rr", x), OP.subtract)
        if s == 0:
            ts(X("cl", x), X("cf", x), 4096.0, OP.mult, float(MID), OP.add)
        elif x == "A" and t < RO - 1:
            ts(A("c8"), A("cf", 0, 8), 4096.0, OP.mult, float(MID), OP.add)

    H = ["h0", "h1"]

    def first_escape():
        old, new = H
        act(A("hz"), A(old), AF.Relu, bias=1.0, scale=-8.0)
        ts(A("e8"), A("yy", 0, 8), ESC, OP.is_gt)
        tt(A("ht"), A("hz"), A("yy", 0, 8), OP.mult)
        tt(A("ht"), A("ht"), A(old), OP.add)
        tt(A(new), A("ht"), A("e8"), OP.mult)
        H.reverse()

    def slots(t, x):
        lo, hi = CH[x]
        n = hi - lo
        b, at = TB[x][0], TB[x][1] + 2 * n
        even, odd = A(b, at, at + 2 * n, 2), A(b, at + 1, at + 2 * n, 2)
        mm([(even, M("slt"), X("es", x))])
        mm([(odd, M("blk"), X("es", x)), (odd, M("nslt"), X("es", x))])
        two([(TX(x, 4), F32(0), X("spr", x))], [(TX(x, 4), M("nb4"), X("es", x))])
        scan(A("inc", 8 + 2 * lo, 8 + 2 * hi), TX(x, 2, 2 * n), A("pat", 0, 2 * n), A("inc", 7 + 2 * lo, 8 + 2 * lo), OP.add, OP.add)
        tt(A("ue", 2 * lo, 2 * lo + n), TX(x, 4), X2("inc", x, 7), OP.max)
        ts(A("ue", 2 * lo + n, 2 * hi), X2("inc", x, 9), float(CAP - CEN), OP.min, -1.0, OP.add)
        o = TX(x, 5, n // 8)
        mm(tolist(o, "sel0", "ue", 2 * lo, 2 * hi))
        ts(A("ol", lo // 8, hi // 8), o, float(CEN), OP.add)
        cp(IX(A("kw"), A("ol", lo // 8, lo // 8 + n // 16)), X("xf", x))

    def send(t):
        last = t == RO - 1
        scan(A("kr2"), A("kw", 0, CAP), A("zer"), 0.0, OP.max, OP.add)
        mm(tolist(HB(0, 0, NS), "sel0", "kr2", 0, CAP))
        ts(A("kl"), HB(0, 0, NS), 2.0, OP.mult)
        if not last:
            lin(CFG["k16s"], A("k16b"), HB(0, 0, NS), 16.0, 0.0)
        cuts = CFG["parts"]
        for lo, hi in zip(cuts, cuts[1:]):
            tt(A("oh", lo, hi), IX(A("inc", 8, 328), A("kl", lo // 16, hi // 16)), A("mrow", lo, hi), OP.is_equal)
        for h, (lo, hi) in enumerate(zip(cuts + (0,), cuts[1:] + (0,))):
            if h == min(CFG["linkat"], len(cuts) - 1):
                send_links(t)
            if not last and hi:
                o = HB(2, lo // 16, hi // 16)
                two([(o, M("id"), A("k16b", lo // 16, hi // 16))], tolist(o, "selw", "oh", lo, hi))
                cp(A("il", lo // 16, hi // 16), o)
                (cp if h in CFG["payv"] else act)(A("pay", lo, hi), IX(A("win", OWN, OWN + LN), A("il", lo // 16, hi // 16)))
                at = OWN - CAP * (t + 1)
                remote(A("win", at + lo, at + hi), A("pay", lo, hi), "%d%d" % (t, h))

    def send_links(t):
        cuts = CFG["lparts"]
        for lo, hi in zip(cuts, cuts[1:]):
            tt(A("lo16", lo, hi), IX(A("lk"), A("kl", lo // 16, hi // 16)), A("oh", lo, hi), OP.mult)
        mm(tolist(HB(1, 0, NS), "selt", "lo16", 0, CAP))
        lin(CFG["msgs"], A("msg"), HB(1, 0, NS), 1 / FAR, 0.0)
        remote(A("mi", NS * t, NS * t + NS), A("msg"), "%d3" % t)

    def own_links(t, x):
        for p in PIECES[x]:
            (cp if p in CFG["lgv"] else act)(P("lg", p), IX(A("dt", PG, PG + W0 + B * t), L("cl", p)))
        o = A(LKB[x][0], LKB[x][1], LKB[x][1] + CH[x][1] - CH[x][0])
        mm(tolist(o, "sel1", "lg", 16 * CH[x][0], 16 * CH[x][1]))
        act(X2("lk", x), o)

    def links_in(t):
        for h in range(2):
            lo, hi, bk = 384 * h, 384 * h + 384, CFG["sb"][h]
            two([(BK(bk, 0, 384), M("omat"), A("oh", lo, hi))], spread("b%d" % bk, 0, 24, A("mi", NS * t + 24 * h, NS * t + 24 * h + 24)))
            scan(A("sc", lo, hi), A("oh", lo, hi), BK(bk, 0, 384), A("sc", lo - 1, lo) if h else 0.0, OP.max, OP.min)
        ts(A("nsf"), A("nsi", 4 * t + 3, 4 * t + 4), 0.5, OP.subtract, float(CAP - CEN), OP.min)

    def receive(t, x):
        last = t == RO - 1
        lo, hi = CH[x]
        sa = X2("inc", x, 8)
        ts(TX(x, 0), sa, A("nsf"), OP.is_ge, FAR, OP.mult)
        ts(X("rcv", x), sa, A("nsf"), OP.is_lt)
        if not last:
            two([(TX(x, 4), F32(0), X("jg", x, NK * t))], [(TX(x, 4), M("nfar"), X("es", x))])
            tt(X("xs", x), TX(x, 0), sa, OP.add)
            tt(TX(x, 4), TX(x, 4), X("xs", x), OP.min)
            ts(X("rl", x), TX(x, 4), float(CAP * (t + 1) + LN - CEN), OP.min, float(CEN), OP.add)
        lin(CFG["cqs"], X("cq", x), X("cf", x), 0.5 / FAR, 0.5 / FAR)
        tt(TX(x, 2), TX(x, 0), X("cq", x), OP.mult)
        if x == "A" and not last:
            tt(A(H[0]), A(H[0]), TX("A", 0, 8), OP.min)
        tt(X("gu", x), IX(A("sc"), A("ol", lo // 8 + (hi - lo) // 16, hi // 8)), X("rcv", x), OP.mult)
        tt(TX(x, 2), TX(x, 2), X("gu", x), OP.add)
        ts(X("yo" if last else "cl", x), TX(x, 2), FAR, OP.mult, MID - FAR / 2, OP.add)
        if not last:
            lin(CFG["cqs"], X("cf", x), TX(x, 2), 2.0, -1.0)
            for p in PIECES[x]:
                w = IX(A("win", OWN - CAP * (t + 1), FREE + 16), L("rl", p))
                if p in CFG["recvv"]:
                    ts(P("ne", p), w, 0.0, OP.is_lt)
                else:
                    act(P("ne", p), w, AF.Sigmoid, bias=-128.0, scale=-256.0 / EPS)

    def wb_first(t):
        new, old = H
        tt(A("cnd"), A(old), A(new), OP.is_gt)
        tt(A("ka", 0, 8), A("ka", 0, 8), A("cnd"), OP.mult)
        tt(A("ka", 8, 16), A("ka", 8, 16), A("cnd"), OP.mult)
        ts(A("k16"), A("ka"), 4096.0, OP.mult, 2048.0, OP.add)
        wa, wb = CFG["wb"][:2]
        mm(spread("b%d" % wa, 0, 16, A("k16")), 1)
        lin(CFG["cqs"], A("k32"), A("ka"), 4096.0, 2048.0)
        ts(A("fdu"), A("k16"), float(MID), OP.add, float(W0 + B * t - 1), OP.min)
        ts(A("nc"), A("k16"), 2048.0, OP.is_equal, 4.0, OP.mult)
        mm([(BK(wb, 0, 256), M("nid"), A("thr"))] + spread("b%d" % wb, 0, 16, A("nc")), stop=False)
        it = []
        for k in range(2):
            for p in range(8):
                e, o = B * (8 * k + p) + 16 * p, B * k + 16 * p
                ts(A("eq", e, e + B - 16 * p), BK(wa, o, B * k + B), A("k32", 8 * k + p, 8 * k + p + 1), OP.is_equal)
                it.append((BK(wb, o, o + 16), M("blkw"), A("eq", e, e + 16)))
                if p < 7:
                    it.append((BK(wb, o + 16, B * k + B), M("blk2"), A("eq", e + 16, e + B - 16 * p)))
                if (p + 1) % CFG["eqg"] == 0:
                    mm(it, start=False, stop=k == 1 and p == 7)
                    it = []
        act(A("kr"), BK(wb, 0, 256), AF.Sigmoid, scale=-2.0 ** 23)
        o = BK(wb, 256, 272)
        mm([(o, M("nid"), A("c32k", 0, 16)), (o, M("id"), A("k16"))] + tolist(o, "seln", "kr", 0, 256))
        tt(A("fy"), o, A("dj"), OP.max)
        ts(A("lw"), A("fy"), float(MID + B), OP.add)

    def write_back(t):
        wn = W0 + B * t
        l8, lf, ld = A("c8"), A("fdu", 0, 8), A("fdu", 8, 16)
        wc, wd, we = CFG["wb"][2:]
        o = BK(wc, 0, B)
        if t == RO - 1:
            o, s = BK(we, 256, 384), BK(we, 384, 392)
            tt(A("d8"), IX(A("dt", 0, PG + wn), A("c2", 0, 8)), A("cd", 0, B), OP.mult)
            mm(tolist(s, "selt", "d8", 0, B))
            ts(A("ht"), s, MAGIC, OP.add, MAGIC, OP.subtract)
            tt(A("ht"), s, A("ht"), OP.subtract)
            ts(l8, A("ht"), 4096.0, OP.mult, float(MID), OP.add)
        mm([(o, M("moh"), A("cd", 0, B))])
        act(A("ohb"), o)
        if t == RO - 1:
            act(A("nob"), o, bias=1.0, scale=-1.0)
            act(A("cap"), o, bias=16.0, scale=-2.0)
            act(A("hx"), IX(A("ynb", 0, wn), l8), bias=128.25, scale=0.5)
            mm([(o, M("id"), A("hx")), (o, M("i512"), A("kr", 0, B))])
            act(A("ynb", wn, wn + B), o, AF.Relu, bias=-640.0)
            tt(A("xb"), IX(A("ynb", 0, wn), lf), A("nob"), OP.mult)
            tt(IX(A("ynb", -B, wn), A("lw", 0, 8)), A("xb"), A("ohb"), OP.add)
            tt(A("xb"), IX(A("ynb", 0, wn), ld), A("cap"), OP.min)
            tt(IX(A("ynb", -B, wn), A("lw", 8, 16)), A("xb"), A("ohb"), OP.add)
            return
        act(A("up"), A("ohb"), bias=1024.0, scale=36.0 - 1024.0)
        act(A("lo"), A("ohb"), bias=-1.0, scale=37.0)
        act(A("cap"), A("ohb"), bias=1024.0, scale=478.0 - 1024.0)
        wr = A("wr", B * t, B * t + B)
        act(wr, xm, bias=(wn - MID) / 4096.0, scale=1.0 / 4096)
        act(A("af"), IX(A("dt", 0, wn), lf))
        mm([(BK(wc, 384, 512), F32(0), wr), (BK(wc, 384, 512), F32(1), A("af"))])
        tt(A("dl"), BK(wc, 384, 512), A("ohb"), OP.mult)
        act(A("zr"), IX(A("kt", 0, wn), ld), AF.Relu, scale=-1 / EPS)
        mm([(o, M("i18"), A("ohb")), (o, M("id"), A("zr"))])
        act(A("gro"), o, AF.Relu, bias=-2.0, scale=2.0)
        act(A("hx"), IX(A("kt", 0, wn), l8), bias=128.25 - 1.0 / 34, scale=1.0 / 68)
        act(A("z0"), IX(A("kt", 0, wn), l8), AF.Relu, scale=-4 / EPS)
        o = BK(wc, 2 * B, 3 * B)
        mm([(o, M("i34"), A("hx")), (o, M("nid"), A("z0")), (o, M("i512"), A("kr", 0, B))])
        ts(A("kt", wn, wn + B), o, 34.0 * 128 - 2 + 512, OP.subtract, -EPS, OP.max)
        act(A("dt", wn, wn + B), IX(A("dt", 0, wn), l8))
        act(A("dt", PG + wn, PG + wn + B), IX(A("lf", 0, wn), l8), AF.Identity, bias=col(PB), scale=col(PS))
        act(A("g1"), IX(A("lf", 0, wn), l8))
        o = BK(wd, B, 2 * B)
        two([(o, F32(5), wr)], [(o, M("r1"), A("g1"))])
        act(A("lf", wn, wn + B), o)
        o = BK(we, 384, 512)
        mm([(o, F32(0), A("af")), (o, F32(2), A("dl"))])
        act(A("ax"), o)
        if CFG["arv"]:
            ts(A("ar"), o, MAGIC, OP.add, MAGIC, OP.subtract)
        else:
            act(A("ar"), o, bias=MAGIC)
            act(A("ar"), A("ar"), bias=-MAGIC)
        tt(A("xa"), IX(A("kt", 0, wn), lf), A("up"), OP.min)
        tt(IX(A("kt", -B, wn), A("lw", 0, 8)), A("xa"), A("lo"), OP.max)
        tt(A("xa"), IX(A("kt", 0, wn), ld), A("cap"), OP.min)
        tt(IX(A("kt", -B, wn), A("lw", 8, 16)), A("xa"), A("gro"), OP.add)
        tt(IX(A("dt", -B, wn), A("lw", 0, 8)), A("ax"), A("ar"), OP.subtract)

    for t in range(RO):
        last = t == RO - 1
        fill(A("kw", 0, CAP), [[0, CAP]], 0)
        if last:
            n = (W - B) // 6
            for h in range(6):
                act(A("ynb", n * h, n * (h + 1)), A("kt", n * h, n * (h + 1)), AF.Relu, bias=-1.0 / 17, scale=1.0 / 34)
        for s in range(SP):
            for x in CH:
                counts(t, s, x)
                targets(SP * t + s, x)
            if t + s > 0:
                targets_list(SP * t + s + 1)
            if s == 1:
                act(A("ka", 0, 8), A(H[0]), bias=-1.5)
                act(A("ka", 8, 16), A("cf", 0, 8), bias=-0.5)
                for x in CH:
                    own_links(t, x)
                    slots(t, x)
                remote(A("nsi", 4 * t, 4 * t + 4), A("inc", 324, 328), "%d2" % t)
                send(t)
            first_escape()
            for x in CH:
                for p in PIECES[x]:
                    compare(s, p)
                pointers(t, s, x)
                if s == 1 and x == CFG["wbx"]:
                    wb_first(t)
        write_back(t)
        if last:
            dma("y", HBM(T.yn[:, :]), A("ynb", 0, W))
        links_in(t)
        for x in CH:
            receive(t, x)
    dma("y", HBM(T.yc[:, :]), A("yo"))

    cnt, waited, got, bank = {}, {}, {}, {}

    def need(q, sem, val):
        if waited.get((q, sem), 0) < val:
            E[q].wait_ge(T.sem[sem], val)
            waited[(q, sem)] = val
    if len(calls) not in ORDER:
        ORDER[len(calls)] = in_order(calls)
    for i in ORDER[len(calls)]:
        q, pre, banks = calls[i][0], calls[i][3], calls[i][4]
        sem, n, make = makes[i]
        if make:
            todo = {}
            for k in pre + [bank[b] for b in banks if b in bank and calls[bank[b]][0] != q]:
                if k not in calls[i][5]:
                    todo[got[k][0]] = max(todo.get(got[k][0], 0), got[k][1])
            for s in sorted(todo):
                need(q, s, todo[s])
            make(T.sem[sem])
        cnt[sem] = cnt.get(sem, 0) + n
        got[i] = (sem, cnt[sem])
        bank.update({b: i for b in banks})
    for s in sorted(cnt):
        need("g", s, cnt[s])
